import numpy as np
import ml_dtypes


def mxq(x, axis, fmt="e4m3"):
    dtype, down = {"e4m3": (ml_dtypes.float8_e4m3fn, 7), "e5m2": (ml_dtypes.float8_e5m2, 14)}[fmt]
    v = np.moveaxis(np.asarray(x, np.float32).astype(ml_dtypes.bfloat16).astype(np.float64), axis, -1)
    blocks = v.reshape(v.shape[:-1] + (-1, 32))
    amax = np.abs(blocks).max(-1, keepdims=True)
    byte = np.maximum(np.where(amax > 0, np.frexp(amax)[1] - 1 + 127, 0) - down, 1)
    scale = np.exp2(byte - 127.0)
    codes = (blocks / scale).astype(np.float32).astype(dtype).astype(np.float64)
    return np.moveaxis((codes * scale).reshape(v.shape), -1, axis)


WIDE = False


def mx_kscale(k):
    if not WIDE:
        return np.ones(k)
    levels = np.array([24, -24, 12, -12, 0])
    if k % 512:
        return np.exp2(np.random.permutation(np.resize(levels, k // 32))).repeat(32)
    a = np.empty((k // 512, 16))
    for p in range(k // 512):
        a[p, :8] = np.random.permutation(np.resize(levels, 8))
        for g in range(8):
            far = levels[np.abs(levels - a[p, g]) >= 10]
            a[p, g + 8] = far[np.random.randint(len(far))]
    return np.exp2(a.ravel()).repeat(32)


def f64(x):
    return np.asarray(x).astype(np.float64)


def striped(idx):
    return np.tile(idx.reshape(-1, 16).T, (8, 1)).astype(np.uint16)


def unstriped(offs):
    return offs[:16].T.reshape(-1).astype(np.int64)


E2M1 = np.array([0.0, 0.5, 1.0, 1.5, 2.0, 3.0, 4.0, 6.0, -0.0, -0.5, -1.0, -1.5, -2.0, -3.0, -4.0, -6.0])


def pack_weight(w, fmt):
    k, n = w.shape
    w = f64(np.asarray(w, np.float32).astype(ml_dtypes.bfloat16)).reshape(k // 32, 32, n)
    amax = np.abs(w).max(1)
    if fmt == "e4m3":
        byte = np.frexp(amax)[1] - 1 + 127 - 7
    else:
        mant, ex = np.frexp(amax / 6.0)
        byte = np.where(mant > 0.5, ex, ex - 1) + 127
    byte = np.clip(np.where(amax > 0, byte, 1), 1, 254)
    scaled = (w * np.exp2(127.0 - byte)[:, None, :]).reshape(k, n).astype(np.float32)
    by_word = np.ascontiguousarray(scaled.reshape(k // 512, 128, 4, n).transpose(0, 1, 3, 2))
    if fmt == "e4m3":
        words = by_word.astype(ml_dtypes.float8_e4m3fn).view(np.uint8)
    else:
        c = by_word.astype(ml_dtypes.float4_e2m1fn).view(np.uint8) & 0xF
        words = (c[..., 0::2] | (c[..., 1::2] << 4)).reshape(k // 512, 128, 2 * n)
    return np.ascontiguousarray(words), np.ascontiguousarray(byte.astype(np.uint8).reshape(k // 512, 16, n))


def unpack_weight(words, scales, fmt):
    g, _, n = scales.shape
    words = np.ascontiguousarray(words).reshape(g, 128, n, -1)
    if fmt == "e4m3":
        vals = words.view(ml_dtypes.float8_e4m3fn).astype(np.float64)
    else:
        nib = np.empty((g, 128, n, 4), np.uint8)
        nib[..., 0::2] = words & 0xF
        nib[..., 1::2] = words >> 4
        vals = E2M1[nib]
    vals = vals * np.repeat(np.exp2(scales.astype(np.float64) - 127.0), 8, axis=1)[..., None]
    return vals.transpose(0, 1, 3, 2).reshape(g * 512, n)


def pack_table4(v):
    words, scales = pack_weight(v, "e2m1")
    g, t = words.shape[0] // 2, v.shape[1]
    return np.ascontiguousarray(words.reshape(g, 2, 128, t, 2).transpose(0, 2, 3, 1, 4).reshape(g, 128, t, 4)), scales


def unpack_table4(words, scales):
    g, _, t, _ = words.shape
    return unpack_weight(words.reshape(g, 128, t, 2, 2).transpose(0, 3, 1, 2, 4).reshape(2 * g, 128, 2 * t), scales, "e2m1")


def sigm(f):
    return 1.0 / (1.0 + np.exp(-np.maximum(f, -700.0)))


K, L, R, N, T, J = 512, 1024, 512, 1024, 4096, 2048


def setup_inputs():
    n = np.random.standard_normal
    s = mx_kscale(K)[:, None]
    s2 = mx_kscale(L)[:, None]
    u = mx_kscale(R)[:, None]
    p_tab = pack_weight(n((K, T)) * s, "e4m3")
    p_tab2 = pack_table4(n((L, T)) * s2)
    p_wa = pack_weight(n((K, R)) / np.sqrt(K) / s, "e2m1")
    p_en = pack_weight(n((R, N)) / np.sqrt(R) / u, "e4m3")
    return {
        "tab_words": p_tab[0],
        "tab_scales": p_tab[1],
        "tab2_words": p_tab2[0],
        "tab2_scales": p_tab2[1],
        "wa_words": p_wa[0],
        "wa_scales": p_wa[1],
        "wb": (n((L, R)) / np.sqrt(L) / s2).astype(np.float32),
        "sm": (np.random.uniform(0.5, 2.0, R) * u[:, 0]).astype(np.float32),
        "en_words": p_en[0],
        "en_scales": p_en[1],
        "offs": striped(np.random.permutation(T)[:J]),
        "offs2": striped(np.random.permutation(T)[:J]),
    }


def reference(tab_words, tab_scales, tab2_words, tab2_scales, wa_words, wa_scales, wb, sm, en_words, en_scales, offs, offs2):
    idx = unstriped(offs)
    idx2 = unstriped(offs2)
    tab_ = unpack_weight(tab_words, tab_scales, "e4m3")[:, idx]
    tab2_ = unpack_table4(tab2_words, tab2_scales)[:, idx2]
    wa_ = unpack_weight(wa_words, wa_scales, "e2m1")
    wb_ = mxq(f64(wb), 0, "e4m3")
    z = wa_.T @ tab_ + wb_.T @ tab2_
    h = f64(sm)[:, None] * np.tanh(z)
    h_ = mxq(h, 0, "e4m3")
    en_ = unpack_weight(en_words, en_scales, "e4m3")
    y = en_.T @ h_
    return sigm(y)

@@ -1,0 +1,278 @@
+from contextlib import ExitStack
+
+import concourse.mybir as mybir
+
+K, L, R, N, T, J = 512, 1024, 512, 1024, 4096, 2048
+FLOPS = 2 * J * (K * R + L * R + R * N)
+
+F32 = mybir.dt.float32
+BF16 = mybir.dt.bfloat16
+I32 = mybir.dt.int32
+U32 = mybir.dt.uint32
+U16 = mybir.dt.uint16
+U8 = mybir.dt.uint8
+FP8X4 = mybir.dt.float8_e4m3fn_x4
+FP4X4 = mybir.dt.float4_e2m1fn_x4
+ACT = mybir.ActivationFunctionType
+MULT = mybir.AluOpType.mult
+
+P = 128
+PACK = 4
+CHUNK = 512
+CHUNKS = J // CHUNK
+LIST_COLS = CHUNK // 16
+QUADS = 4
+HALF = R // 2
+
+
+def tile_list_kg_tanh_sig_kernel(
+    tc, tab_words, tab_scales, tab2_words, tab2_scales, wa_words, wa_scales, wb, sm, en_words, en_scales, offs, offs2, out
+):
+    nc = tc.nc
+    with ExitStack() as ctx:
+        keep = ctx.enter_context(tc.tile_pool(name="keep", bufs=1))
+        ring = ctx.enter_context(tc.tile_pool(name="ring", bufs=2))
+        arena = ctx.enter_context(tc.tile_pool(name="arena", bufs=1))
+        stage = ctx.enter_context(tc.tile_pool(name="stage", bufs=8))
+        psum = ctx.enter_context(tc.psum_pool(name="psum", bufs=8))
+
+        list1 = keep.tile([P, J // 16], U16, name="list1")
+        list2 = keep.tile([P, J // 16], U16, name="list2")
+        nc.sync.dma_start(list2[:], offs2)
+        nc.sync.dma_start(list1[:], offs)
+
+        tab_s = keep.tile([P, T // 4], I32, name="tab_s", align_bytes=64)
+        tab2_s = keep.tile([P, T // 4], I32, name="tab2_s", tag="early_late", align_bytes=64)
+        moved_s = keep.tile([P, J // 4], I32, name="moved_s", align_bytes=64)
+        nc.vector.memset(tab2_s[:], 0)
+        nc.vector.memset(tab_s[:], 0)
+        for q in range(QUADS):
+            nc.sync.dma_start(tab2_s[32 * q : 32 * q + 8, :], tab2_scales[:, 4 * q : 4 * q + 4, :].bitcast(I32))
+        for q in range(QUADS):
+            nc.sync.dma_start(tab_s[32 * q : 32 * q + 4, :], tab_scales[0, 4 * q : 4 * q + 4, :].bitcast(I32))
+        nc.vector.memset(moved_s[:], 0)
+
+        with tc.tile_pool(name="first", bufs=1) as first:
+            warm = first.tile([P, 2], F32, name="warm")
+            nc.gpsimd.memset(warm[:, 0:1], 0.0)
+            nc.scalar.activation(warm[:, 1:2], warm[:, 0:1], ACT.Sigmoid)
+
+        loads = ctx.enter_context(tc.tile_pool(name="loads", bufs=1))
+        tab_w = loads.tile([P, T], I32, name="tab_w", align_bytes=64)
+        tab2_w = loads.tile([P, T], I32, name="tab2_w", align_bytes=64)
+        wa_raw = loads.tile([P, R // 2], I32, name="wa_raw", align_bytes=64)
+        wa_s_raw = loads.tile([P, R // 4], I32, name="wa_s_raw", tag="small_planes", align_bytes=64)
+        sm_sb = loads.tile([P, PACK], F32, name="sm_sb")
+        nc.vector.memset(wa_s_raw[:], 0)
+        nc.sync.dma_start(tab_w[:], tab_words[0].rearrange("p t i -> p (t i)").bitcast(I32))
+        nc.sync.dma_start(wa_raw[:], wa_words[0].bitcast(I32))
+        for q in range(QUADS):
+            nc.sync.dma_start(wa_s_raw[32 * q : 32 * q + 4, :], wa_scales[0, 4 * q : 4 * q + 4, :].bitcast(I32))
+        nc.sync.dma_start(sm_sb[:], sm.rearrange("(p t) -> p t", t=PACK))
+        nc.sync.dma_start(tab2_w[:], tab2_words[0].rearrange("p t i -> p (t i)").bitcast(I32))
+        wb_raw = {}
+        for a in range(2):
+            rows = wb[512 * a : 512 * (a + 1), :].rearrange("(p i) r -> p i r", i=PACK)
+            for h in range(2):
+                wb_raw[a, h] = loads.tile([P, PACK, HALF], F32, name="wb_raw%d%d" % (a, h))
+                nc.sync.dma_start(wb_raw[a, h][:], rows[:, :, HALF * h : HALF * (h + 1)])
+
+        en = {}
+
+        def load_en_words():
+            en["w"] = keep.tile([P, N], I32, name="en_w", tag="early_late", align_bytes=64)
+            nc.sync.dma_start(en["w"][:], en_words[0].rearrange("p n i -> p (n i)").bitcast(I32))
+
+        def load_en_scales():
+            en["s"] = loads.tile([P, N // 4], I32, name="en_s", tag="small_planes", align_bytes=64)
+            nc.gpsimd.memset(en["s"][:], 0)
+            for q in range(QUADS):
+                nc.sync.dma_start(en["s"][32 * q : 32 * q + 4, :], en_scales[0, 4 * q : 4 * q + 4, :].bitcast(I32))
+
+        got2_s = keep.tile([P, J], U8, name="got2_s", align_bytes=64)
+        got_s = {}
+        got_w = {}
+        parted = {}
+
+        spots = {
+            ("wb_bf", 0): 0, ("wb_bf", 1): 4096,
+            ("got_w", 0): 8192, ("got_w", 1): 10240, ("got_s", 0): 12288, ("got_s", 1): 12800,
+            ("got2_w", 0): 13312, ("got2_w", 1): 13312,
+            ("got_w", 2): 4096, ("got_s", 2): 6144, ("got_s", 3): 6144,
+            ("h_bf", 0): 15360, ("h_bf", 1): 17408, ("got2_w", 2): 17408, ("h_bf", 4): 15360, ("h_bf", 5): 17408,
+            ("h_bf", 2): 19456, ("h_bf", 3): 21504, ("got_w", 3): 19456, ("got2_w", 3): 21504,
+            ("h_bf", 6): 19456, ("h_bf", 7): 21504,
+        }
+
+        def place(shape, dtype, kind, index):
+            return arena.tile(shape, dtype, name="%s%d" % (kind, index), align_bytes=64, offset=spots[kind, index])
+
+        def gather_tab2_scales():
+            nc.vector.tensor_copy(got2_s[:], tab2_s[:].bitcast(U8).indirect(list2[:]))
+            for q in range(QUADS):
+                nc.sync.dma_start(moved_s[32 * q : 32 * q + 4, :], got2_s[32 * q + 4 : 32 * q + 8, :].bitcast(I32))
+
+        def gather_tab(c):
+            cols = slice(LIST_COLS * c, LIST_COLS * (c + 1))
+            got_s[c] = place([P, CHUNK], U8, "got_s", c)
+            nc.vector.tensor_copy(got_s[c][:], tab_s[:].bitcast(U8).indirect(list1[:, cols]))
+            got_w[c] = place([P, CHUNK], U32, "got_w", c)
+            nc.vector.tensor_copy(got_w[c][:], tab_w[:].bitcast(U32).indirect(list1[:, cols]))
+
+        def gather_tab2(c):
+            cols = slice(LIST_COLS * c, LIST_COLS * (c + 1))
+            both = place([P, CHUNK], U32, "got2_w", c)
+            nc.vector.tensor_copy(both[:], tab2_w[:].bitcast(U32).indirect(list2[:, cols]))
+            parted[c] = ring.tile([P, 4 * CHUNK], U8, name="parted", align_bytes=64)
+            nc.vector.tensor_copy(
+                parted[c][:].bitcast(U16).rearrange("p (d j) -> p d j", d=2),
+                both[:].bitcast(U16).rearrange("p (j d) -> p d j", d=2),
+            )
+
+        wa_w = keep.tile([P, 2 * R], U8, name="wa_w", align_bytes=64)
+        wa_s = keep.tile([P, R], U8, name="wa_s", align_bytes=64)
+
+        def permute_wa():
+            nc.vector.tensor_copy(
+                wa_w[:].bitcast(U16).rearrange("p (t m) -> p t m", t=PACK),
+                wa_raw[:].bitcast(U16).rearrange("p (m t) -> p t m", t=PACK),
+            )
+            nc.vector.tensor_copy(
+                wa_s[:].rearrange("p (t m) -> p t m", t=PACK),
+                wa_s_raw[:].bitcast(U8).rearrange("p (m t) -> p t m", t=PACK),
+            )
+
+        wb_bf = [place([P, PACK, P, PACK], BF16, "wb_bf", a) for a in range(2)]
+        wb_w = [keep.tile([P, R], U32, name="wb_w%d" % a, align_bytes=64) for a in range(2)]
+        wb_s = [keep.tile([P, R], U8, name="wb_s%d" % a, align_bytes=64) for a in range(2)]
+
+        def round_wb(a, h, copy):
+            copy(
+                wb_bf[a][:, :, 64 * h : 64 * (h + 1), :].rearrange("p t m i -> p m t i"),
+                wb_raw[a, h][:].rearrange("p i (m t) -> p m t i", t=PACK),
+            )
+
+        def quantize_wb(a, t0, t1):
+            nc.vector.quantize_mx(
+                out=wb_w[a][:, P * t0 : P * t1].bitcast(FP8X4),
+                scales=wb_s[a][:, P * t0 : P * t1],
+                in_=wb_bf[a][:, t0:t1].rearrange("p t m i -> p (t m i)"),
+            )
+
+        z = {}
+
+        def z_pass(c, step, tiles):
+            for t in tiles:
+                cols = slice(P * t, P * (t + 1))
+                if step == 0:
+                    z[c, t] = psum.tile([P, CHUNK], F32, name="bank")
+                    nc.tensor.matmul_mx(
+                        out=z[c, t][:],
+                        lhsT=wa_w[:, 2 * P * t : 2 * P * (t + 1)].bitcast(FP4X4),
+                        lhsT_scale=wa_s[:, cols],
+                        rhs=got_w[c][:].bitcast(FP8X4),
+                        rhs_scale=got_s[c][:],
+                        start=True,
+                        stop=False,
+                    )
+                else:
+                    a = step - 1
+                    plane = got2_s[:] if a == 0 else moved_s[:].bitcast(U8)
+                    nc.tensor.matmul_mx(
+                        out=z[c, t][:],
+                        lhsT=wb_w[a][:, cols].bitcast(FP8X4),
+                        lhsT_scale=wb_s[a][:, cols],
+                        rhs=parted[c][:, 2 * CHUNK * a : 2 * CHUNK * (a + 1)].bitcast(FP4X4),
+                        rhs_scale=plane[:, CHUNK * c : CHUNK * (c + 1)],
+                        start=False,
+                        stop=(a == 1),
+                    )
+
+        tanh_z = {}
+        h_bf = {}
+        h_w = {}
+        h_s = {}
+
+        def tanh_chunk(c, pieces):
+            tanh_z[c] = ring.tile([P, PACK, CHUNK], F32, name="tanh_z")
+            width = CHUNK // pieces
+            for piece in range(pieces):
+                cols = slice(width * piece, width * (piece + 1))
+                for t in range(PACK):
+                    nc.scalar.activation(tanh_z[c][:, t, cols], z[c, t][:, cols], ACT.Tanh)
+
+        def make_h(c):
+            half = CHUNK // 2
+            h_w[c] = ring.tile([P, CHUNK], U32, name="h_w", align_bytes=64)
+            h_s[c] = ring.tile([P, CHUNK], U8, name="h_s", align_bytes=64)
+            for s in range(2):
+                h_bf[c, s] = place([P, half * PACK], BF16, "h_bf", 2 * c + s)
+                nc.vector.tensor_tensor(
+                    h_bf[c, s][:].rearrange("p (g e t) -> p g t e", e=2, t=PACK),
+                    tanh_z[c][:, :, half * s : half * (s + 1)].rearrange("p t (g e) -> p g t e", e=2),
+                    sm_sb[:].rearrange("p (g t e) -> p g t e", g=1, e=1).to_broadcast([P, half // 2, PACK, 2]),
+                    MULT,
+                )
+            for s in range(2):
+                cols = slice(half * s, half * (s + 1))
+                nc.vector.quantize_mx(out=h_w[c][:, cols].bitcast(FP8X4), scales=h_s[c][:, cols], in_=h_bf[c, s][:])
+
+        def z_tab2(c):
+            for t in range(PACK):
+                z_pass(c, 1, [t])
+                z_pass(c, 2, [t])
+
+        def score_chunk(c):
+            for b in range(N // P):
+                cols = slice(P * b, P * (b + 1))
+                y = psum.tile([P, CHUNK], F32, name="bank")
+                nc.tensor.matmul_mx(
+                    out=y[:],
+                    lhsT=en["w"][:, cols].bitcast(FP8X4),
+                    lhsT_scale=en["s"][:].bitcast(U8)[:, cols],
+                    rhs=h_w[c][:].bitcast(FP8X4),
+                    rhs_scale=h_s[c][:],
+                    start=True,
+                    stop=True,
+                )
+                prob = stage.tile([P, CHUNK], F32, name="prob")
+                nc.scalar.activation(prob[:], y[:], ACT.Sigmoid)
+                nc.sync.dma_start(out[cols, CHUNK * c : CHUNK * (c + 1)], prob[:])
+
+        every = range(PACK)
+        gather_tab2_scales()
+        load_en_words()
+        gather_tab(0)
+        gather_tab(1)
+        permute_wa()
+        load_en_scales()
+        z_pass(0, 0, every)
+        z_pass(1, 0, every)
+        gather_tab2(0)
+        round_wb(0, 0, nc.scalar.copy)
+        round_wb(0, 1, nc.scalar.copy)
+        round_wb(1, 0, nc.scalar.copy)
+        quantize_wb(0, 0, PACK)
+        z_pass(0, 1, every)
+        round_wb(1, 1, nc.vector.tensor_copy)
+        for t in range(PACK):
+            quantize_wb(1, t, t + 1)
+        z_pass(0, 2, every)
+        gather_tab2(1)
+        gather_tab(2)
+        tanh_chunk(0, 2)
+        z_tab2(1)
+        make_h(0)
+        tanh_chunk(1, 1)
+        for c in range(CHUNKS):
+            if c == 1:
+                gather_tab(3)
+            if c + 2 < CHUNKS:
+                gather_tab2(c + 2)
+            score_chunk(c)
+            if c + 1 < CHUNKS:
+                make_h(c + 1)
+            if c + 2 < CHUNKS:
+                z_pass(c + 2, 0, every)
+                z_tab2(c + 2)
+                tanh_chunk(c + 2, 1)

@@ -22,7 +22,6 @@ CHUNK = 512
 CHUNKS = J // CHUNK
 LIST_COLS = CHUNK // 16
 QUADS = 4
-HALF = R // 2
 
 
 def tile_list_kg_tanh_sig_kernel(
@@ -40,9 +39,32 @@ def tile_list_kg_tanh_sig_kernel(
         list2 = keep.tile([P, J // 16], U16, name="list2")
         nc.sync.dma_start(list2[:], offs2)
         nc.sync.dma_start(list1[:], offs)
+        wb_raw = {}
+
+        def load_wb(pool, a, i0, i1):
+            wb_raw[a, i0] = pool.tile([P, i1 - i0, R], F32, name="wb_raw%d%d" % (a, i0))
+            rows = wb[512 * a : 512 * (a + 1), :].rearrange("(p i) r -> p i r", i=PACK)
+            nc.sync.dma_start(wb_raw[a, i0][:], rows[:, i0:i1, :])
+
+        load_wb(keep, 0, 0, 2)
+
+        spots = {
+            ("en_w", 0): 0, ("tab2_s", 0): 4032, ("en_s", 0): 4096, ("got_s", 0): 5120, ("wa_s", 0): 6144,
+            ("wb_s", 0): 6656, ("wb_s", 1): 7168, ("sm", 0): 7680, ("tab_w", 0): 7744,
+            ("got_s", 3): 26112, ("got2_w", 2): 26112, ("h_bf", 0): 26624, ("h_bf", 4): 26624,
+            ("h_bf", 1): 29696, ("got_w", 2): 29696, ("h_bf", 5): 29696,
+            ("h_bf", 2): 31744, ("got2_w", 3): 31744, ("h_bf", 6): 31744,
+            ("h_bf", 3): 33792, ("got_w", 3): 33792, ("h_bf", 7): 33792,
+            ("got_w", 0): 35840, ("parted", 1): 35840, ("parted", 3): 35840,
+            ("got2_w", 0): 37888, ("got_s", 2): 37888, ("got2_w", 1): 38400,
+            ("got_w", 1): 41984, ("wa_w", 0): 44032, ("parted", 0): 45056, ("parted", 2): 45056,
+        }
+
+        def place(shape, dtype, kind, index):
+            return arena.tile(shape, dtype, name="%s%d" % (kind, index), align_bytes=64, offset=spots[kind, index])
 
         tab_s = keep.tile([P, T // 4], I32, name="tab_s", align_bytes=64)
-        tab2_s = keep.tile([P, T // 4], I32, name="tab2_s", tag="early_late", align_bytes=64)
+        tab2_s = place([P, T // 4], I32, "tab2_s", 0)
         moved_s = keep.tile([P, J // 4], I32, name="moved_s", align_bytes=64)
         nc.vector.memset(tab2_s[:], 0)
         nc.vector.memset(tab_s[:], 0)
@@ -58,54 +80,43 @@ def tile_list_kg_tanh_sig_kernel(
             nc.scalar.activation(warm[:, 1:2], warm[:, 0:1], ACT.Sigmoid)
 
         loads = ctx.enter_context(tc.tile_pool(name="loads", bufs=1))
-        tab_w = loads.tile([P, T], I32, name="tab_w", align_bytes=64)
         tab2_w = loads.tile([P, T], I32, name="tab2_w", align_bytes=64)
         wa_raw = loads.tile([P, R // 2], I32, name="wa_raw", align_bytes=64)
-        wa_s_raw = loads.tile([P, R // 4], I32, name="wa_s_raw", tag="small_planes", align_bytes=64)
-        sm_sb = loads.tile([P, PACK], F32, name="sm_sb")
+        wa_s_raw = loads.tile([P, R // 4], I32, name="wa_s_raw", align_bytes=64)
         nc.vector.memset(wa_s_raw[:], 0)
-        nc.sync.dma_start(tab_w[:], tab_words[0].rearrange("p t i -> p (t i)").bitcast(I32))
+        load_wb(loads, 0, 2, 4)
+        load_wb(loads, 1, 0, 4)
         nc.sync.dma_start(wa_raw[:], wa_words[0].bitcast(I32))
         for q in range(QUADS):
             nc.sync.dma_start(wa_s_raw[32 * q : 32 * q + 4, :], wa_scales[0, 4 * q : 4 * q + 4, :].bitcast(I32))
-        nc.sync.dma_start(sm_sb[:], sm.rearrange("(p t) -> p t", t=PACK))
         nc.sync.dma_start(tab2_w[:], tab2_words[0].rearrange("p t i -> p (t i)").bitcast(I32))
-        wb_raw = {}
-        for a in range(2):
-            rows = wb[512 * a : 512 * (a + 1), :].rearrange("(p i) r -> p i r", i=PACK)
-            for h in range(2):
-                wb_raw[a, h] = loads.tile([P, PACK, HALF], F32, name="wb_raw%d%d" % (a, h))
-                nc.sync.dma_start(wb_raw[a, h][:], rows[:, :, HALF * h : HALF * (h + 1)])
 
-        en = {}
+        late = {}
 
-        def load_en_words():
-            en["w"] = keep.tile([P, N], I32, name="en_w", tag="early_late", align_bytes=64)
-            nc.sync.dma_start(en["w"][:], en_words[0].rearrange("p n i -> p (n i)").bitcast(I32))
-
-        def load_en_scales():
-            en["s"] = loads.tile([P, N // 4], I32, name="en_s", tag="small_planes", align_bytes=64)
-            nc.gpsimd.memset(en["s"][:], 0)
+        def load_late():
+            late["tab_w"] = place([P, T], I32, "tab_w", 0)
+            nc.sync.dma_start(late["tab_w"][:], tab_words[0].rearrange("p t i -> p (t i)").bitcast(I32))
+            late["en_w"] = place([P, N], I32, "en_w", 0)
+            nc.sync.dma_start(late["en_w"][:], en_words[0].rearrange("p n i -> p (n i)").bitcast(I32))
+            late["sm"] = place([P, PACK], F32, "sm", 0)
+            nc.sync.dma_start(late["sm"][:], sm.rearrange("(p t) -> p t", t=PACK))
+            late["en_s"] = place([P, N // 4], I32, "en_s", 0)
+            nc.gpsimd.memset(late["en_s"][:], 0)
             for q in range(QUADS):
-                nc.sync.dma_start(en["s"][32 * q : 32 * q + 4, :], en_scales[0, 4 * q : 4 * q + 4, :].bitcast(I32))
+                nc.sync.dma_start(late["en_s"][32 * q : 32 * q + 4, :], en_scales[0, 4 * q : 4 * q + 4, :].bitcast(I32))
 
-        got2_s = keep.tile([P, J], U8, name="got2_s", align_bytes=64)
         got_s = {}
+        got2_s = keep.tile([P, J], U8, name="got2_s", align_bytes=64)
         got_w = {}
+        got2_w = {}
         parted = {}
 
-        spots = {
-            ("wb_bf", 0): 0, ("wb_bf", 1): 4096,
-            ("got_w", 0): 8192, ("got_w", 1): 10240, ("got_s", 0): 12288, ("got_s", 1): 12800,
-            ("got2_w", 0): 13312, ("got2_w", 1): 13312,
-            ("got_w", 2): 4096, ("got_s", 2): 6144, ("got_s", 3): 6144,
-            ("h_bf", 0): 15360, ("h_bf", 1): 17408, ("got2_w", 2): 17408, ("h_bf", 4): 15360, ("h_bf", 5): 17408,
-            ("h_bf", 2): 19456, ("h_bf", 3): 21504, ("got_w", 3): 19456, ("got2_w", 3): 21504,
-            ("h_bf", 6): 19456, ("h_bf", 7): 21504,
-        }
-
-        def place(shape, dtype, kind, index):
-            return arena.tile(shape, dtype, name="%s%d" % (kind, index), align_bytes=64, offset=spots[kind, index])
+        def gather_tab_scales(c, count):
+            picked = tab_s[:].bitcast(U8).indirect(list1[:, LIST_COLS * c : LIST_COLS * (c + count)])
+            plane = place([P, count * CHUNK], U8, "got_s", c)
+            nc.vector.tensor_copy(plane[:], picked)
+            for k in range(count):
+                got_s[c + k] = plane[:, CHUNK * k : CHUNK * (k + 1)]
 
         def gather_tab2_scales():
             nc.vector.tensor_copy(got2_s[:], tab2_s[:].bitcast(U8).indirect(list2[:]))
@@ -114,69 +125,58 @@ def tile_list_kg_tanh_sig_kernel(
 
         def gather_tab(c):
             cols = slice(LIST_COLS * c, LIST_COLS * (c + 1))
-            got_s[c] = place([P, CHUNK], U8, "got_s", c)
-            nc.vector.tensor_copy(got_s[c][:], tab_s[:].bitcast(U8).indirect(list1[:, cols]))
             got_w[c] = place([P, CHUNK], U32, "got_w", c)
-            nc.vector.tensor_copy(got_w[c][:], tab_w[:].bitcast(U32).indirect(list1[:, cols]))
+            nc.vector.tensor_copy(got_w[c][:], late["tab_w"][:].bitcast(U32).indirect(list1[:, cols]))
 
         def gather_tab2(c):
             cols = slice(LIST_COLS * c, LIST_COLS * (c + 1))
-            both = place([P, CHUNK], U32, "got2_w", c)
-            nc.vector.tensor_copy(both[:], tab2_w[:].bitcast(U32).indirect(list2[:, cols]))
-            parted[c] = ring.tile([P, 4 * CHUNK], U8, name="parted", align_bytes=64)
+            got2_w[c] = place([P, CHUNK], U32, "got2_w", c)
+            nc.vector.tensor_copy(got2_w[c][:], tab2_w[:].bitcast(U32).indirect(list2[:, cols]))
+
+        def part_tab2(c):
+            parted[c] = place([P, 4 * CHUNK], U8, "parted", c)
             nc.vector.tensor_copy(
                 parted[c][:].bitcast(U16).rearrange("p (d j) -> p d j", d=2),
-                both[:].bitcast(U16).rearrange("p (j d) -> p d j", d=2),
+                got2_w[c][:].bitcast(U16).rearrange("p (j d) -> p d j", d=2),
             )
 
-        wa_w = keep.tile([P, 2 * R], U8, name="wa_w", align_bytes=64)
-        wa_s = keep.tile([P, R], U8, name="wa_s", align_bytes=64)
+        wa_w = place([P, 2 * R], U8, "wa_w", 0)
+        wa_s = place([P, R], U8, "wa_s", 0)
 
         def permute_wa():
-            nc.vector.tensor_copy(
-                wa_w[:].bitcast(U16).rearrange("p (t m) -> p t m", t=PACK),
-                wa_raw[:].bitcast(U16).rearrange("p (m t) -> p t m", t=PACK),
-            )
             nc.vector.tensor_copy(
                 wa_s[:].rearrange("p (t m) -> p t m", t=PACK),
                 wa_s_raw[:].bitcast(U8).rearrange("p (m t) -> p t m", t=PACK),
             )
-
-        wb_bf = [place([P, PACK, P, PACK], BF16, "wb_bf", a) for a in range(2)]
-        wb_w = [keep.tile([P, R], U32, name="wb_w%d" % a, align_bytes=64) for a in range(2)]
-        wb_s = [keep.tile([P, R], U8, name="wb_s%d" % a, align_bytes=64) for a in range(2)]
-
-        def round_wb(a, h, copy):
-            copy(
-                wb_bf[a][:, :, 64 * h : 64 * (h + 1), :].rearrange("p t m i -> p m t i"),
-                wb_raw[a, h][:].rearrange("p i (m t) -> p m t i", t=PACK),
+            nc.vector.tensor_copy(
+                wa_w[:].bitcast(U16).rearrange("p (t m) -> p t m", t=PACK),
+                wa_raw[:].bitcast(U16).rearrange("p (m t) -> p t m", t=PACK),
             )
 
-        def quantize_wb(a, t0, t1):
+        wb_bf = [keep.tile([P, PACK, P, PACK], BF16, name="wb_bf%d" % a, align_bytes=64) for a in range(2)]
+        wb_w = [keep.tile([P, R], U32, name="wb_w%d" % a, align_bytes=64) for a in range(2)]
+        wb_s = [place([P, R], U8, "wb_s", a) for a in range(2)]
+
+        def quantize_wb(a):
+            for i0, i1 in ((0, 2), (2, 4)) if a == 0 else ((0, 4),):
+                nc.scalar.copy(
+                    wb_bf[a][:, :, :, i0:i1].rearrange("p t m i -> p m t i"),
+                    wb_raw[a, i0][:].rearrange("p i (m t) -> p m t i", t=PACK),
+                )
             nc.vector.quantize_mx(
-                out=wb_w[a][:, P * t0 : P * t1].bitcast(FP8X4),
-                scales=wb_s[a][:, P * t0 : P * t1],
-                in_=wb_bf[a][:, t0:t1].rearrange("p t m i -> p (t m i)"),
+                out=wb_w[a][:].bitcast(FP8X4), scales=wb_s[a][:], in_=wb_bf[a][:].rearrange("p t m i -> p (t m i)")
             )
 
         z = {}
 
-        def z_pass(c, step, tiles):
-            for t in tiles:
+        def open_z(c):
+            for t in range(PACK):
+                z[c, t] = psum.tile([P, CHUNK], F32, name="bank")
+
+        def z_tab2(c, first):
+            for t in range(PACK):
                 cols = slice(P * t, P * (t + 1))
-                if step == 0:
-                    z[c, t] = psum.tile([P, CHUNK], F32, name="bank")
-                    nc.tensor.matmul_mx(
-                        out=z[c, t][:],
-                        lhsT=wa_w[:, 2 * P * t : 2 * P * (t + 1)].bitcast(FP4X4),
-                        lhsT_scale=wa_s[:, cols],
-                        rhs=got_w[c][:].bitcast(FP8X4),
-                        rhs_scale=got_s[c][:],
-                        start=True,
-                        stop=False,
-                    )
-                else:
-                    a = step - 1
+                for a in range(2):
                     plane = got2_s[:] if a == 0 else moved_s[:].bitcast(U8)
                     nc.tensor.matmul_mx(
                         out=z[c, t][:],
@@ -184,21 +184,33 @@ def tile_list_kg_tanh_sig_kernel(
                         lhsT_scale=wb_s[a][:, cols],
                         rhs=parted[c][:, 2 * CHUNK * a : 2 * CHUNK * (a + 1)].bitcast(FP4X4),
                         rhs_scale=plane[:, CHUNK * c : CHUNK * (c + 1)],
-                        start=False,
-                        stop=(a == 1),
+                        start=(first and a == 0),
+                        stop=(not first and a == 1),
                     )
+
+        def z_tab(c, first):
+            for t in range(PACK):
+                nc.tensor.matmul_mx(
+                    out=z[c, t][:],
+                    lhsT=wa_w[:, 2 * P * t : 2 * P * (t + 1)].bitcast(FP4X4),
+                    lhsT_scale=wa_s[:, P * t : P * (t + 1)],
+                    rhs=got_w[c][:].bitcast(FP8X4),
+                    rhs_scale=got_s[c],
+                    start=first,
+                    stop=not first,
+                )
 
         tanh_z = {}
         h_bf = {}
         h_w = {}
         h_s = {}
 
-        def tanh_chunk(c, pieces):
+        def tanh_chunk(c, pieces, order):
             tanh_z[c] = ring.tile([P, PACK, CHUNK], F32, name="tanh_z")
             width = CHUNK // pieces
             for piece in range(pieces):
                 cols = slice(width * piece, width * (piece + 1))
-                for t in range(PACK):
+                for t in order:
                     nc.scalar.activation(tanh_z[c][:, t, cols], z[c, t][:, cols], ACT.Tanh)
 
         def make_h(c):
@@ -210,17 +222,12 @@ def tile_list_kg_tanh_sig_kernel(
                 nc.vector.tensor_tensor(
                     h_bf[c, s][:].rearrange("p (g e t) -> p g t e", e=2, t=PACK),
                     tanh_z[c][:, :, half * s : half * (s + 1)].rearrange("p t (g e) -> p g t e", e=2),
-                    sm_sb[:].rearrange("p (g t e) -> p g t e", g=1, e=1).to_broadcast([P, half // 2, PACK, 2]),
+                    late["sm"][:].rearrange("p (g t e) -> p g t e", g=1, e=1).to_broadcast([P, half // 2, PACK, 2]),
                     MULT,
                 )
             for s in range(2):
                 cols = slice(half * s, half * (s + 1))
                 nc.vector.quantize_mx(out=h_w[c][:, cols].bitcast(FP8X4), scales=h_s[c][:, cols], in_=h_bf[c, s][:])
-
-        def z_tab2(c):
-            for t in range(PACK):
-                z_pass(c, 1, [t])
-                z_pass(c, 2, [t])
 
         def score_chunk(c):
             for b in range(N // P):
@@ -228,8 +235,8 @@ def tile_list_kg_tanh_sig_kernel(
                 y = psum.tile([P, CHUNK], F32, name="bank")
                 nc.tensor.matmul_mx(
                     out=y[:],
-                    lhsT=en["w"][:, cols].bitcast(FP8X4),
-                    lhsT_scale=en["s"][:].bitcast(U8)[:, cols],
+                    lhsT=late["en_w"][:, cols].bitcast(FP8X4),
+                    lhsT_scale=late["en_s"][:].bitcast(U8)[:, cols],
                     rhs=h_w[c][:].bitcast(FP8X4),
                     rhs_scale=h_s[c][:],
                     start=True,
@@ -241,38 +248,39 @@ def tile_list_kg_tanh_sig_kernel(
 
         every = range(PACK)
         gather_tab2_scales()
-        load_en_words()
-        gather_tab(0)
-        gather_tab(1)
+        load_late()
+        gather_tab_scales(0, 2)
+        quantize_wb(0)
         permute_wa()
-        load_en_scales()
-        z_pass(0, 0, every)
-        z_pass(1, 0, every)
+        quantize_wb(1)
         gather_tab2(0)
-        round_wb(0, 0, nc.scalar.copy)
-        round_wb(0, 1, nc.scalar.copy)
-        round_wb(1, 0, nc.scalar.copy)
-        quantize_wb(0, 0, PACK)
-        z_pass(0, 1, every)
-        round_wb(1, 1, nc.vector.tensor_copy)
-        for t in range(PACK):
-            quantize_wb(1, t, t + 1)
-        z_pass(0, 2, every)
+        part_tab2(0)
+        open_z(0)
+        z_tab2(0, True)
         gather_tab2(1)
-        gather_tab(2)
-        tanh_chunk(0, 2)
-        z_tab2(1)
+        gather_tab_scales(2, 1)
+        gather_tab(0)
+        z_tab(0, False)
+        gather_tab(1)
+        part_tab2(1)
+        open_z(1)
+        z_tab(1, True)
+        z_tab2(1, False)
+        tanh_chunk(0, 2, every)
         make_h(0)
-        tanh_chunk(1, 1)
+        tanh_chunk(1, 1, every)
         for c in range(CHUNKS):
-            if c == 1:
-                gather_tab(3)
             if c + 2 < CHUNKS:
                 gather_tab2(c + 2)
+                part_tab2(c + 2)
+                gather_tab(c + 2)
+            if c == 0:
+                gather_tab_scales(3, 1)
             score_chunk(c)
             if c + 1 < CHUNKS:
                 make_h(c + 1)
             if c + 2 < CHUNKS:
-                z_pass(c + 2, 0, every)
-                z_tab2(c + 2)
-                tanh_chunk(c + 2, 1)
+                open_z(c + 2)
+                z_tab2(c + 2, True)
+                z_tab(c + 2, False)
+                tanh_chunk(c + 2, 1, every)

@@ -49,14 +49,14 @@ def tile_list_kg_tanh_sig_kernel(
         load_wb(keep, 0, 0, 2)
 
         spots = {
-            ("en_w", 0): 0, ("tab2_s", 0): 4032, ("en_s", 0): 4096, ("got_s", 0): 5120, ("wa_s", 0): 6144,
+            ("en_w", 0): 0, ("tab2_s", 0): 4032, ("en_s", 0): 4096, ("got_s", 2): 5120, ("wa_s", 0): 6144,
             ("wb_s", 0): 6656, ("wb_s", 1): 7168, ("sm", 0): 7680, ("tab_w", 0): 7744,
-            ("got_s", 3): 26112, ("got2_w", 2): 26112, ("h_bf", 0): 26624, ("h_bf", 4): 26624,
+            ("got_s", 0): 25600, ("got2_w", 2): 26624, ("h_bf", 0): 26624, ("h_bf", 4): 26624,
             ("h_bf", 1): 29696, ("got_w", 2): 29696, ("h_bf", 5): 29696,
             ("h_bf", 2): 31744, ("got2_w", 3): 31744, ("h_bf", 6): 31744,
             ("h_bf", 3): 33792, ("got_w", 3): 33792, ("h_bf", 7): 33792,
             ("got_w", 0): 35840, ("parted", 1): 35840, ("parted", 3): 35840,
-            ("got2_w", 0): 37888, ("got_s", 2): 37888, ("got2_w", 1): 38400,
+            ("got2_w", 0): 37888, ("got_s", 3): 37888, ("got2_w", 1): 38400,
             ("got_w", 1): 41984, ("wa_w", 0): 44032, ("parted", 0): 45056, ("parted", 2): 45056,
         }
 
@@ -66,12 +66,12 @@ def tile_list_kg_tanh_sig_kernel(
         tab_s = keep.tile([P, T // 4], I32, name="tab_s", align_bytes=64)
         tab2_s = place([P, T // 4], I32, "tab2_s", 0)
         moved_s = keep.tile([P, J // 4], I32, name="moved_s", align_bytes=64)
-        nc.vector.memset(tab2_s[:], 0)
         nc.vector.memset(tab_s[:], 0)
-        for q in range(QUADS):
-            nc.sync.dma_start(tab2_s[32 * q : 32 * q + 8, :], tab2_scales[:, 4 * q : 4 * q + 4, :].bitcast(I32))
+        nc.vector.memset(tab2_s[:], 0)
         for q in range(QUADS):
             nc.sync.dma_start(tab_s[32 * q : 32 * q + 4, :], tab_scales[0, 4 * q : 4 * q + 4, :].bitcast(I32))
+        for q in range(QUADS):
+            nc.sync.dma_start(tab2_s[32 * q : 32 * q + 8, :], tab2_scales[:, 4 * q : 4 * q + 4, :].bitcast(I32))
         nc.vector.memset(moved_s[:], 0)
 
         with tc.tile_pool(name="first", bufs=1) as first:
@@ -220,9 +220,9 @@ def tile_list_kg_tanh_sig_kernel(
             for s in range(2):
                 h_bf[c, s] = place([P, half * PACK], BF16, "h_bf", 2 * c + s)
                 nc.vector.tensor_tensor(
-                    h_bf[c, s][:].rearrange("p (g e t) -> p g t e", e=2, t=PACK),
-                    tanh_z[c][:, :, half * s : half * (s + 1)].rearrange("p t (g e) -> p g t e", e=2),
-                    late["sm"][:].rearrange("p (g t e) -> p g t e", g=1, e=1).to_broadcast([P, half // 2, PACK, 2]),
+                    h_bf[c, s][:].rearrange("p (g e t) -> p g t e", e=4, t=PACK),
+                    tanh_z[c][:, :, half * s : half * (s + 1)].rearrange("p t (g e) -> p g t e", e=4),
+                    late["sm"][:].rearrange("p (g t e) -> p g t e", g=1, e=1).to_broadcast([P, half // 4, PACK, 4]),
                     MULT,
                 )
             for s in range(2):
@@ -247,18 +247,19 @@ def tile_list_kg_tanh_sig_kernel(
                 nc.sync.dma_start(out[cols, CHUNK * c : CHUNK * (c + 1)], prob[:])
 
         every = range(PACK)
+        gather_tab_scales(0, 2)
         gather_tab2_scales()
         load_late()
-        gather_tab_scales(0, 2)
         quantize_wb(0)
         permute_wa()
         quantize_wb(1)
+        gather_tab_scales(2, 1)
         gather_tab2(0)
         part_tab2(0)
         open_z(0)
         z_tab2(0, True)
         gather_tab2(1)
-        gather_tab_scales(2, 1)
+        gather_tab_scales(3, 1)
         gather_tab(0)
         z_tab(0, False)
         gather_tab(1)
@@ -274,8 +275,6 @@ def tile_list_kg_tanh_sig_kernel(
                 gather_tab2(c + 2)
                 part_tab2(c + 2)
                 gather_tab(c + 2)
-            if c == 0:
-                gather_tab_scales(3, 1)
             score_chunk(c)
             if c + 1 < CHUNKS:
                 make_h(c + 1)

@@ -18,10 +18,39 @@ MULT = mybir.AluOpType.mult
 
 P = 128
 PACK = 4
+K_PASS = P * PACK
+V2_PASSES = L // K_PASS
 CHUNK = 512
 CHUNKS = J // CHUNK
+HALF_CHUNK = CHUNK // 2
 LIST_COLS = CHUNK // 16
-QUADS = 4
+BLOCKS = 16
+QUAD = 32
+QUAD_ROWS = 4
+PASS1_SHIFT = 16
+RUN = 4
+
+ARENA = {
+    ("v2_scale_window", 0): 4032,
+    ("en_words", 0): 0,
+    ("en_plane", 0): 4096,
+    ("v_plane", 2): 5120,
+    ("wa_plane", 0): 6144,
+    ("wb_plane", 0): 6656,
+    ("wb_plane", 1): 7168,
+    ("sm", 0): 7680,
+    ("v_window", 0): 7744,
+    ("h_bf", 0): 26624, ("v2_words", 2): 26624, ("h_bf", 4): 26624,
+    ("h_bf", 1): 29696, ("v_words", 2): 29696, ("h_bf", 5): 29696,
+    ("h_bf", 2): 31744, ("v2_words", 3): 31744, ("h_bf", 6): 31744,
+    ("h_bf", 3): 33792, ("v_words", 3): 33792, ("h_bf", 7): 33792,
+    ("v_words", 0): 35840, ("v2_parted", 1): 35840, ("v2_parted", 3): 35840,
+    ("v2_words", 0): 37888, ("v_plane", 3): 37888, ("v2_words", 1): 38400,
+    ("v2_parted", 0): 45056, ("v2_parted", 2): 45056,
+    ("v_plane", 0): 25600,
+    ("v_words", 1): 41984,
+    ("wa_words", 0): 44032,
+}
 
 
 def tile_list_kg_tanh_sig_kernel(
@@ -32,47 +61,39 @@ def tile_list_kg_tanh_sig_kernel(
         keep = ctx.enter_context(tc.tile_pool(name="keep", bufs=1))
         ring = ctx.enter_context(tc.tile_pool(name="ring", bufs=2))
         arena = ctx.enter_context(tc.tile_pool(name="arena", bufs=1))
-        stage = ctx.enter_context(tc.tile_pool(name="stage", bufs=8))
+        stage = ctx.enter_context(tc.tile_pool(name="stage", bufs=N // P))
         psum = ctx.enter_context(tc.psum_pool(name="psum", bufs=8))
+
+        def place(shape, dtype, kind, index=0):
+            return arena.tile(shape, dtype, name="%s%d" % (kind, index), align_bytes=64, offset=ARENA[kind, index])
+
+        def load_plane(plane, scales):
+            for r in range(QUAD_ROWS):
+                nc.sync.dma_start(plane[r:P:QUAD, :], scales[0, r:BLOCKS:QUAD_ROWS, :].bitcast(I32))
+
+        wb_raw = {}
+
+        def load_wb(pool, a, i0, i1):
+            wb_raw[a, i0] = pool.tile([P, i1 - i0, R], F32, name="wb_raw%d%d" % (a, i0))
+            rows = wb[K_PASS * a : K_PASS * (a + 1), :].rearrange("(p i) r -> p i r", i=PACK)
+            nc.sync.dma_start(wb_raw[a, i0][:], rows[:, i0:i1, :])
 
         list1 = keep.tile([P, J // 16], U16, name="list1")
         list2 = keep.tile([P, J // 16], U16, name="list2")
         nc.sync.dma_start(list2[:], offs2)
         nc.sync.dma_start(list1[:], offs)
-        wb_raw = {}
+        load_wb(keep, 0, 0, PACK // 2)
 
-        def load_wb(pool, a, i0, i1):
-            wb_raw[a, i0] = pool.tile([P, i1 - i0, R], F32, name="wb_raw%d%d" % (a, i0))
-            rows = wb[512 * a : 512 * (a + 1), :].rearrange("(p i) r -> p i r", i=PACK)
-            nc.sync.dma_start(wb_raw[a, i0][:], rows[:, i0:i1, :])
-
-        load_wb(keep, 0, 0, 2)
-
-        spots = {
-            ("en_w", 0): 0, ("tab2_s", 0): 4032, ("en_s", 0): 4096, ("got_s", 2): 5120, ("wa_s", 0): 6144,
-            ("wb_s", 0): 6656, ("wb_s", 1): 7168, ("sm", 0): 7680, ("tab_w", 0): 7744,
-            ("got_s", 0): 25600, ("got2_w", 2): 26624, ("h_bf", 0): 26624, ("h_bf", 4): 26624,
-            ("h_bf", 1): 29696, ("got_w", 2): 29696, ("h_bf", 5): 29696,
-            ("h_bf", 2): 31744, ("got2_w", 3): 31744, ("h_bf", 6): 31744,
-            ("h_bf", 3): 33792, ("got_w", 3): 33792, ("h_bf", 7): 33792,
-            ("got_w", 0): 35840, ("parted", 1): 35840, ("parted", 3): 35840,
-            ("got2_w", 0): 37888, ("got_s", 3): 37888, ("got2_w", 1): 38400,
-            ("got_w", 1): 41984, ("wa_w", 0): 44032, ("parted", 0): 45056, ("parted", 2): 45056,
-        }
-
-        def place(shape, dtype, kind, index):
-            return arena.tile(shape, dtype, name="%s%d" % (kind, index), align_bytes=64, offset=spots[kind, index])
-
-        tab_s = keep.tile([P, T // 4], I32, name="tab_s", align_bytes=64)
-        tab2_s = place([P, T // 4], I32, "tab2_s", 0)
-        moved_s = keep.tile([P, J // 4], I32, name="moved_s", align_bytes=64)
-        nc.vector.memset(tab_s[:], 0)
-        nc.vector.memset(tab2_s[:], 0)
-        for q in range(QUADS):
-            nc.sync.dma_start(tab_s[32 * q : 32 * q + 4, :], tab_scales[0, 4 * q : 4 * q + 4, :].bitcast(I32))
-        for q in range(QUADS):
-            nc.sync.dma_start(tab2_s[32 * q : 32 * q + 8, :], tab2_scales[:, 4 * q : 4 * q + 4, :].bitcast(I32))
-        nc.vector.memset(moved_s[:], 0)
+        v_scale_window = keep.tile([P, T // 4], I32, name="v_scale_window", align_bytes=64)
+        v2_scale_window = place([P, T // 4], I32, "v2_scale_window")
+        v2_plane1 = keep.tile([P, J // 4], I32, name="v2_plane1", align_bytes=64)
+        nc.vector.memset(v_scale_window[:], 0)
+        nc.vector.memset(v2_scale_window[:], 0)
+        load_plane(v_scale_window, tab_scales)
+        for r in range(QUAD_ROWS):
+            rows = tab2_scales[:, r:BLOCKS:QUAD_ROWS, :].rearrange("a q t -> q a t")
+            nc.sync.dma_start(v2_scale_window[r:P:PASS1_SHIFT, :], rows.bitcast(I32))
+        nc.vector.memset(v2_plane1[:], 0)
 
         with tc.tile_pool(name="first", bufs=1) as first:
             warm = first.tile([P, 2], F32, name="warm")
@@ -80,91 +101,90 @@ def tile_list_kg_tanh_sig_kernel(
             nc.scalar.activation(warm[:, 1:2], warm[:, 0:1], ACT.Sigmoid)
 
         loads = ctx.enter_context(tc.tile_pool(name="loads", bufs=1))
-        tab2_w = loads.tile([P, T], I32, name="tab2_w", align_bytes=64)
-        wa_raw = loads.tile([P, R // 2], I32, name="wa_raw", align_bytes=64)
-        wa_s_raw = loads.tile([P, R // 4], I32, name="wa_s_raw", align_bytes=64)
-        nc.vector.memset(wa_s_raw[:], 0)
-        load_wb(loads, 0, 2, 4)
-        load_wb(loads, 1, 0, 4)
-        nc.sync.dma_start(wa_raw[:], wa_words[0].bitcast(I32))
-        for q in range(QUADS):
-            nc.sync.dma_start(wa_s_raw[32 * q : 32 * q + 4, :], wa_scales[0, 4 * q : 4 * q + 4, :].bitcast(I32))
-        nc.sync.dma_start(tab2_w[:], tab2_words[0].rearrange("p t i -> p (t i)").bitcast(I32))
+        v2_window = loads.tile([P, T], I32, name="v2_window", align_bytes=64)
+        wa_words_raw = loads.tile([P, R // 2], I32, name="wa_words_raw", align_bytes=64)
+        wa_plane_raw = loads.tile([P, R // 4], I32, name="wa_plane_raw", align_bytes=64)
+        nc.vector.memset(wa_plane_raw[:], 0)
+        load_wb(loads, 0, PACK // 2, PACK)
+        load_wb(loads, 1, 0, PACK)
+        nc.sync.dma_start(wa_words_raw[:], wa_words[0].bitcast(I32))
+        load_plane(wa_plane_raw, wa_scales)
+        nc.sync.dma_start(v2_window[:], tab2_words[0].rearrange("p t i -> p (t i)").bitcast(I32))
 
-        late = {}
+        v2_plane0 = keep.tile([P, J], U8, name="v2_plane0", align_bytes=64)
+        v_plane = {}
+        v_words = {}
+        v2_words = {}
+        v2_parted = {}
 
-        def load_late():
-            late["tab_w"] = place([P, T], I32, "tab_w", 0)
-            nc.sync.dma_start(late["tab_w"][:], tab_words[0].rearrange("p t i -> p (t i)").bitcast(I32))
-            late["en_w"] = place([P, N], I32, "en_w", 0)
-            nc.sync.dma_start(late["en_w"][:], en_words[0].rearrange("p n i -> p (n i)").bitcast(I32))
-            late["sm"] = place([P, PACK], F32, "sm", 0)
-            nc.sync.dma_start(late["sm"][:], sm.rearrange("(p t) -> p t", t=PACK))
-            late["en_s"] = place([P, N // 4], I32, "en_s", 0)
-            nc.gpsimd.memset(late["en_s"][:], 0)
-            for q in range(QUADS):
-                nc.sync.dma_start(late["en_s"][32 * q : 32 * q + 4, :], en_scales[0, 4 * q : 4 * q + 4, :].bitcast(I32))
-
-        got_s = {}
-        got2_s = keep.tile([P, J], U8, name="got2_s", align_bytes=64)
-        got_w = {}
-        got2_w = {}
-        parted = {}
-
-        def gather_tab_scales(c, count):
-            picked = tab_s[:].bitcast(U8).indirect(list1[:, LIST_COLS * c : LIST_COLS * (c + count)])
-            plane = place([P, count * CHUNK], U8, "got_s", c)
-            nc.vector.tensor_copy(plane[:], picked)
+        def gather_v_scales(c, count):
+            picked = v_scale_window[:].bitcast(U8).indirect(list1[:, LIST_COLS * c : LIST_COLS * (c + count)])
+            planes = place([P, count * CHUNK], U8, "v_plane", c)
+            nc.vector.tensor_copy(planes[:], picked)
             for k in range(count):
-                got_s[c + k] = plane[:, CHUNK * k : CHUNK * (k + 1)]
+                v_plane[c + k] = planes[:, CHUNK * k : CHUNK * (k + 1)]
 
-        def gather_tab2_scales():
-            nc.vector.tensor_copy(got2_s[:], tab2_s[:].bitcast(U8).indirect(list2[:]))
-            for q in range(QUADS):
-                nc.sync.dma_start(moved_s[32 * q : 32 * q + 4, :], got2_s[32 * q + 4 : 32 * q + 8, :].bitcast(I32))
+        gather_v_scales(0, 2)
 
-        def gather_tab(c):
-            cols = slice(LIST_COLS * c, LIST_COLS * (c + 1))
-            got_w[c] = place([P, CHUNK], U32, "got_w", c)
-            nc.vector.tensor_copy(got_w[c][:], late["tab_w"][:].bitcast(U32).indirect(list1[:, cols]))
+        nc.vector.tensor_copy(v2_plane0[:], v2_scale_window[:].bitcast(U8).indirect(list2[:]))
+        for r in range(QUAD_ROWS):
+            nc.sync.dma_start(v2_plane1[r:P:QUAD, :], v2_plane0[PASS1_SHIFT + r : P : QUAD, :].bitcast(I32))
+        v2_planes = (v2_plane0[:], v2_plane1[:].bitcast(U8))
 
-        def gather_tab2(c):
-            cols = slice(LIST_COLS * c, LIST_COLS * (c + 1))
-            got2_w[c] = place([P, CHUNK], U32, "got2_w", c)
-            nc.vector.tensor_copy(got2_w[c][:], tab2_w[:].bitcast(U32).indirect(list2[:, cols]))
+        v_window = place([P, T], I32, "v_window")
+        nc.sync.dma_start(v_window[:], tab_words[0].rearrange("p t i -> p (t i)").bitcast(I32))
+        en_codes = place([P, N], I32, "en_words")
+        nc.sync.dma_start(en_codes[:], en_words[0].rearrange("p n i -> p (n i)").bitcast(I32))
+        sm_slots = place([P, PACK], F32, "sm")
+        nc.sync.dma_start(sm_slots[:], sm.rearrange("(p t) -> p t", t=PACK))
+        en_plane = place([P, N // 4], I32, "en_plane")
+        nc.gpsimd.memset(en_plane[:], 0)
+        load_plane(en_plane, en_scales)
 
-        def part_tab2(c):
-            parted[c] = place([P, 4 * CHUNK], U8, "parted", c)
+        def gather_v(c):
+            offsets = list1[:, LIST_COLS * c : LIST_COLS * (c + 1)]
+            v_words[c] = place([P, CHUNK], U32, "v_words", c)
+            nc.vector.tensor_copy(v_words[c][:], v_window[:].bitcast(U32).indirect(offsets))
+
+        def gather_v2(c):
+            offsets = list2[:, LIST_COLS * c : LIST_COLS * (c + 1)]
+            v2_words[c] = place([P, CHUNK], U32, "v2_words", c)
+            nc.vector.tensor_copy(v2_words[c][:], v2_window[:].bitcast(U32).indirect(offsets))
+
+        def part_v2(c):
+            v2_parted[c] = place([P, 2 * V2_PASSES * CHUNK], U8, "v2_parted", c)
             nc.vector.tensor_copy(
-                parted[c][:].bitcast(U16).rearrange("p (d j) -> p d j", d=2),
-                got2_w[c][:].bitcast(U16).rearrange("p (j d) -> p d j", d=2),
+                v2_parted[c][:].bitcast(U16).rearrange("p (a j) -> p a j", a=V2_PASSES),
+                v2_words[c][:].bitcast(U16).rearrange("p (j a) -> p a j", a=V2_PASSES),
             )
 
-        wa_w = place([P, 2 * R], U8, "wa_w", 0)
-        wa_s = place([P, R], U8, "wa_s", 0)
+        wa_codes = place([P, 2 * R], U8, "wa_words")
+        wa_plane = place([P, R], U8, "wa_plane")
 
-        def permute_wa():
+        def reorder_wa():
             nc.vector.tensor_copy(
-                wa_s[:].rearrange("p (t m) -> p t m", t=PACK),
-                wa_s_raw[:].bitcast(U8).rearrange("p (m t) -> p t m", t=PACK),
+                wa_plane[:].rearrange("p (t m) -> p t m", t=PACK),
+                wa_plane_raw[:].bitcast(U8).rearrange("p (m t) -> p t m", t=PACK),
             )
             nc.vector.tensor_copy(
-                wa_w[:].bitcast(U16).rearrange("p (t m) -> p t m", t=PACK),
-                wa_raw[:].bitcast(U16).rearrange("p (m t) -> p t m", t=PACK),
+                wa_codes[:].bitcast(U16).rearrange("p (t m) -> p t m", t=PACK),
+                wa_words_raw[:].bitcast(U16).rearrange("p (m t) -> p t m", t=PACK),
             )
 
-        wb_bf = [keep.tile([P, PACK, P, PACK], BF16, name="wb_bf%d" % a, align_bytes=64) for a in range(2)]
-        wb_w = [keep.tile([P, R], U32, name="wb_w%d" % a, align_bytes=64) for a in range(2)]
-        wb_s = [place([P, R], U8, "wb_s", a) for a in range(2)]
+        wb_bf = [keep.tile([P, PACK, P, PACK], BF16, name="wb_bf%d" % a, align_bytes=64) for a in range(V2_PASSES)]
+        wb_codes = [keep.tile([P, R], U32, name="wb_codes%d" % a, align_bytes=64) for a in range(V2_PASSES)]
+        wb_plane = [place([P, R], U8, "wb_plane", a) for a in range(V2_PASSES)]
 
-        def quantize_wb(a):
-            for i0, i1 in ((0, 2), (2, 4)) if a == 0 else ((0, 4),):
+        def quantize_wb(a, pieces):
+            for i0, i1 in pieces:
                 nc.scalar.copy(
                     wb_bf[a][:, :, :, i0:i1].rearrange("p t m i -> p m t i"),
                     wb_raw[a, i0][:].rearrange("p i (m t) -> p m t i", t=PACK),
                 )
             nc.vector.quantize_mx(
-                out=wb_w[a][:].bitcast(FP8X4), scales=wb_s[a][:], in_=wb_bf[a][:].rearrange("p t m i -> p (t m i)")
+                out=wb_codes[a][:].bitcast(FP8X4),
+                scales=wb_plane[a][:],
+                in_=wb_bf[a][:].rearrange("p t m i -> p (t m i)"),
             )
 
         z = {}
@@ -173,72 +193,71 @@ def tile_list_kg_tanh_sig_kernel(
             for t in range(PACK):
                 z[c, t] = psum.tile([P, CHUNK], F32, name="bank")
 
-        def z_tab2(c, first):
+        def add_v2_passes(c, opens):
             for t in range(PACK):
                 cols = slice(P * t, P * (t + 1))
-                for a in range(2):
-                    plane = got2_s[:] if a == 0 else moved_s[:].bitcast(U8)
+                for a in range(V2_PASSES):
                     nc.tensor.matmul_mx(
                         out=z[c, t][:],
-                        lhsT=wb_w[a][:, cols].bitcast(FP8X4),
-                        lhsT_scale=wb_s[a][:, cols],
-                        rhs=parted[c][:, 2 * CHUNK * a : 2 * CHUNK * (a + 1)].bitcast(FP4X4),
-                        rhs_scale=plane[:, CHUNK * c : CHUNK * (c + 1)],
-                        start=(first and a == 0),
-                        stop=(not first and a == 1),
+                        lhsT=wb_codes[a][:, cols].bitcast(FP8X4),
+                        lhsT_scale=wb_plane[a][:, cols],
+                        rhs=v2_parted[c][:, 2 * CHUNK * a : 2 * CHUNK * (a + 1)].bitcast(FP4X4),
+                        rhs_scale=v2_planes[a][:, CHUNK * c : CHUNK * (c + 1)],
+                        start=(opens and a == 0),
+                        stop=(not opens and a == V2_PASSES - 1),
                     )
 
-        def z_tab(c, first):
+        def add_v_pass(c, opens):
             for t in range(PACK):
                 nc.tensor.matmul_mx(
                     out=z[c, t][:],
-                    lhsT=wa_w[:, 2 * P * t : 2 * P * (t + 1)].bitcast(FP4X4),
-                    lhsT_scale=wa_s[:, P * t : P * (t + 1)],
-                    rhs=got_w[c][:].bitcast(FP8X4),
-                    rhs_scale=got_s[c],
-                    start=first,
-                    stop=not first,
+                    lhsT=wa_codes[:, 2 * P * t : 2 * P * (t + 1)].bitcast(FP4X4),
+                    lhsT_scale=wa_plane[:, P * t : P * (t + 1)],
+                    rhs=v_words[c][:].bitcast(FP8X4),
+                    rhs_scale=v_plane[c],
+                    start=opens,
+                    stop=not opens,
                 )
 
         tanh_z = {}
-        h_bf = {}
-        h_w = {}
-        h_s = {}
+        h_codes = {}
+        h_plane = {}
 
-        def tanh_chunk(c, pieces, order):
+        def tanh_chunk(c, width):
             tanh_z[c] = ring.tile([P, PACK, CHUNK], F32, name="tanh_z")
-            width = CHUNK // pieces
-            for piece in range(pieces):
-                cols = slice(width * piece, width * (piece + 1))
-                for t in order:
-                    nc.scalar.activation(tanh_z[c][:, t, cols], z[c, t][:, cols], ACT.Tanh)
+            for j0 in range(0, CHUNK, width):
+                for t in range(PACK):
+                    nc.scalar.activation(tanh_z[c][:, t, j0 : j0 + width], z[c, t][:, j0 : j0 + width], ACT.Tanh)
 
         def make_h(c):
-            half = CHUNK // 2
-            h_w[c] = ring.tile([P, CHUNK], U32, name="h_w", align_bytes=64)
-            h_s[c] = ring.tile([P, CHUNK], U8, name="h_s", align_bytes=64)
-            for s in range(2):
-                h_bf[c, s] = place([P, half * PACK], BF16, "h_bf", 2 * c + s)
+            h_codes[c] = ring.tile([P, CHUNK], U32, name="h_codes", align_bytes=64)
+            h_plane[c] = ring.tile([P, CHUNK], U8, name="h_plane", align_bytes=64)
+            halves = [slice(HALF_CHUNK * s, HALF_CHUNK * (s + 1)) for s in range(2)]
+            factor = sm_slots[:].rearrange("p (g t e) -> p g t e", g=1, e=1)
+            h_bf = []
+            for s, cols in enumerate(halves):
+                h_bf.append(place([P, HALF_CHUNK * PACK], BF16, "h_bf", 2 * c + s))
                 nc.vector.tensor_tensor(
-                    h_bf[c, s][:].rearrange("p (g e t) -> p g t e", e=4, t=PACK),
-                    tanh_z[c][:, :, half * s : half * (s + 1)].rearrange("p t (g e) -> p g t e", e=4),
-                    late["sm"][:].rearrange("p (g t e) -> p g t e", g=1, e=1).to_broadcast([P, half // 4, PACK, 4]),
+                    h_bf[s][:].rearrange("p (g e t) -> p g t e", e=RUN, t=PACK),
+                    tanh_z[c][:, :, cols].rearrange("p t (g e) -> p g t e", e=RUN),
+                    factor.to_broadcast([P, HALF_CHUNK // RUN, PACK, RUN]),
                     MULT,
                 )
-            for s in range(2):
-                cols = slice(half * s, half * (s + 1))
-                nc.vector.quantize_mx(out=h_w[c][:, cols].bitcast(FP8X4), scales=h_s[c][:, cols], in_=h_bf[c, s][:])
+            for s, cols in enumerate(halves):
+                nc.vector.quantize_mx(
+                    out=h_codes[c][:, cols].bitcast(FP8X4), scales=h_plane[c][:, cols], in_=h_bf[s][:]
+                )
 
         def score_chunk(c):
-            for b in range(N // P):
-                cols = slice(P * b, P * (b + 1))
+            for n0 in range(0, N, P):
+                cols = slice(n0, n0 + P)
                 y = psum.tile([P, CHUNK], F32, name="bank")
                 nc.tensor.matmul_mx(
                     out=y[:],
-                    lhsT=late["en_w"][:, cols].bitcast(FP8X4),
-                    lhsT_scale=late["en_s"][:].bitcast(U8)[:, cols],
-                    rhs=h_w[c][:].bitcast(FP8X4),
-                    rhs_scale=h_s[c][:],
+                    lhsT=en_codes[:, cols].bitcast(FP8X4),
+                    lhsT_scale=en_plane[:].bitcast(U8)[:, cols],
+                    rhs=h_codes[c][:].bitcast(FP8X4),
+                    rhs_scale=h_plane[c][:],
                     start=True,
                     stop=True,
                 )
@@ -246,40 +265,38 @@ def tile_list_kg_tanh_sig_kernel(
                 nc.scalar.activation(prob[:], y[:], ACT.Sigmoid)
                 nc.sync.dma_start(out[cols, CHUNK * c : CHUNK * (c + 1)], prob[:])
 
-        every = range(PACK)
-        gather_tab_scales(0, 2)
-        gather_tab2_scales()
-        load_late()
-        quantize_wb(0)
-        permute_wa()
-        quantize_wb(1)
-        gather_tab_scales(2, 1)
-        gather_tab2(0)
-        part_tab2(0)
+        quantize_wb(0, ((0, PACK // 2), (PACK // 2, PACK)))
+        reorder_wa()
+        quantize_wb(1, ((0, PACK),))
+        gather_v_scales(2, 1)
+        gather_v2(0)
+        part_v2(0)
         open_z(0)
-        z_tab2(0, True)
-        gather_tab2(1)
-        gather_tab_scales(3, 1)
-        gather_tab(0)
-        z_tab(0, False)
-        gather_tab(1)
-        part_tab2(1)
+        add_v2_passes(0, True)
+        gather_v2(1)
+        gather_v_scales(3, 1)
+
+        gather_v(0)
+        add_v_pass(0, False)
+        gather_v(1)
+        part_v2(1)
         open_z(1)
-        z_tab(1, True)
-        z_tab2(1, False)
-        tanh_chunk(0, 2, every)
+        add_v_pass(1, True)
+        add_v2_passes(1, False)
+        tanh_chunk(0, HALF_CHUNK)
         make_h(0)
-        tanh_chunk(1, 1, every)
+        tanh_chunk(1, CHUNK)
+
         for c in range(CHUNKS):
             if c + 2 < CHUNKS:
-                gather_tab2(c + 2)
-                part_tab2(c + 2)
-                gather_tab(c + 2)
+                gather_v2(c + 2)
+                part_v2(c + 2)
+                gather_v(c + 2)
             score_chunk(c)
             if c + 1 < CHUNKS:
                 make_h(c + 1)
             if c + 2 < CHUNKS:
                 open_z(c + 2)
-                z_tab2(c + 2, True)
-                z_tab(c + 2, False)
-                tanh_chunk(c + 2, 1, every)
+                add_v2_passes(c + 2, True)
+                add_v_pass(c + 2, False)
+                tanh_chunk(c + 2, CHUNK)

@@ -27,30 +27,9 @@ LIST_COLS = CHUNK // 16
 BLOCKS = 16
 QUAD = 32
 QUAD_ROWS = 4
-PASS1_SHIFT = 16
+V2_ROWS_AT = P - V2_PASSES * BLOCKS
 RUN = 4
-
-ARENA = {
-    ("v2_scale_window", 0): 4032,
-    ("en_words", 0): 0,
-    ("en_plane", 0): 4096,
-    ("v_plane", 2): 5120,
-    ("wa_plane", 0): 6144,
-    ("wb_plane", 0): 6656,
-    ("wb_plane", 1): 7168,
-    ("sm", 0): 7680,
-    ("v_window", 0): 7744,
-    ("h_bf", 0): 26624, ("v2_words", 2): 26624, ("h_bf", 4): 26624,
-    ("h_bf", 1): 29696, ("v_words", 2): 29696, ("h_bf", 5): 29696,
-    ("h_bf", 2): 31744, ("v2_words", 3): 31744, ("h_bf", 6): 31744,
-    ("h_bf", 3): 33792, ("v_words", 3): 33792, ("h_bf", 7): 33792,
-    ("v_words", 0): 35840, ("v2_parted", 1): 35840, ("v2_parted", 3): 35840,
-    ("v2_words", 0): 37888, ("v_plane", 3): 37888, ("v2_words", 1): 38400,
-    ("v2_parted", 0): 45056, ("v2_parted", 2): 45056,
-    ("v_plane", 0): 25600,
-    ("v_words", 1): 41984,
-    ("wa_words", 0): 44032,
-}
+ALIGN = 64
 
 
 def tile_list_kg_tanh_sig_kernel(
@@ -62,104 +41,118 @@ def tile_list_kg_tanh_sig_kernel(
         ring = ctx.enter_context(tc.tile_pool(name="ring", bufs=2))
         arena = ctx.enter_context(tc.tile_pool(name="arena", bufs=1))
         stage = ctx.enter_context(tc.tile_pool(name="stage", bufs=N // P))
-        psum = ctx.enter_context(tc.psum_pool(name="psum", bufs=8))
+        psum = ctx.enter_context(tc.psum_pool(name="psum", bufs=1))
 
-        def place(shape, dtype, kind, index=0):
-            return arena.tile(shape, dtype, name="%s%d" % (kind, index), align_bytes=64, offset=ARENA[kind, index])
+        cells = {}
+        free = [0]
+
+        def cell(name, size):
+            cells[name] = free[0]
+            free[0] = free[0] + size
+
+        def place(name, shape, dtype, where, skip=0):
+            return arena.tile(shape, dtype, name=name, align_bytes=ALIGN, offset=cells[where] + skip)
+
+        cell("v2_words0", 4 * CHUNK)
+        cell("v2_words1", 4 * CHUNK)
+        cell("wb_bf0", 8 * R)
+        cell("wb_bf1", 8 * R)
+        cell("h_bf0", 4 * CHUNK)
+        cell("h_bf1", 4 * CHUNK)
+        cell("h_bf2", 5 * CHUNK)
+        cell("h_bf3", 4 * CHUNK)
 
         def load_plane(plane, scales):
             for r in range(QUAD_ROWS):
                 nc.sync.dma_start(plane[r:P:QUAD, :], scales[0, r:BLOCKS:QUAD_ROWS, :].bitcast(I32))
 
-        wb_raw = {}
-
-        def load_wb(pool, a, i0, i1):
-            wb_raw[a, i0] = pool.tile([P, i1 - i0, R], F32, name="wb_raw%d%d" % (a, i0))
-            rows = wb[K_PASS * a : K_PASS * (a + 1), :].rearrange("(p i) r -> p i r", i=PACK)
-            nc.sync.dma_start(wb_raw[a, i0][:], rows[:, i0:i1, :])
+        def load_wb(a):
+            raw = keep.tile([P, PACK, R], F32, name="wb_raw%d" % a)
+            nc.sync.dma_start(raw[:], wb[K_PASS * a : K_PASS * (a + 1), :].rearrange("(p i) r -> p i r", i=PACK))
+            return raw
 
         list1 = keep.tile([P, J // 16], U16, name="list1")
         list2 = keep.tile([P, J // 16], U16, name="list2")
-        nc.sync.dma_start(list2[:], offs2)
-        nc.sync.dma_start(list1[:], offs)
-        load_wb(keep, 0, 0, PACK // 2)
-
-        v_scale_window = keep.tile([P, T // 4], I32, name="v_scale_window", align_bytes=64)
-        v2_scale_window = place([P, T // 4], I32, "v2_scale_window")
-        v2_plane1 = keep.tile([P, J // 4], I32, name="v2_plane1", align_bytes=64)
-        nc.vector.memset(v_scale_window[:], 0)
-        nc.vector.memset(v2_scale_window[:], 0)
-        load_plane(v_scale_window, tab_scales)
-        for r in range(QUAD_ROWS):
-            rows = tab2_scales[:, r:BLOCKS:QUAD_ROWS, :].rearrange("a q t -> q a t")
-            nc.sync.dma_start(v2_scale_window[r:P:PASS1_SHIFT, :], rows.bitcast(I32))
-        nc.vector.memset(v2_plane1[:], 0)
-
-        with tc.tile_pool(name="first", bufs=1) as first:
-            warm = first.tile([P, 2], F32, name="warm")
-            nc.gpsimd.memset(warm[:, 0:1], 0.0)
-            nc.scalar.activation(warm[:, 1:2], warm[:, 0:1], ACT.Sigmoid)
-
-        loads = ctx.enter_context(tc.tile_pool(name="loads", bufs=1))
-        v2_window = loads.tile([P, T], I32, name="v2_window", align_bytes=64)
-        wa_words_raw = loads.tile([P, R // 2], I32, name="wa_words_raw", align_bytes=64)
-        wa_plane_raw = loads.tile([P, R // 4], I32, name="wa_plane_raw", align_bytes=64)
+        v2_scale_window = keep.tile([P, T // 4], I32, name="v2_scale_window", align_bytes=ALIGN)
+        v_scale_window = keep.tile([P, T // 4], I32, name="v_scale_window", align_bytes=ALIGN)
+        wa_plane_raw = keep.tile([P, R // 4], I32, name="wa_plane_raw", align_bytes=ALIGN)
+        en_plane = keep.tile([P, N // 4], I32, name="en_plane", align_bytes=ALIGN)
+        v2_planes = [keep.tile([P, J // 4], I32, name="v2_plane%d" % a, align_bytes=ALIGN) for a in range(V2_PASSES)]
+        warm = keep.tile([P, 2], F32, name="warm")
+        nc.gpsimd.memset(warm[:, 0:1], 0.0)
+        nc.scalar.activation(warm[:, 1:2], warm[:, 0:1], ACT.Sigmoid)
+        nc.gpsimd.memset(v_scale_window[:], 0)
+        nc.vector.memset(v2_scale_window[0:V2_ROWS_AT, :], 0)
+        nc.vector.memset(v2_planes[0][:], 0)
         nc.vector.memset(wa_plane_raw[:], 0)
-        load_wb(loads, 0, PACK // 2, PACK)
-        load_wb(loads, 1, 0, PACK)
-        nc.sync.dma_start(wa_words_raw[:], wa_words[0].bitcast(I32))
-        load_plane(wa_plane_raw, wa_scales)
+        nc.gpsimd.memset(v2_planes[1][:], 0)
+        nc.gpsimd.memset(en_plane[:], 0)
+
+        nc.sync.dma_start(v2_scale_window[V2_ROWS_AT:P, :], tab2_scales.rearrange("a q t -> (a q) t").bitcast(I32))
+        nc.sync.dma_start(list2[:], offs2)
+        wb_raw = {0: load_wb(0)}
+        nc.sync.dma_start(list1[:], offs)
+        load_plane(v_scale_window, tab_scales)
+        v2_window = keep.tile([P, T], I32, name="v2_window", align_bytes=ALIGN)
         nc.sync.dma_start(v2_window[:], tab2_words[0].rearrange("p t i -> p (t i)").bitcast(I32))
 
-        v2_plane0 = keep.tile([P, J], U8, name="v2_plane0", align_bytes=64)
+        v2_rows = keep.tile([P, J], U8, name="v2_rows", align_bytes=ALIGN)
+        nc.vector.tensor_copy(v2_rows[:], v2_scale_window[:].bitcast(U8).indirect(list2[:]))
+
+        def move_v2_rows(a):
+            first = V2_ROWS_AT + BLOCKS * a
+            for r in range(QUAD_ROWS):
+                rows = v2_rows[first + r : first + BLOCKS : QUAD_ROWS, :]
+                nc.sync.dma_start(v2_planes[a][r:P:QUAD, :], rows.bitcast(I32))
+
+        v_window = keep.tile([P, T], I32, name="v_window", align_bytes=ALIGN)
+        v_source = tab_words[0].rearrange("p t i -> p (t i)").bitcast(I32)
+        move_v2_rows(0)
+        wb_raw[1] = load_wb(1)
+        wa_words_raw = keep.tile([P, R // 2], I32, name="wa_words_raw", align_bytes=ALIGN)
+        nc.sync.dma_start(wa_words_raw[:], wa_words[0].bitcast(I32))
+        load_plane(wa_plane_raw, wa_scales)
+        nc.sync.dma_start(v_window[:, : T // 2], v_source[:, : T // 2])
+        move_v2_rows(1)
+        sm_slots = keep.tile([P, PACK], F32, name="sm_slots")
+        nc.sync.dma_start(sm_slots[:], sm.rearrange("(p t) -> p t", t=PACK))
+        nc.sync.dma_start(v_window[:, T // 2 :], v_source[:, T // 2 :])
+
+        en_codes = keep.tile([P, N], I32, name="en_codes", align_bytes=ALIGN)
+        nc.sync.dma_start(en_codes[:], en_words[0].rearrange("p n i -> p (n i)").bitcast(I32))
+        load_plane(en_plane, en_scales)
+
         v_plane = {}
         v_words = {}
         v2_words = {}
         v2_parted = {}
 
-        def gather_v_scales(c, count):
+        def gather_v_scales(c, count, planes):
             picked = v_scale_window[:].bitcast(U8).indirect(list1[:, LIST_COLS * c : LIST_COLS * (c + count)])
-            planes = place([P, count * CHUNK], U8, "v_plane", c)
             nc.vector.tensor_copy(planes[:], picked)
             for k in range(count):
                 v_plane[c + k] = planes[:, CHUNK * k : CHUNK * (k + 1)]
 
-        gather_v_scales(0, 2)
-
-        nc.vector.tensor_copy(v2_plane0[:], v2_scale_window[:].bitcast(U8).indirect(list2[:]))
-        for r in range(QUAD_ROWS):
-            nc.sync.dma_start(v2_plane1[r:P:QUAD, :], v2_plane0[PASS1_SHIFT + r : P : QUAD, :].bitcast(I32))
-        v2_planes = (v2_plane0[:], v2_plane1[:].bitcast(U8))
-
-        v_window = place([P, T], I32, "v_window")
-        nc.sync.dma_start(v_window[:], tab_words[0].rearrange("p t i -> p (t i)").bitcast(I32))
-        en_codes = place([P, N], I32, "en_words")
-        nc.sync.dma_start(en_codes[:], en_words[0].rearrange("p n i -> p (n i)").bitcast(I32))
-        sm_slots = place([P, PACK], F32, "sm")
-        nc.sync.dma_start(sm_slots[:], sm.rearrange("(p t) -> p t", t=PACK))
-        en_plane = place([P, N // 4], I32, "en_plane")
-        nc.gpsimd.memset(en_plane[:], 0)
-        load_plane(en_plane, en_scales)
-
-        def gather_v(c):
+        def gather_v(c, words):
             offsets = list1[:, LIST_COLS * c : LIST_COLS * (c + 1)]
-            v_words[c] = place([P, CHUNK], U32, "v_words", c)
-            nc.vector.tensor_copy(v_words[c][:], v_window[:].bitcast(U32).indirect(offsets))
+            v_words[c] = words
+            nc.vector.tensor_copy(words[:], v_window[:].bitcast(U32).indirect(offsets))
 
-        def gather_v2(c):
+        def gather_v2(c, words):
             offsets = list2[:, LIST_COLS * c : LIST_COLS * (c + 1)]
-            v2_words[c] = place([P, CHUNK], U32, "v2_words", c)
-            nc.vector.tensor_copy(v2_words[c][:], v2_window[:].bitcast(U32).indirect(offsets))
+            v2_words[c] = words
+            nc.vector.tensor_copy(words[:], v2_window[:].bitcast(U32).indirect(offsets))
 
         def part_v2(c):
-            v2_parted[c] = place([P, 2 * V2_PASSES * CHUNK], U8, "v2_parted", c)
+            v2_parted[c] = keep.tile([P, 2 * V2_PASSES * CHUNK], U8, name="v2_parted%d" % c, align_bytes=ALIGN)
             nc.vector.tensor_copy(
                 v2_parted[c][:].bitcast(U16).rearrange("p (a j) -> p a j", a=V2_PASSES),
                 v2_words[c][:].bitcast(U16).rearrange("p (j a) -> p a j", a=V2_PASSES),
             )
 
-        wa_codes = place([P, 2 * R], U8, "wa_words")
-        wa_plane = place([P, R], U8, "wa_plane")
+
+        wa_codes = place("wa_codes", [P, 2 * R], U8, "v2_words0")
+        wa_plane = place("wa_plane", [P, R], U8, "v2_words0", 2 * R)
 
         def reorder_wa():
             nc.vector.tensor_copy(
@@ -171,16 +164,15 @@ def tile_list_kg_tanh_sig_kernel(
                 wa_words_raw[:].bitcast(U16).rearrange("p (m t) -> p t m", t=PACK),
             )
 
-        wb_bf = [keep.tile([P, PACK, P, PACK], BF16, name="wb_bf%d" % a, align_bytes=64) for a in range(V2_PASSES)]
-        wb_codes = [keep.tile([P, R], U32, name="wb_codes%d" % a, align_bytes=64) for a in range(V2_PASSES)]
-        wb_plane = [place([P, R], U8, "wb_plane", a) for a in range(V2_PASSES)]
+        wb_bf = [place("wb_bf%d" % a, [P, PACK, P, PACK], BF16, "wb_bf%d" % a) for a in range(V2_PASSES)]
+        wb_codes = [keep.tile([P, R], U32, name="wb_codes%d" % a, align_bytes=ALIGN) for a in range(V2_PASSES)]
+        wb_plane = [keep.tile([P, R], U8, name="wb_plane%d" % a, align_bytes=ALIGN) for a in range(V2_PASSES)]
 
-        def quantize_wb(a, pieces):
-            for i0, i1 in pieces:
-                nc.scalar.copy(
-                    wb_bf[a][:, :, :, i0:i1].rearrange("p t m i -> p m t i"),
-                    wb_raw[a, i0][:].rearrange("p i (m t) -> p m t i", t=PACK),
-                )
+        def quantize_wb(a):
+            nc.scalar.copy(
+                wb_bf[a][:].rearrange("p t m i -> p m i t"),
+                wb_raw[a][:].rearrange("p i (m t) -> p m i t", t=PACK),
+            )
             nc.vector.quantize_mx(
                 out=wb_codes[a][:].bitcast(FP8X4),
                 scales=wb_plane[a][:],
@@ -191,9 +183,9 @@ def tile_list_kg_tanh_sig_kernel(
 
         def open_z(c):
             for t in range(PACK):
-                z[c, t] = psum.tile([P, CHUNK], F32, name="bank")
+                z[c, t] = psum.tile([P, CHUNK], F32, name="bank%d" % (t + PACK * min(c, 1)))
 
-        def add_v2_passes(c, opens):
+        def add_v2_passes(c):
             for t in range(PACK):
                 cols = slice(P * t, P * (t + 1))
                 for a in range(V2_PASSES):
@@ -202,12 +194,12 @@ def tile_list_kg_tanh_sig_kernel(
                         lhsT=wb_codes[a][:, cols].bitcast(FP8X4),
                         lhsT_scale=wb_plane[a][:, cols],
                         rhs=v2_parted[c][:, 2 * CHUNK * a : 2 * CHUNK * (a + 1)].bitcast(FP4X4),
-                        rhs_scale=v2_planes[a][:, CHUNK * c : CHUNK * (c + 1)],
-                        start=(opens and a == 0),
-                        stop=(not opens and a == V2_PASSES - 1),
+                        rhs_scale=v2_planes[a][:].bitcast(U8)[:, CHUNK * c : CHUNK * (c + 1)],
+                        start=(a == 0),
+                        stop=False,
                     )
 
-        def add_v_pass(c, opens):
+        def add_v_pass(c):
             for t in range(PACK):
                 nc.tensor.matmul_mx(
                     out=z[c, t][:],
@@ -215,8 +207,8 @@ def tile_list_kg_tanh_sig_kernel(
                     lhsT_scale=wa_plane[:, P * t : P * (t + 1)],
                     rhs=v_words[c][:].bitcast(FP8X4),
                     rhs_scale=v_plane[c],
-                    start=opens,
-                    stop=not opens,
+                    start=False,
+                    stop=True,
                 )
 
         tanh_z = {}
@@ -230,13 +222,17 @@ def tile_list_kg_tanh_sig_kernel(
                     nc.scalar.activation(tanh_z[c][:, t, j0 : j0 + width], z[c, t][:, j0 : j0 + width], ACT.Tanh)
 
         def make_h(c):
-            h_codes[c] = ring.tile([P, CHUNK], U32, name="h_codes", align_bytes=64)
-            h_plane[c] = ring.tile([P, CHUNK], U8, name="h_plane", align_bytes=64)
+            h_codes[c] = ring.tile([P, CHUNK], U32, name="h_codes", align_bytes=ALIGN)
+            h_plane[c] = ring.tile([P, CHUNK], U8, name="h_plane", align_bytes=ALIGN)
             halves = [slice(HALF_CHUNK * s, HALF_CHUNK * (s + 1)) for s in range(2)]
             factor = sm_slots[:].rearrange("p (g t e) -> p g t e", g=1, e=1)
             h_bf = []
             for s, cols in enumerate(halves):
-                h_bf.append(place([P, HALF_CHUNK * PACK], BF16, "h_bf", 2 * c + s))
+                name = "h_bf%d" % (2 * c + s)
+                if name in cells:
+                    h_bf.append(place(name, [P, HALF_CHUNK * PACK], BF16, name))
+                else:
+                    h_bf.append(keep.tile([P, HALF_CHUNK * PACK], BF16, name=name, align_bytes=ALIGN))
                 nc.vector.tensor_tensor(
                     h_bf[s][:].rearrange("p (g e t) -> p g t e", e=RUN, t=PACK),
                     tanh_z[c][:, :, cols].rearrange("p t (g e) -> p g t e", e=RUN),
@@ -249,9 +245,9 @@ def tile_list_kg_tanh_sig_kernel(
                 )
 
         def score_chunk(c):
-            for n0 in range(0, N, P):
-                cols = slice(n0, n0 + P)
-                y = psum.tile([P, CHUNK], F32, name="bank")
+            for b in range(N // P):
+                cols = slice(P * b, P * (b + 1))
+                y = psum.tile([P, CHUNK], F32, name="bank%d" % (b % PACK))
                 nc.tensor.matmul_mx(
                     out=y[:],
                     lhsT=en_codes[:, cols].bitcast(FP8X4),
@@ -265,38 +261,38 @@ def tile_list_kg_tanh_sig_kernel(
                 nc.scalar.activation(prob[:], y[:], ACT.Sigmoid)
                 nc.sync.dma_start(out[cols, CHUNK * c : CHUNK * (c + 1)], prob[:])
 
-        quantize_wb(0, ((0, PACK // 2), (PACK // 2, PACK)))
+        gather_v_scales(0, 1, keep.tile([P, CHUNK], U8, name="v_plane0", align_bytes=ALIGN))
+        quantize_wb(0)
+        for c in range(2):
+            gather_v2(c, place("v2_words%d" % c, [P, CHUNK], U32, "v2_words%d" % c))
+            part_v2(c)
         reorder_wa()
-        quantize_wb(1, ((0, PACK),))
-        gather_v_scales(2, 1)
-        gather_v2(0)
-        part_v2(0)
-        open_z(0)
-        add_v2_passes(0, True)
-        gather_v2(1)
-        gather_v_scales(3, 1)
-
-        gather_v(0)
-        add_v_pass(0, False)
-        gather_v(1)
-        part_v2(1)
-        open_z(1)
-        add_v_pass(1, True)
-        add_v2_passes(1, False)
+        gather_v_scales(1, 1, place("v_plane1", [P, CHUNK], U8, "v2_words1"))
+        quantize_wb(1)
+        for c in range(2):
+            open_z(c)
+            add_v2_passes(c)
+        gather_v_scales(2, 1, place("v_plane2", [P, CHUNK], U8, "wb_bf1"))
+        for c in range(2):
+            gather_v(c, keep.tile([P, CHUNK], U32, name="v_words%d" % c, align_bytes=ALIGN))
+            add_v_pass(c)
         tanh_chunk(0, HALF_CHUNK)
         make_h(0)
         tanh_chunk(1, CHUNK)
 
         for c in range(CHUNKS):
-            if c + 2 < CHUNKS:
-                gather_v2(c + 2)
-                part_v2(c + 2)
-                gather_v(c + 2)
+            ahead = c + 2
+            if ahead < CHUNKS:
+                if ahead not in v_plane:
+                    gather_v_scales(ahead, 1, place("v_plane3", [P, CHUNK], U8, "h_bf2"))
+                gather_v2(ahead, place("v2_words%d" % ahead, [P, CHUNK], U32, "h_bf%d" % (2 * c), CHUNK * c))
+                part_v2(ahead)
+                gather_v(ahead, place("v_words%d" % ahead, [P, CHUNK], U32, "h_bf%d" % (2 * c + 1)))
             score_chunk(c)
             if c + 1 < CHUNKS:
                 make_h(c + 1)
-            if c + 2 < CHUNKS:
-                open_z(c + 2)
-                add_v2_passes(c + 2, True)
-                add_v_pass(c + 2, False)
-                tanh_chunk(c + 2, CHUNK)
+            if ahead < CHUNKS:
+                open_z(ahead)
+                add_v2_passes(ahead)
+                add_v_pass(ahead)
+                tanh_chunk(ahead, CHUNK)

@@ -28,8 +28,12 @@ BLOCKS = 16
 QUAD = 32
 QUAD_ROWS = 4
 V2_ROWS_AT = P - V2_PASSES * BLOCKS
-RUN = 4
+GROUP = CHUNK // PACK
+GROUPS = CHUNK // GROUP
 ALIGN = 64
+H_BYTES = 2 * PACK * CHUNK
+WORD_BYTES = 4 * CHUNK
+LAST_PIECE = H_BYTES - 2 * PACK * GROUP
 
 
 def tile_list_kg_tanh_sig_kernel(
@@ -57,10 +61,8 @@ def tile_list_kg_tanh_sig_kernel(
         cell("v2_words1", 4 * CHUNK)
         cell("wb_bf0", 8 * R)
         cell("wb_bf1", 8 * R)
-        cell("h_bf0", 4 * CHUNK)
-        cell("h_bf1", 4 * CHUNK)
-        cell("h_bf2", 5 * CHUNK)
-        cell("h_bf3", 4 * CHUNK)
+        for c in range(CHUNKS):
+            cell("h_bf%d" % c, H_BYTES + WORD_BYTES)
 
         def load_plane(plane, scales):
             for r in range(QUAD_ROWS):
@@ -182,67 +184,82 @@ def tile_list_kg_tanh_sig_kernel(
         z = {}
 
         def open_z(c):
-            for t in range(PACK):
-                z[c, t] = psum.tile([P, CHUNK], F32, name="bank%d" % (t + PACK * min(c, 1)))
+            for b in range(GROUPS):
+                z[c, b] = psum.tile([P, PACK, GROUP], F32, name="bank%d" % (b + GROUPS * min(c, 1)))
 
-        def add_v2_passes(c):
-            for t in range(PACK):
-                cols = slice(P * t, P * (t + 1))
+        def v2_pass(c, a, b, t, start, stop):
+            cols = slice(P * t, P * (t + 1))
+            j0 = CHUNK * a + GROUP * b
+            nc.tensor.matmul_mx(
+                out=z[c, b][:, t, :],
+                lhsT=wb_codes[a][:, cols].bitcast(FP8X4),
+                lhsT_scale=wb_plane[a][:, cols],
+                rhs=v2_parted[c][:, 2 * j0 : 2 * (j0 + GROUP)].bitcast(FP4X4),
+                rhs_scale=v2_planes[a][:].bitcast(U8)[:, CHUNK * c + GROUP * b : CHUNK * c + GROUP * (b + 1)],
+                start=start,
+                stop=stop,
+            )
+
+        def v_pass(c, b, t, start, stop):
+            cols = slice(GROUP * b, GROUP * (b + 1))
+            nc.tensor.matmul_mx(
+                out=z[c, b][:, t, :],
+                lhsT=wa_codes[:, 2 * P * t : 2 * P * (t + 1)].bitcast(FP4X4),
+                lhsT_scale=wa_plane[:, P * t : P * (t + 1)],
+                rhs=v_words[c][:, cols].bitcast(FP8X4),
+                rhs_scale=v_plane[c][:, cols],
+                start=start,
+                stop=stop,
+            )
+
+        def add_v2_passes(c, opens):
+            for b in range(GROUPS):
                 for a in range(V2_PASSES):
-                    nc.tensor.matmul_mx(
-                        out=z[c, t][:],
-                        lhsT=wb_codes[a][:, cols].bitcast(FP8X4),
-                        lhsT_scale=wb_plane[a][:, cols],
-                        rhs=v2_parted[c][:, 2 * CHUNK * a : 2 * CHUNK * (a + 1)].bitcast(FP4X4),
-                        rhs_scale=v2_planes[a][:].bitcast(U8)[:, CHUNK * c : CHUNK * (c + 1)],
-                        start=(a == 0),
-                        stop=False,
-                    )
+                    for t in range(PACK):
+                        first = a == 0 and t == 0
+                        last = a == V2_PASSES - 1 and t == PACK - 1
+                        v2_pass(c, a, b, t, opens and first, last and not opens)
 
-        def add_v_pass(c):
-            for t in range(PACK):
-                nc.tensor.matmul_mx(
-                    out=z[c, t][:],
-                    lhsT=wa_codes[:, 2 * P * t : 2 * P * (t + 1)].bitcast(FP4X4),
-                    lhsT_scale=wa_plane[:, P * t : P * (t + 1)],
-                    rhs=v_words[c][:].bitcast(FP8X4),
-                    rhs_scale=v_plane[c],
-                    start=False,
-                    stop=True,
-                )
+        def add_v_pass(c, opens):
+            for b in range(GROUPS):
+                for t in range(PACK):
+                    v_pass(c, b, t, opens and t == 0, t == PACK - 1 and not opens)
 
         tanh_z = {}
         h_codes = {}
         h_plane = {}
 
-        def tanh_chunk(c, width):
-            tanh_z[c] = ring.tile([P, PACK, CHUNK], F32, name="tanh_z")
-            for j0 in range(0, CHUNK, width):
-                for t in range(PACK):
-                    nc.scalar.activation(tanh_z[c][:, t, j0 : j0 + width], z[c, t][:, j0 : j0 + width], ACT.Tanh)
+        def tanh_chunk(c):
+            tanh_z[c] = ring.tile([P, CHUNK, PACK], F32, name="tanh_z")
+            for b in range(GROUPS):
+                nc.scalar.activation(
+                    tanh_z[c][:, GROUP * b : GROUP * (b + 1), :], z[c, b][:].rearrange("p t j -> p j t"), ACT.Tanh
+                )
 
-        def make_h(c):
+        def make_h(c, width):
             h_codes[c] = ring.tile([P, CHUNK], U32, name="h_codes", align_bytes=ALIGN)
             h_plane[c] = ring.tile([P, CHUNK], U8, name="h_plane", align_bytes=ALIGN)
-            halves = [slice(HALF_CHUNK * s, HALF_CHUNK * (s + 1)) for s in range(2)]
-            factor = sm_slots[:].rearrange("p (g t e) -> p g t e", g=1, e=1)
-            h_bf = []
-            for s, cols in enumerate(halves):
-                name = "h_bf%d" % (2 * c + s)
-                if name in cells:
-                    h_bf.append(place(name, [P, HALF_CHUNK * PACK], BF16, name))
-                else:
-                    h_bf.append(keep.tile([P, HALF_CHUNK * PACK], BF16, name=name, align_bytes=ALIGN))
-                nc.vector.tensor_tensor(
-                    h_bf[s][:].rearrange("p (g e t) -> p g t e", e=RUN, t=PACK),
-                    tanh_z[c][:, :, cols].rearrange("p t (g e) -> p g t e", e=RUN),
-                    factor.to_broadcast([P, HALF_CHUNK // RUN, PACK, RUN]),
-                    MULT,
-                )
-            for s, cols in enumerate(halves):
+            factor = sm_slots[:].rearrange("p (j t) -> p j t", j=1).to_broadcast([P, width, PACK])
+            h_bf = {}
+
+            def scale(j0):
+                name = "h_bf%d_%d" % (c, j0)
+                where = "h_bf%d" % (c - 1 if c > 0 and j0 == 0 else c)
+                h_bf[j0] = place(name, [P, width, PACK], BF16, where, 2 * PACK * j0)
+                nc.vector.tensor_tensor(h_bf[j0][:], tanh_z[c][:, j0 : j0 + width, :], factor, MULT)
+
+            def quantize(j0):
                 nc.vector.quantize_mx(
-                    out=h_codes[c][:, cols].bitcast(FP8X4), scales=h_plane[c][:, cols], in_=h_bf[s][:]
+                    out=h_codes[c][:, j0 : j0 + width].bitcast(FP8X4),
+                    scales=h_plane[c][:, j0 : j0 + width],
+                    in_=h_bf[j0][:].rearrange("p j t -> p (j t)"),
                 )
+
+            scale(0)
+            for j0 in range(width, CHUNK, width):
+                scale(j0)
+                quantize(j0 - width)
+            quantize(CHUNK - width)
 
         def score_chunk(c):
             for b in range(N // P):
@@ -271,28 +288,28 @@ def tile_list_kg_tanh_sig_kernel(
         quantize_wb(1)
         for c in range(2):
             open_z(c)
-            add_v2_passes(c)
+            add_v2_passes(c, True)
         gather_v_scales(2, 1, place("v_plane2", [P, CHUNK], U8, "wb_bf1"))
         for c in range(2):
             gather_v(c, keep.tile([P, CHUNK], U32, name="v_words%d" % c, align_bytes=ALIGN))
-            add_v_pass(c)
-        tanh_chunk(0, HALF_CHUNK)
-        make_h(0)
-        tanh_chunk(1, CHUNK)
+            add_v_pass(c, False)
+        tanh_chunk(0)
+        make_h(0, GROUP)
+        tanh_chunk(1)
 
         for c in range(CHUNKS):
             ahead = c + 2
             if ahead < CHUNKS:
                 if ahead not in v_plane:
-                    gather_v_scales(ahead, 1, place("v_plane3", [P, CHUNK], U8, "h_bf2"))
-                gather_v2(ahead, place("v2_words%d" % ahead, [P, CHUNK], U32, "h_bf%d" % (2 * c), CHUNK * c))
+                    gather_v_scales(ahead, 1, place("v_plane3", [P, CHUNK], U8, "h_bf1", LAST_PIECE + ALIGN))
+                gather_v(ahead, place("v_words%d" % ahead, [P, CHUNK], U32, "h_bf%d" % c, H_BYTES - ALIGN))
+                gather_v2(ahead, place("v2_words%d" % ahead, [P, CHUNK], U32, "h_bf%d" % c, LAST_PIECE + ALIGN - WORD_BYTES))
                 part_v2(ahead)
-                gather_v(ahead, place("v_words%d" % ahead, [P, CHUNK], U32, "h_bf%d" % (2 * c + 1)))
             score_chunk(c)
             if c + 1 < CHUNKS:
-                make_h(c + 1)
+                make_h(c + 1, HALF_CHUNK)
             if ahead < CHUNKS:
                 open_z(ahead)
-                add_v2_passes(ahead)
-                add_v_pass(ahead)
-                tanh_chunk(ahead, CHUNK)
+                add_v_pass(ahead, True)
+                add_v2_passes(ahead, False)
+                tanh_chunk(ahead)

@@ -31,6 +31,10 @@ V2_ROWS_AT = P - V2_PASSES * BLOCKS
 GROUP = CHUNK // PACK
 GROUPS = CHUNK // GROUP
 ALIGN = 64
+SPANS = (slice(0, J - CHUNK), slice(J - CHUNK, J))
+V_ROWS_AT = 4
+V_ROW_STEP = P // BLOCKS
+V_SPLIT = 5 * T // 8
 H_BYTES = 2 * PACK * CHUNK
 WORD_BYTES = 4 * CHUNK
 LAST_PIECE = H_BYTES - 2 * PACK * GROUP
@@ -44,7 +48,7 @@ def tile_list_kg_tanh_sig_kernel(
         keep = ctx.enter_context(tc.tile_pool(name="keep", bufs=1))
         ring = ctx.enter_context(tc.tile_pool(name="ring", bufs=2))
         arena = ctx.enter_context(tc.tile_pool(name="arena", bufs=1))
-        stage = ctx.enter_context(tc.tile_pool(name="stage", bufs=N // P))
+        stage = ctx.enter_context(tc.tile_pool(name="stage", bufs=2 * N // P))
         psum = ctx.enter_context(tc.psum_pool(name="psum", bufs=1))
 
         cells = {}
@@ -64,10 +68,6 @@ def tile_list_kg_tanh_sig_kernel(
         for c in range(CHUNKS):
             cell("h_bf%d" % c, H_BYTES + WORD_BYTES)
 
-        def load_plane(plane, scales):
-            for r in range(QUAD_ROWS):
-                nc.sync.dma_start(plane[r:P:QUAD, :], scales[0, r:BLOCKS:QUAD_ROWS, :].bitcast(I32))
-
         def load_wb(a):
             raw = keep.tile([P, PACK, R], F32, name="wb_raw%d" % a)
             nc.sync.dma_start(raw[:], wb[K_PASS * a : K_PASS * (a + 1), :].rearrange("(p i) r -> p i r", i=PACK))
@@ -80,60 +80,80 @@ def tile_list_kg_tanh_sig_kernel(
         wa_plane_raw = keep.tile([P, R // 4], I32, name="wa_plane_raw", align_bytes=ALIGN)
         en_plane = keep.tile([P, N // 4], I32, name="en_plane", align_bytes=ALIGN)
         v2_planes = [keep.tile([P, J // 4], I32, name="v2_plane%d" % a, align_bytes=ALIGN) for a in range(V2_PASSES)]
+        v_plane = keep.tile([P, J // 4], I32, name="v_plane", align_bytes=ALIGN)
         warm = keep.tile([P, 2], F32, name="warm")
         nc.gpsimd.memset(warm[:, 0:1], 0.0)
         nc.scalar.activation(warm[:, 1:2], warm[:, 0:1], ACT.Sigmoid)
         nc.gpsimd.memset(v_scale_window[:], 0)
-        nc.vector.memset(v2_scale_window[0:V2_ROWS_AT, :], 0)
-        nc.vector.memset(v2_planes[0][:], 0)
         nc.vector.memset(wa_plane_raw[:], 0)
-        nc.gpsimd.memset(v2_planes[1][:], 0)
+        nc.vector.memset(v2_scale_window[0:V2_ROWS_AT, :], 0)
+        for plane in v2_planes + [v_plane]:
+            nc.vector.memset(plane[:], 0)
         nc.gpsimd.memset(en_plane[:], 0)
+
+        def load_plane_rows(plane, scales, r):
+            nc.sync.dma_start(plane[r:P:QUAD, :], scales[0, r:BLOCKS:QUAD_ROWS, :].bitcast(I32))
 
         nc.sync.dma_start(v2_scale_window[V2_ROWS_AT:P, :], tab2_scales.rearrange("a q t -> (a q) t").bitcast(I32))
         nc.sync.dma_start(list2[:], offs2)
         wb_raw = {0: load_wb(0)}
         nc.sync.dma_start(list1[:], offs)
-        load_plane(v_scale_window, tab_scales)
+        nc.sync.dma_start(v_scale_window[V_ROWS_AT:P:V_ROW_STEP, :], tab_scales[0].bitcast(I32))
+        wa_words_raw = keep.tile([P, R // 2], I32, name="wa_words_raw", align_bytes=ALIGN)
+        nc.sync.dma_start(wa_words_raw[:], wa_words[0].bitcast(I32))
+        for r in range(QUAD_ROWS // 2):
+            load_plane_rows(wa_plane_raw, wa_scales, r)
         v2_window = keep.tile([P, T], I32, name="v2_window", align_bytes=ALIGN)
         nc.sync.dma_start(v2_window[:], tab2_words[0].rearrange("p t i -> p (t i)").bitcast(I32))
+        for r in range(QUAD_ROWS // 2, QUAD_ROWS):
+            load_plane_rows(wa_plane_raw, wa_scales, r)
 
-        v2_rows = keep.tile([P, J], U8, name="v2_rows", align_bytes=ALIGN)
-        nc.vector.tensor_copy(v2_rows[:], v2_scale_window[:].bitcast(U8).indirect(list2[:]))
+        v2_rows = {}
+        v_rows = {}
 
-        def move_v2_rows(a):
-            first = V2_ROWS_AT + BLOCKS * a
+        def gather_v2_scales(s, rows):
+            v2_rows[s] = rows
+            offsets = list2[:, SPANS[s].start // 16 : SPANS[s].stop // 16]
+            nc.vector.tensor_copy(rows[:], v2_scale_window[:].bitcast(U8).indirect(offsets))
+
+        def gather_v_scales(s, rows):
+            v_rows[s] = rows
+            offsets = list1[:, SPANS[s].start // 16 : SPANS[s].stop // 16]
+            nc.vector.tensor_copy(rows[:], v_scale_window[:].bitcast(U8).indirect(offsets))
+
+        def move_rows(plane, rows, s, first, step):
+            cols = slice(SPANS[s].start // 4, SPANS[s].stop // 4)
             for r in range(QUAD_ROWS):
-                rows = v2_rows[first + r : first + BLOCKS : QUAD_ROWS, :]
-                nc.sync.dma_start(v2_planes[a][r:P:QUAD, :], rows.bitcast(I32))
+                source = rows[first + step * r : first + step * (BLOCKS - 1) + 1 : step * QUAD_ROWS, :]
+                nc.sync.dma_start(plane[r:P:QUAD, cols], source.bitcast(I32))
+
+        def move_v2_rows(s, a):
+            move_rows(v2_planes[a], v2_rows[s], s, V2_ROWS_AT + BLOCKS * a, 1)
+
+        def move_v_rows(s):
+            move_rows(v_plane, v_rows[s], s, V_ROWS_AT, V_ROW_STEP)
+
+        gather_v2_scales(0, keep.tile([P, J - CHUNK], U8, name="v2_rows0", align_bytes=ALIGN))
+        gather_v_scales(0, keep.tile([P, J - CHUNK], U8, name="v_rows0", align_bytes=ALIGN))
 
         v_window = keep.tile([P, T], I32, name="v_window", align_bytes=ALIGN)
         v_source = tab_words[0].rearrange("p t i -> p (t i)").bitcast(I32)
-        move_v2_rows(0)
+        move_v2_rows(0, 0)
         wb_raw[1] = load_wb(1)
-        wa_words_raw = keep.tile([P, R // 2], I32, name="wa_words_raw", align_bytes=ALIGN)
-        nc.sync.dma_start(wa_words_raw[:], wa_words[0].bitcast(I32))
-        load_plane(wa_plane_raw, wa_scales)
-        nc.sync.dma_start(v_window[:, : T // 2], v_source[:, : T // 2])
-        move_v2_rows(1)
+        move_v2_rows(0, 1)
+        nc.sync.dma_start(v_window[:, :V_SPLIT], v_source[:, :V_SPLIT])
+        move_v_rows(0)
+        nc.sync.dma_start(v_window[:, V_SPLIT:], v_source[:, V_SPLIT:])
         sm_slots = keep.tile([P, PACK], F32, name="sm_slots")
         nc.sync.dma_start(sm_slots[:], sm.rearrange("(p t) -> p t", t=PACK))
-        nc.sync.dma_start(v_window[:, T // 2 :], v_source[:, T // 2 :])
-
         en_codes = keep.tile([P, N], I32, name="en_codes", align_bytes=ALIGN)
         nc.sync.dma_start(en_codes[:], en_words[0].rearrange("p n i -> p (n i)").bitcast(I32))
-        load_plane(en_plane, en_scales)
+        for r in range(QUAD_ROWS):
+            load_plane_rows(en_plane, en_scales, r)
 
-        v_plane = {}
         v_words = {}
         v2_words = {}
         v2_parted = {}
-
-        def gather_v_scales(c, count, planes):
-            picked = v_scale_window[:].bitcast(U8).indirect(list1[:, LIST_COLS * c : LIST_COLS * (c + count)])
-            nc.vector.tensor_copy(planes[:], picked)
-            for k in range(count):
-                v_plane[c + k] = planes[:, CHUNK * k : CHUNK * (k + 1)]
 
         def gather_v(c, words):
             offsets = list1[:, LIST_COLS * c : LIST_COLS * (c + 1)]
@@ -207,7 +227,7 @@ def tile_list_kg_tanh_sig_kernel(
                 lhsT=wa_codes[:, 2 * P * t : 2 * P * (t + 1)].bitcast(FP4X4),
                 lhsT_scale=wa_plane[:, P * t : P * (t + 1)],
                 rhs=v_words[c][:, cols].bitcast(FP8X4),
-                rhs_scale=v_plane[c][:, cols],
+                rhs_scale=v_plane[:].bitcast(U8)[:, CHUNK * c + GROUP * b : CHUNK * c + GROUP * (b + 1)],
                 start=start,
                 stop=stop,
             )
@@ -264,7 +284,7 @@ def tile_list_kg_tanh_sig_kernel(
         def score_chunk(c):
             for b in range(N // P):
                 cols = slice(P * b, P * (b + 1))
-                y = psum.tile([P, CHUNK], F32, name="bank%d" % (b % PACK))
+                y = psum.tile([P, CHUNK], F32, name="bank%d" % (b % GROUPS))
                 nc.tensor.matmul_mx(
                     out=y[:],
                     lhsT=en_codes[:, cols].bitcast(FP8X4),
@@ -278,18 +298,20 @@ def tile_list_kg_tanh_sig_kernel(
                 nc.scalar.activation(prob[:], y[:], ACT.Sigmoid)
                 nc.sync.dma_start(out[cols, CHUNK * c : CHUNK * (c + 1)], prob[:])
 
-        gather_v_scales(0, 1, keep.tile([P, CHUNK], U8, name="v_plane0", align_bytes=ALIGN))
         quantize_wb(0)
         for c in range(2):
             gather_v2(c, place("v2_words%d" % c, [P, CHUNK], U32, "v2_words%d" % c))
             part_v2(c)
         reorder_wa()
-        gather_v_scales(1, 1, place("v_plane1", [P, CHUNK], U8, "v2_words1"))
         quantize_wb(1)
         for c in range(2):
             open_z(c)
             add_v2_passes(c, True)
-        gather_v_scales(2, 1, place("v_plane2", [P, CHUNK], U8, "wb_bf1"))
+        gather_v_scales(1, place("v_rows1", [P, CHUNK], U8, "wb_bf1"))
+        move_v_rows(1)
+        gather_v2_scales(1, place("v2_rows1", [P, CHUNK], U8, "wb_bf1", CHUNK))
+        for a in range(V2_PASSES):
+            move_v2_rows(1, a)
         for c in range(2):
             gather_v(c, keep.tile([P, CHUNK], U32, name="v_words%d" % c, align_bytes=ALIGN))
             add_v_pass(c, False)
@@ -300,8 +322,6 @@ def tile_list_kg_tanh_sig_kernel(
         for c in range(CHUNKS):
             ahead = c + 2
             if ahead < CHUNKS:
-                if ahead not in v_plane:
-                    gather_v_scales(ahead, 1, place("v_plane3", [P, CHUNK], U8, "h_bf1", LAST_PIECE + ALIGN))
                 gather_v(ahead, place("v_words%d" % ahead, [P, CHUNK], U32, "h_bf%d" % c, H_BYTES - ALIGN))
                 gather_v2(ahead, place("v2_words%d" % ahead, [P, CHUNK], U32, "h_bf%d" % c, LAST_PIECE + ALIGN - WORD_BYTES))
                 part_v2(ahead)

@@ -22,22 +22,17 @@ K_PASS = P * PACK
 V2_PASSES = L // K_PASS
 CHUNK = 512
 CHUNKS = J // CHUNK
-HALF_CHUNK = CHUNK // 2
-LIST_COLS = CHUNK // 16
+HALF = CHUNK // 2
 BLOCKS = 16
 QUAD = 32
 QUAD_ROWS = 4
 V2_ROWS_AT = P - V2_PASSES * BLOCKS
-GROUP = CHUNK // PACK
-GROUPS = CHUNK // GROUP
-ALIGN = 64
-SPANS = (slice(0, J - CHUNK), slice(J - CHUNK, J))
 V_ROWS_AT = 4
 V_ROW_STEP = P // BLOCKS
-V_SPLIT = 5 * T // 8
-H_BYTES = 2 * PACK * CHUNK
-WORD_BYTES = 4 * CHUNK
-LAST_PIECE = H_BYTES - 2 * PACK * GROUP
+GROUP = CHUNK // PACK
+RUN = 4
+ALIGN = 64
+WORDS = 4 * CHUNK
 
 
 def tile_list_kg_tanh_sig_kernel(
@@ -46,9 +41,8 @@ def tile_list_kg_tanh_sig_kernel(
     nc = tc.nc
     with ExitStack() as ctx:
         keep = ctx.enter_context(tc.tile_pool(name="keep", bufs=1))
-        ring = ctx.enter_context(tc.tile_pool(name="ring", bufs=2))
         arena = ctx.enter_context(tc.tile_pool(name="arena", bufs=1))
-        stage = ctx.enter_context(tc.tile_pool(name="stage", bufs=2 * N // P))
+        stage = ctx.enter_context(tc.tile_pool(name="stage", bufs=CHUNKS * N // P))
         psum = ctx.enter_context(tc.psum_pool(name="psum", bufs=1))
 
         cells = {}
@@ -61,12 +55,19 @@ def tile_list_kg_tanh_sig_kernel(
         def place(name, shape, dtype, where, skip=0):
             return arena.tile(shape, dtype, name=name, align_bytes=ALIGN, offset=cells[where] + skip)
 
-        cell("v2_words0", 4 * CHUNK)
-        cell("v2_words1", 4 * CHUNK)
-        cell("wb_bf0", 8 * R)
+        cell("v_scale_window", T)
+        cell("v2_words0", WORDS)
+        cell("v2_words1", WORDS)
         cell("wb_bf1", 8 * R)
-        for c in range(CHUNKS):
-            cell("h_bf%d" % c, H_BYTES + WORD_BYTES)
+        cell("tanh0", 4 * PACK * CHUNK + WORDS // 2)
+        cell("tanh1", 4 * PACK * CHUNK)
+        cell("v2_parted3", WORDS)
+
+        def bank(b, shape):
+            return psum.tile(shape, F32, name="bank%d" % b)
+
+        def offsets(lst, j0, j1):
+            return lst[:, j0 // 16 : j1 // 16]
 
         def load_wb(a):
             raw = keep.tile([P, PACK, R], F32, name="wb_raw%d" % a)
@@ -76,119 +77,96 @@ def tile_list_kg_tanh_sig_kernel(
         list1 = keep.tile([P, J // 16], U16, name="list1")
         list2 = keep.tile([P, J // 16], U16, name="list2")
         v2_scale_window = keep.tile([P, T // 4], I32, name="v2_scale_window", align_bytes=ALIGN)
-        v_scale_window = keep.tile([P, T // 4], I32, name="v_scale_window", align_bytes=ALIGN)
+        v_scale_window = place("v_scale_window", [P, T // 4], I32, "v_scale_window")
         wa_plane_raw = keep.tile([P, R // 4], I32, name="wa_plane_raw", align_bytes=ALIGN)
         en_plane = keep.tile([P, N // 4], I32, name="en_plane", align_bytes=ALIGN)
-        v2_planes = [keep.tile([P, J // 4], I32, name="v2_plane%d" % a, align_bytes=ALIGN) for a in range(V2_PASSES)]
-        v_plane = keep.tile([P, J // 4], I32, name="v_plane", align_bytes=ALIGN)
+        v2_planes_early = [
+            keep.tile([P, (J - CHUNK) // 4], I32, name="v2_plane_early%d" % a, align_bytes=ALIGN) for a in range(V2_PASSES)
+        ]
+        v2_planes_late = [
+            keep.tile([P, CHUNK // 4], I32, name="v2_plane_late%d" % a, align_bytes=ALIGN) for a in range(V2_PASSES)
+        ]
+        v_plane_early = keep.tile([P, 2 * CHUNK // 4], I32, name="v_plane_early", align_bytes=ALIGN)
         warm = keep.tile([P, 2], F32, name="warm")
         nc.gpsimd.memset(warm[:, 0:1], 0.0)
         nc.scalar.activation(warm[:, 1:2], warm[:, 0:1], ACT.Sigmoid)
         nc.gpsimd.memset(v_scale_window[:], 0)
         nc.vector.memset(wa_plane_raw[:], 0)
         nc.vector.memset(v2_scale_window[0:V2_ROWS_AT, :], 0)
-        for plane in v2_planes + [v_plane]:
+        for plane in v2_planes_early + v2_planes_late + [v_plane_early]:
             nc.vector.memset(plane[:], 0)
         nc.gpsimd.memset(en_plane[:], 0)
 
-        def load_plane_rows(plane, scales, r):
-            nc.sync.dma_start(plane[r:P:QUAD, :], scales[0, r:BLOCKS:QUAD_ROWS, :].bitcast(I32))
+        def load_plane(plane, scales):
+            for r in range(QUAD_ROWS):
+                nc.sync.dma_start(plane[r:P:QUAD, :], scales[0, r:BLOCKS:QUAD_ROWS, :].bitcast(I32))
 
         nc.sync.dma_start(v2_scale_window[V2_ROWS_AT:P, :], tab2_scales.rearrange("a q t -> (a q) t").bitcast(I32))
         nc.sync.dma_start(list2[:], offs2)
         wb_raw = {0: load_wb(0)}
         nc.sync.dma_start(list1[:], offs)
         nc.sync.dma_start(v_scale_window[V_ROWS_AT:P:V_ROW_STEP, :], tab_scales[0].bitcast(I32))
-        wa_words_raw = keep.tile([P, R // 2], I32, name="wa_words_raw", align_bytes=ALIGN)
-        nc.sync.dma_start(wa_words_raw[:], wa_words[0].bitcast(I32))
-        for r in range(QUAD_ROWS // 2):
-            load_plane_rows(wa_plane_raw, wa_scales, r)
+        load_plane(wa_plane_raw, wa_scales)
         v2_window = keep.tile([P, T], I32, name="v2_window", align_bytes=ALIGN)
         nc.sync.dma_start(v2_window[:], tab2_words[0].rearrange("p t i -> p (t i)").bitcast(I32))
-        for r in range(QUAD_ROWS // 2, QUAD_ROWS):
-            load_plane_rows(wa_plane_raw, wa_scales, r)
+        wa_words_raw = keep.tile([P, R // 2], I32, name="wa_words_raw", align_bytes=ALIGN)
+        nc.sync.dma_start(wa_words_raw[:], wa_words[0].bitcast(I32))
 
-        v2_rows = {}
-        v_rows = {}
+        def gather_bytes(rows, window, lst, j0, j1):
+            nc.vector.tensor_copy(rows[:], window[:].bitcast(U8).indirect(offsets(lst, j0, j1)))
 
-        def gather_v2_scales(s, rows):
-            v2_rows[s] = rows
-            offsets = list2[:, SPANS[s].start // 16 : SPANS[s].stop // 16]
-            nc.vector.tensor_copy(rows[:], v2_scale_window[:].bitcast(U8).indirect(offsets))
-
-        def gather_v_scales(s, rows):
-            v_rows[s] = rows
-            offsets = list1[:, SPANS[s].start // 16 : SPANS[s].stop // 16]
-            nc.vector.tensor_copy(rows[:], v_scale_window[:].bitcast(U8).indirect(offsets))
-
-        def move_rows(plane, rows, s, first, step):
-            cols = slice(SPANS[s].start // 4, SPANS[s].stop // 4)
+        def move_rows(plane, rows, first, step):
             for r in range(QUAD_ROWS):
                 source = rows[first + step * r : first + step * (BLOCKS - 1) + 1 : step * QUAD_ROWS, :]
-                nc.sync.dma_start(plane[r:P:QUAD, cols], source.bitcast(I32))
+                nc.sync.dma_start(plane[r:P:QUAD, :], source.bitcast(I32))
 
-        def move_v2_rows(s, a):
-            move_rows(v2_planes[a], v2_rows[s], s, V2_ROWS_AT + BLOCKS * a, 1)
-
-        def move_v_rows(s):
-            move_rows(v_plane, v_rows[s], s, V_ROWS_AT, V_ROW_STEP)
-
-        gather_v2_scales(0, keep.tile([P, J - CHUNK], U8, name="v2_rows0", align_bytes=ALIGN))
-        gather_v_scales(0, keep.tile([P, J - CHUNK], U8, name="v_rows0", align_bytes=ALIGN))
+        v2_rows_early = keep.tile([P, J - CHUNK], U8, name="v2_rows_early", align_bytes=ALIGN)
+        gather_bytes(v2_rows_early, v2_scale_window, list2, 0, J - CHUNK)
+        v_rows_early = keep.tile([P, 2 * CHUNK], U8, name="v_rows_early", align_bytes=ALIGN)
+        gather_bytes(v_rows_early, v_scale_window, list1, 0, 2 * CHUNK)
 
         v_window = keep.tile([P, T], I32, name="v_window", align_bytes=ALIGN)
-        v_source = tab_words[0].rearrange("p t i -> p (t i)").bitcast(I32)
-        move_v2_rows(0, 0)
+        move_rows(v2_planes_early[0], v2_rows_early, V2_ROWS_AT, 1)
         wb_raw[1] = load_wb(1)
-        move_v2_rows(0, 1)
-        nc.sync.dma_start(v_window[:, :V_SPLIT], v_source[:, :V_SPLIT])
-        move_v_rows(0)
-        nc.sync.dma_start(v_window[:, V_SPLIT:], v_source[:, V_SPLIT:])
+        move_rows(v2_planes_early[1], v2_rows_early, V2_ROWS_AT + BLOCKS, 1)
+        nc.sync.dma_start(v_window[:], tab_words[0].rearrange("p t i -> p (t i)").bitcast(I32))
+        move_rows(v_plane_early, v_rows_early, V_ROWS_AT, V_ROW_STEP)
         sm_slots = keep.tile([P, PACK], F32, name="sm_slots")
         nc.sync.dma_start(sm_slots[:], sm.rearrange("(p t) -> p t", t=PACK))
         en_codes = keep.tile([P, N], I32, name="en_codes", align_bytes=ALIGN)
         nc.sync.dma_start(en_codes[:], en_words[0].rearrange("p n i -> p (n i)").bitcast(I32))
-        for r in range(QUAD_ROWS):
-            load_plane_rows(en_plane, en_scales, r)
+        load_plane(en_plane, en_scales)
+        load_plane(v_scale_window, tab_scales)
 
         v_words = {}
         v2_words = {}
         v2_parted = {}
+        v_planes = {}
+
+        def gather_words(words, window, lst, c):
+            nc.vector.tensor_copy(words[:], window[:].bitcast(U32).indirect(offsets(lst, CHUNK * c, CHUNK * (c + 1))))
 
         def gather_v(c, words):
-            offsets = list1[:, LIST_COLS * c : LIST_COLS * (c + 1)]
             v_words[c] = words
-            nc.vector.tensor_copy(words[:], v_window[:].bitcast(U32).indirect(offsets))
+            gather_words(words, v_window, list1, c)
 
         def gather_v2(c, words):
-            offsets = list2[:, LIST_COLS * c : LIST_COLS * (c + 1)]
             v2_words[c] = words
-            nc.vector.tensor_copy(words[:], v2_window[:].bitcast(U32).indirect(offsets))
+            gather_words(words, v2_window, list2, c)
 
-        def part_v2(c):
-            v2_parted[c] = keep.tile([P, 2 * V2_PASSES * CHUNK], U8, name="v2_parted%d" % c, align_bytes=ALIGN)
+        def part_v2(c, parted):
+            v2_parted[c] = parted
             nc.vector.tensor_copy(
-                v2_parted[c][:].bitcast(U16).rearrange("p (a j) -> p a j", a=V2_PASSES),
+                parted[:].bitcast(U16).rearrange("p (a j) -> p a j", a=V2_PASSES),
                 v2_words[c][:].bitcast(U16).rearrange("p (j a) -> p a j", a=V2_PASSES),
             )
 
+        def own(name, shape, dtype):
+            return keep.tile(shape, dtype, name=name, align_bytes=ALIGN)
 
-        wa_codes = place("wa_codes", [P, 2 * R], U8, "v2_words0")
-        wa_plane = place("wa_plane", [P, R], U8, "v2_words0", 2 * R)
-
-        def reorder_wa():
-            nc.vector.tensor_copy(
-                wa_plane[:].rearrange("p (t m) -> p t m", t=PACK),
-                wa_plane_raw[:].bitcast(U8).rearrange("p (m t) -> p t m", t=PACK),
-            )
-            nc.vector.tensor_copy(
-                wa_codes[:].bitcast(U16).rearrange("p (t m) -> p t m", t=PACK),
-                wa_words_raw[:].bitcast(U16).rearrange("p (m t) -> p t m", t=PACK),
-            )
-
-        wb_bf = [place("wb_bf%d" % a, [P, PACK, P, PACK], BF16, "wb_bf%d" % a) for a in range(V2_PASSES)]
-        wb_codes = [keep.tile([P, R], U32, name="wb_codes%d" % a, align_bytes=ALIGN) for a in range(V2_PASSES)]
-        wb_plane = [keep.tile([P, R], U8, name="wb_plane%d" % a, align_bytes=ALIGN) for a in range(V2_PASSES)]
+        wb_bf = [own("wb_bf0", [P, PACK, P, PACK], BF16), place("wb_bf1", [P, PACK, P, PACK], BF16, "wb_bf1")]
+        wb_codes = [own("wb_codes%d" % a, [P, R], U32) for a in range(V2_PASSES)]
+        wb_plane = [own("wb_plane%d" % a, [P, R], U8) for a in range(V2_PASSES)]
 
         def quantize_wb(a):
             nc.scalar.copy(
@@ -201,72 +179,48 @@ def tile_list_kg_tanh_sig_kernel(
                 in_=wb_bf[a][:].rearrange("p t m i -> p (t m i)"),
             )
 
-        z = {}
-
-        def open_z(c):
-            for b in range(GROUPS):
-                z[c, b] = psum.tile([P, PACK, GROUP], F32, name="bank%d" % (b + GROUPS * min(c, 1)))
-
-        def v2_pass(c, a, b, t, start, stop):
+        def v2_pass(c, a, t, j0, width, target, start, stop):
             cols = slice(P * t, P * (t + 1))
-            j0 = CHUNK * a + GROUP * b
+            at = CHUNK * a + j0
+            if c < CHUNKS - 1:
+                plane = v2_planes_early[a][:].bitcast(U8)[:, CHUNK * c + j0 : CHUNK * c + j0 + width]
+            else:
+                plane = v2_planes_late[a][:].bitcast(U8)[:, j0 : j0 + width]
             nc.tensor.matmul_mx(
-                out=z[c, b][:, t, :],
+                out=target,
                 lhsT=wb_codes[a][:, cols].bitcast(FP8X4),
                 lhsT_scale=wb_plane[a][:, cols],
-                rhs=v2_parted[c][:, 2 * j0 : 2 * (j0 + GROUP)].bitcast(FP4X4),
-                rhs_scale=v2_planes[a][:].bitcast(U8)[:, CHUNK * c + GROUP * b : CHUNK * c + GROUP * (b + 1)],
+                rhs=v2_parted[c][:, 2 * at : 2 * (at + width)].bitcast(FP4X4),
+                rhs_scale=plane,
                 start=start,
                 stop=stop,
             )
 
-        def v_pass(c, b, t, start, stop):
-            cols = slice(GROUP * b, GROUP * (b + 1))
+        def v_pass(c, t, j0, width, target, start, stop):
             nc.tensor.matmul_mx(
-                out=z[c, b][:, t, :],
+                out=target,
                 lhsT=wa_codes[:, 2 * P * t : 2 * P * (t + 1)].bitcast(FP4X4),
                 lhsT_scale=wa_plane[:, P * t : P * (t + 1)],
-                rhs=v_words[c][:, cols].bitcast(FP8X4),
-                rhs_scale=v_plane[:].bitcast(U8)[:, CHUNK * c + GROUP * b : CHUNK * c + GROUP * (b + 1)],
+                rhs=v_words[c][:, j0 : j0 + width].bitcast(FP8X4),
+                rhs_scale=v_planes[c][:, j0 : j0 + width],
                 start=start,
                 stop=stop,
             )
 
-        def add_v2_passes(c, opens):
-            for b in range(GROUPS):
-                for a in range(V2_PASSES):
-                    for t in range(PACK):
-                        first = a == 0 and t == 0
-                        last = a == V2_PASSES - 1 and t == PACK - 1
-                        v2_pass(c, a, b, t, opens and first, last and not opens)
-
-        def add_v_pass(c, opens):
-            for b in range(GROUPS):
-                for t in range(PACK):
-                    v_pass(c, b, t, opens and t == 0, t == PACK - 1 and not opens)
-
+        z = {}
         tanh_z = {}
         h_codes = {}
         h_plane = {}
 
-        def tanh_chunk(c):
-            tanh_z[c] = ring.tile([P, CHUNK, PACK], F32, name="tanh_z")
-            for b in range(GROUPS):
-                nc.scalar.activation(
-                    tanh_z[c][:, GROUP * b : GROUP * (b + 1), :], z[c, b][:].rearrange("p t j -> p j t"), ACT.Tanh
-                )
+        def tanh_slots(c, tile):
+            tanh_z[c] = tile
+            for t in range(PACK):
+                nc.scalar.activation(tile[:, t, :], z[c][t][:], ACT.Tanh)
 
-        def make_h(c, width):
-            h_codes[c] = ring.tile([P, CHUNK], U32, name="h_codes", align_bytes=ALIGN)
-            h_plane[c] = ring.tile([P, CHUNK], U8, name="h_plane", align_bytes=ALIGN)
-            factor = sm_slots[:].rearrange("p (j t) -> p j t", j=1).to_broadcast([P, width, PACK])
+        def make_h(c, width, scale, codes):
+            h_codes[c] = codes
+            h_plane[c] = own("h_plane%d" % c, [P, CHUNK], U8)
             h_bf = {}
-
-            def scale(j0):
-                name = "h_bf%d_%d" % (c, j0)
-                where = "h_bf%d" % (c - 1 if c > 0 and j0 == 0 else c)
-                h_bf[j0] = place(name, [P, width, PACK], BF16, where, 2 * PACK * j0)
-                nc.vector.tensor_tensor(h_bf[j0][:], tanh_z[c][:, j0 : j0 + width, :], factor, MULT)
 
             def quantize(j0):
                 nc.vector.quantize_mx(
@@ -275,16 +229,40 @@ def tile_list_kg_tanh_sig_kernel(
                     in_=h_bf[j0][:].rearrange("p j t -> p (j t)"),
                 )
 
-            scale(0)
+            h_bf[0] = scale(0)
             for j0 in range(width, CHUNK, width):
-                scale(j0)
+                h_bf[j0] = scale(j0)
                 quantize(j0 - width)
             quantize(CHUNK - width)
+
+        def scale_group(j0):
+            h_bf = own("h_bf0_%d" % j0, [P, GROUP, PACK], BF16)
+            factor = sm_slots[:].rearrange("p (j t) -> p j t", j=1).to_broadcast([P, GROUP, PACK])
+            nc.vector.tensor_tensor(h_bf[:], tanh_z[0][j0 // GROUP][:], factor, MULT)
+            return h_bf
+
+        def scale_half(c):
+            def scale(j0):
+                name = "h_bf%d_%d" % (c, j0)
+                if c == 1:
+                    h_bf = place(name, [P, HALF, PACK], BF16, "v_scale_window", 2 * PACK * j0)
+                else:
+                    h_bf = own(name, [P, HALF, PACK], BF16)
+                factor = sm_slots[:].rearrange("p (g t i) -> p g t i", g=1, i=1).to_broadcast([P, HALF // RUN, PACK, RUN])
+                nc.vector.tensor_tensor(
+                    h_bf[:].rearrange("p (g i) t -> p g t i", i=RUN),
+                    tanh_z[c][:, :, j0 : j0 + HALF].rearrange("p t (g i) -> p g t i", i=RUN),
+                    factor,
+                    MULT,
+                )
+                return h_bf
+
+            return scale
 
         def score_chunk(c):
             for b in range(N // P):
                 cols = slice(P * b, P * (b + 1))
-                y = psum.tile([P, CHUNK], F32, name="bank%d" % (b % GROUPS))
+                y = bank(b, [P, CHUNK])
                 nc.tensor.matmul_mx(
                     out=y[:],
                     lhsT=en_codes[:, cols].bitcast(FP8X4),
@@ -299,37 +277,82 @@ def tile_list_kg_tanh_sig_kernel(
                 nc.sync.dma_start(out[cols, CHUNK * c : CHUNK * (c + 1)], prob[:])
 
         quantize_wb(0)
+        wa_plane = own("wa_plane", [P, R], U8)
+        nc.vector.tensor_copy(
+            wa_plane[:].rearrange("p (t m) -> p t m", t=PACK),
+            wa_plane_raw[:].bitcast(U8).rearrange("p (m t) -> p t m", t=PACK),
+        )
         for c in range(2):
             gather_v2(c, place("v2_words%d" % c, [P, CHUNK], U32, "v2_words%d" % c))
-            part_v2(c)
-        reorder_wa()
+            part_v2(c, own("v2_parted%d" % c, [P, WORDS], U8))
+            v_planes[c] = v_plane_early[:].bitcast(U8)[:, CHUNK * c : CHUNK * (c + 1)]
+        wa_codes = place("wa_codes", [P, 2 * R], U8, "v2_words0")
+        nc.vector.tensor_copy(
+            wa_codes[:].bitcast(U16).rearrange("p (t m) -> p t m", t=PACK),
+            wa_words_raw[:].bitcast(U16).rearrange("p (m t) -> p t m", t=PACK),
+        )
+        v2_rows_late = place("v2_rows_late", [P, CHUNK], U8, "v2_words1")
+        gather_bytes(v2_rows_late, v2_scale_window, list2, J - CHUNK, J)
         quantize_wb(1)
-        for c in range(2):
-            open_z(c)
-            add_v2_passes(c, True)
-        gather_v_scales(1, place("v_rows1", [P, CHUNK], U8, "wb_bf1"))
-        move_v_rows(1)
-        gather_v2_scales(1, place("v2_rows1", [P, CHUNK], U8, "wb_bf1", CHUNK))
-        for a in range(V2_PASSES):
-            move_v2_rows(1, a)
-        for c in range(2):
-            gather_v(c, keep.tile([P, CHUNK], U32, name="v_words%d" % c, align_bytes=ALIGN))
-            add_v_pass(c, False)
-        tanh_chunk(0)
-        make_h(0, GROUP)
-        tanh_chunk(1)
+        gather_v2(2, place("v2_words2", [P, CHUNK], U32, "wb_bf1"))
 
-        for c in range(CHUNKS):
-            ahead = c + 2
-            if ahead < CHUNKS:
-                gather_v(ahead, place("v_words%d" % ahead, [P, CHUNK], U32, "h_bf%d" % c, H_BYTES - ALIGN))
-                gather_v2(ahead, place("v2_words%d" % ahead, [P, CHUNK], U32, "h_bf%d" % c, LAST_PIECE + ALIGN - WORD_BYTES))
-                part_v2(ahead)
-            score_chunk(c)
-            if c + 1 < CHUNKS:
-                make_h(c + 1, HALF_CHUNK)
-            if ahead < CHUNKS:
-                open_z(ahead)
-                add_v_pass(ahead, True)
-                add_v2_passes(ahead, False)
-                tanh_chunk(ahead)
+        z[0] = [bank(b, [P, PACK, GROUP]) for b in range(PACK)]
+        z[1] = [bank(PACK + t, [P, CHUNK]) for t in range(PACK)]
+        for b in range(PACK):
+            for t in range(PACK):
+                v2_pass(0, 0, t, GROUP * b, GROUP, z[0][b][:, t, :], t == 0, False)
+        for t in range(PACK):
+            v2_pass(1, 0, t, 0, CHUNK, z[1][t][:], True, False)
+        for b in range(PACK):
+            for t in range(PACK):
+                v2_pass(0, 1, t, GROUP * b, GROUP, z[0][b][:, t, :], False, False)
+
+        for c in range(2):
+            gather_v(c, own("v_words%d" % c, [P, CHUNK], U32))
+        tanh_z[0] = []
+        for b in range(PACK):
+            for t in range(PACK):
+                v_pass(0, t, GROUP * b, GROUP, z[0][b][:, t, :], False, t == PACK - 1)
+            piece = place("tanh0_%d" % b, [P, GROUP, PACK], F32, "tanh0", 4 * CHUNK * b)
+            nc.scalar.activation(piece[:], z[0][b][:].rearrange("p t j -> p j t"), ACT.Tanh)
+            tanh_z[0].append(piece)
+        for t in range(PACK):
+            v_pass(1, t, 0, CHUNK, z[1][t][:], False, False)
+            v2_pass(1, 1, t, 0, CHUNK, z[1][t][:], False, True)
+        for a in range(V2_PASSES):
+            move_rows(v2_planes_late[a], v2_rows_late, V2_ROWS_AT + BLOCKS * a, 1)
+        make_h(0, GROUP, scale_group, own("h_codes0", [P, CHUNK], U32))
+        tanh_slots(1, place("tanh1", [P, PACK, CHUNK], F32, "tanh1"))
+
+        last_piece = 4 * CHUNK * (PACK - 1)
+        part_v2(2, place("v2_parted2", [P, WORDS], U8, "tanh0", last_piece - WORDS // 2))
+        gather_v(2, place("v_words2", [P, CHUNK], U32, "tanh0", last_piece + WORDS // 2))
+        v_plane_late = own("v_plane_late", [P, 2 * CHUNK], U8)
+        gather_bytes(v_plane_late, v_scale_window, list1, 2 * CHUNK, J)
+        for c in range(2, CHUNKS):
+            v_planes[c] = v_plane_late[:, CHUNK * (c - 2) : CHUNK * (c - 1)]
+        score_chunk(0)
+        z[2] = [bank(t, [P, CHUNK]) for t in range(PACK)]
+        for t in range(PACK):
+            for a in range(V2_PASSES):
+                v2_pass(2, a, t, 0, CHUNK, z[2][t][:], a == 0, False)
+        for t in range(PACK):
+            v_pass(2, t, 0, CHUNK, z[2][t][:], False, True)
+        make_h(1, HALF, scale_half(1), place("h_codes1", [P, CHUNK], U32, "tanh0", last_piece + WORDS // 2))
+        tanh_slots(2, own("tanh2", [P, PACK, CHUNK], F32))
+
+        gather_v2(3, place("v2_words3", [P, CHUNK], U32, "tanh1"))
+        gather_v(3, place("v_words3", [P, CHUNK], U32, "tanh1", WORDS))
+        part_v2(3, place("v2_parted3", [P, WORDS], U8, "v2_parted3"))
+        score_chunk(1)
+        z[3] = [bank(t, [P, CHUNK]) for t in range(PACK)]
+        for t in range(PACK):
+            v_pass(3, t, 0, CHUNK, z[3][t][:], True, False)
+        for t in range(PACK):
+            for a in range(V2_PASSES):
+                v2_pass(3, a, t, 0, CHUNK, z[3][t][:], False, a == V2_PASSES - 1)
+        make_h(2, HALF, scale_half(2), place("h_codes2", [P, CHUNK], U32, "v2_parted3"))
+        tanh_slots(3, own("tanh3", [P, PACK, CHUNK], F32))
+        score_chunk(2)
+        make_h(3, HALF, scale_half(3), own("h_codes3", [P, CHUNK], U32))
+        score_chunk(3)

@@ -30,7 +30,8 @@ V2_ROWS_AT = P - V2_PASSES * BLOCKS
 V_ROWS_AT = 4
 V_ROW_STEP = P // BLOCKS
 GROUP = CHUNK // PACK
-RUN = 4
+RUN = 2
+BANKS = 8
 ALIGN = 64
 WORDS = 4 * CHUNK
 
@@ -42,7 +43,8 @@ def tile_list_kg_tanh_sig_kernel(
     with ExitStack() as ctx:
         keep = ctx.enter_context(tc.tile_pool(name="keep", bufs=1))
         arena = ctx.enter_context(tc.tile_pool(name="arena", bufs=1))
-        stage = ctx.enter_context(tc.tile_pool(name="stage", bufs=CHUNKS * N // P))
+        stage = ctx.enter_context(tc.tile_pool(name="stage", bufs=3 * N // P))
+        early = ctx.enter_context(tc.tile_pool(name="early", bufs=4))
         psum = ctx.enter_context(tc.psum_pool(name="psum", bufs=1))
 
         cells = {}
@@ -61,10 +63,13 @@ def tile_list_kg_tanh_sig_kernel(
         cell("wb_bf1", 8 * R)
         cell("tanh0", 4 * PACK * CHUNK + WORDS // 2)
         cell("tanh1", 4 * PACK * CHUNK)
-        cell("v2_parted3", WORDS)
 
-        def bank(b, shape):
-            return psum.tile(shape, F32, name="bank%d" % b)
+        fills = [0]
+
+        def next_bank(shape):
+            bank = psum.tile(shape, F32, name="bank%d" % (fills[0] % BANKS))
+            fills[0] = fills[0] + 1
+            return bank
 
         def offsets(lst, j0, j1):
             return lst[:, j0 // 16 : j1 // 16]
@@ -170,8 +175,8 @@ def tile_list_kg_tanh_sig_kernel(
 
         def quantize_wb(a):
             nc.scalar.copy(
-                wb_bf[a][:].rearrange("p t m i -> p m i t"),
-                wb_raw[a][:].rearrange("p i (m t) -> p m i t", t=PACK),
+                wb_bf[a][:].rearrange("p (u e) m i -> p u m i e", e=2),
+                wb_raw[a][:].rearrange("p i (m u e) -> p u m i e", u=2, e=2),
             )
             nc.vector.quantize_mx(
                 out=wb_codes[a][:].bitcast(FP8X4),
@@ -259,19 +264,39 @@ def tile_list_kg_tanh_sig_kernel(
 
             return scale
 
+        def score_pass(c, b, j0, width, target):
+            cols = slice(P * b, P * (b + 1))
+            nc.tensor.matmul_mx(
+                out=target,
+                lhsT=en_codes[:, cols].bitcast(FP8X4),
+                lhsT_scale=en_plane[:].bitcast(U8)[:, cols],
+                rhs=h_codes[c][:, j0 : j0 + width].bitcast(FP8X4),
+                rhs_scale=h_plane[c][:, j0 : j0 + width],
+                start=True,
+                stop=True,
+            )
+
+        def score_halves(c):
+            probs = [early.tile([P, 2, CHUNK], F32, name="prob_pair") for g in range(2)]
+            for half in range(2):
+                for g in range(2):
+                    y = next_bank([P, 2, HALF])
+                    for e in range(2):
+                        score_pass(c, 2 * g + e, HALF * half, HALF, y[:, e, :])
+                    nc.scalar.activation(probs[g][:, :, HALF * half : HALF * (half + 1)], y[:], ACT.Sigmoid)
+                    if half == 1:
+                        rows = out[2 * P * g : 2 * P * (g + 1), CHUNK * c : CHUNK * (c + 1)]
+                        nc.sync.dma_start(rows.rearrange("(e p) j -> p e j", p=P), probs[g][:])
+
         def score_chunk(c):
-            for b in range(N // P):
+            first = 0
+            if c < 2:
+                score_halves(c)
+                first = PACK
+            for b in range(first, N // P):
                 cols = slice(P * b, P * (b + 1))
-                y = bank(b, [P, CHUNK])
-                nc.tensor.matmul_mx(
-                    out=y[:],
-                    lhsT=en_codes[:, cols].bitcast(FP8X4),
-                    lhsT_scale=en_plane[:].bitcast(U8)[:, cols],
-                    rhs=h_codes[c][:].bitcast(FP8X4),
-                    rhs_scale=h_plane[c][:],
-                    start=True,
-                    stop=True,
-                )
+                y = next_bank([P, CHUNK])
+                score_pass(c, b, 0, CHUNK, y[:])
                 prob = stage.tile([P, CHUNK], F32, name="prob")
                 nc.scalar.activation(prob[:], y[:], ACT.Sigmoid)
                 nc.sync.dma_start(out[cols, CHUNK * c : CHUNK * (c + 1)], prob[:])
@@ -296,8 +321,8 @@ def tile_list_kg_tanh_sig_kernel(
         quantize_wb(1)
         gather_v2(2, place("v2_words2", [P, CHUNK], U32, "wb_bf1"))
 
-        z[0] = [bank(b, [P, PACK, GROUP]) for b in range(PACK)]
-        z[1] = [bank(PACK + t, [P, CHUNK]) for t in range(PACK)]
+        z[0] = [next_bank([P, PACK, GROUP]) for b in range(PACK)]
+        z[1] = [next_bank([P, CHUNK]) for t in range(PACK)]
         for b in range(PACK):
             for t in range(PACK):
                 v2_pass(0, 0, t, GROUP * b, GROUP, z[0][b][:, t, :], t == 0, False)
@@ -332,26 +357,26 @@ def tile_list_kg_tanh_sig_kernel(
         for c in range(2, CHUNKS):
             v_planes[c] = v_plane_late[:, CHUNK * (c - 2) : CHUNK * (c - 1)]
         score_chunk(0)
-        z[2] = [bank(t, [P, CHUNK]) for t in range(PACK)]
+        z[2] = [next_bank([P, CHUNK]) for t in range(PACK)]
         for t in range(PACK):
             for a in range(V2_PASSES):
                 v2_pass(2, a, t, 0, CHUNK, z[2][t][:], a == 0, False)
         for t in range(PACK):
             v_pass(2, t, 0, CHUNK, z[2][t][:], False, True)
-        make_h(1, HALF, scale_half(1), place("h_codes1", [P, CHUNK], U32, "tanh0", last_piece + WORDS // 2))
+        make_h(1, HALF, scale_half(1), own("h_codes1", [P, CHUNK], U32))
         tanh_slots(2, own("tanh2", [P, PACK, CHUNK], F32))
 
         gather_v2(3, place("v2_words3", [P, CHUNK], U32, "tanh1"))
         gather_v(3, place("v_words3", [P, CHUNK], U32, "tanh1", WORDS))
-        part_v2(3, place("v2_parted3", [P, WORDS], U8, "v2_parted3"))
+        part_v2(3, own("v2_parted3", [P, WORDS], U8))
         score_chunk(1)
-        z[3] = [bank(t, [P, CHUNK]) for t in range(PACK)]
+        z[3] = [next_bank([P, CHUNK]) for t in range(PACK)]
         for t in range(PACK):
             v_pass(3, t, 0, CHUNK, z[3][t][:], True, False)
         for t in range(PACK):
             for a in range(V2_PASSES):
                 v2_pass(3, a, t, 0, CHUNK, z[3][t][:], False, a == V2_PASSES - 1)
-        make_h(2, HALF, scale_half(2), place("h_codes2", [P, CHUNK], U32, "v2_parted3"))
+        make_h(2, HALF, scale_half(2), own("h_codes2", [P, CHUNK], U32))
         tanh_slots(3, own("tanh3", [P, PACK, CHUNK], F32))
         score_chunk(2)
         make_h(3, HALF, scale_half(3), own("h_codes3", [P, CHUNK], U32))

@@ -32,6 +32,7 @@ V_ROW_STEP = P // BLOCKS
 GROUP = CHUNK // PACK
 RUN = 2
 BANKS = 8
+EARLY_SLOTS = 3
 ALIGN = 64
 WORDS = 4 * CHUNK
 
@@ -43,8 +44,7 @@ def tile_list_kg_tanh_sig_kernel(
     with ExitStack() as ctx:
         keep = ctx.enter_context(tc.tile_pool(name="keep", bufs=1))
         arena = ctx.enter_context(tc.tile_pool(name="arena", bufs=1))
-        stage = ctx.enter_context(tc.tile_pool(name="stage", bufs=3 * N // P))
-        early = ctx.enter_context(tc.tile_pool(name="early", bufs=4))
+        stage = ctx.enter_context(tc.tile_pool(name="stage", bufs=CHUNKS * N // P))
         psum = ctx.enter_context(tc.psum_pool(name="psum", bufs=1))
 
         cells = {}
@@ -57,7 +57,7 @@ def tile_list_kg_tanh_sig_kernel(
         def place(name, shape, dtype, where, skip=0):
             return arena.tile(shape, dtype, name=name, align_bytes=ALIGN, offset=cells[where] + skip)
 
-        cell("v_scale_window", T)
+        cell("h_bf1", 2 * PACK * CHUNK)
         cell("v2_words0", WORDS)
         cell("v2_words1", WORDS)
         cell("wb_bf1", 8 * R)
@@ -82,7 +82,7 @@ def tile_list_kg_tanh_sig_kernel(
         list1 = keep.tile([P, J // 16], U16, name="list1")
         list2 = keep.tile([P, J // 16], U16, name="list2")
         v2_scale_window = keep.tile([P, T // 4], I32, name="v2_scale_window", align_bytes=ALIGN)
-        v_scale_window = place("v_scale_window", [P, T // 4], I32, "v_scale_window")
+        v_scale_window = keep.tile([P, T // 4], I32, name="v_scale_window", align_bytes=ALIGN)
         wa_plane_raw = keep.tile([P, R // 4], I32, name="wa_plane_raw", align_bytes=ALIGN)
         en_plane = keep.tile([P, N // 4], I32, name="en_plane", align_bytes=ALIGN)
         v2_planes_early = [
@@ -140,8 +140,8 @@ def tile_list_kg_tanh_sig_kernel(
         nc.sync.dma_start(sm_slots[:], sm.rearrange("(p t) -> p t", t=PACK))
         en_codes = keep.tile([P, N], I32, name="en_codes", align_bytes=ALIGN)
         nc.sync.dma_start(en_codes[:], en_words[0].rearrange("p n i -> p (n i)").bitcast(I32))
-        load_plane(en_plane, en_scales)
         load_plane(v_scale_window, tab_scales)
+        load_plane(en_plane, en_scales)
 
         v_words = {}
         v2_words = {}
@@ -154,6 +154,10 @@ def tile_list_kg_tanh_sig_kernel(
         def gather_v(c, words):
             v_words[c] = words
             gather_words(words, v_window, list1, c)
+
+        def gather_v_plane(c, plane):
+            v_planes[c] = plane[:]
+            gather_bytes(plane, v_scale_window, list1, CHUNK * c, CHUNK * (c + 1))
 
         def gather_v2(c, words):
             v2_words[c] = words
@@ -250,7 +254,7 @@ def tile_list_kg_tanh_sig_kernel(
             def scale(j0):
                 name = "h_bf%d_%d" % (c, j0)
                 if c == 1:
-                    h_bf = place(name, [P, HALF, PACK], BF16, "v_scale_window", 2 * PACK * j0)
+                    h_bf = place(name, [P, HALF, PACK], BF16, "h_bf1", 2 * PACK * j0)
                 else:
                     h_bf = own(name, [P, HALF, PACK], BF16)
                 factor = sm_slots[:].rearrange("p (g t i) -> p g t i", g=1, i=1).to_broadcast([P, HALF // RUN, PACK, RUN])
@@ -277,29 +281,23 @@ def tile_list_kg_tanh_sig_kernel(
             )
 
         def score_halves(c):
-            probs = [early.tile([P, 2, CHUNK], F32, name="prob_pair") for g in range(2)]
             for half in range(2):
                 for g in range(2):
                     y = next_bank([P, 2, HALF])
                     for e in range(2):
                         score_pass(c, 2 * g + e, HALF * half, HALF, y[:, e, :])
-                    nc.scalar.activation(probs[g][:, :, HALF * half : HALF * (half + 1)], y[:], ACT.Sigmoid)
-                    if half == 1:
-                        rows = out[2 * P * g : 2 * P * (g + 1), CHUNK * c : CHUNK * (c + 1)]
-                        nc.sync.dma_start(rows.rearrange("(e p) j -> p e j", p=P), probs[g][:])
+                    prob = stage.tile([P, 2, HALF], F32, name="prob")
+                    nc.scalar.activation(prob[:], y[:], ACT.Sigmoid)
+                    rows = out[2 * P * g : 2 * P * (g + 1), CHUNK * c + HALF * half : CHUNK * c + HALF * (half + 1)]
+                    nc.sync.dma_start(rows.rearrange("(e p) j -> p e j", p=P), prob[:])
 
-        def score_chunk(c):
-            first = 0
-            if c < 2:
-                score_halves(c)
-                first = PACK
-            for b in range(first, N // P):
-                cols = slice(P * b, P * (b + 1))
+        def score(c, blocks):
+            for b in blocks:
                 y = next_bank([P, CHUNK])
                 score_pass(c, b, 0, CHUNK, y[:])
                 prob = stage.tile([P, CHUNK], F32, name="prob")
                 nc.scalar.activation(prob[:], y[:], ACT.Sigmoid)
-                nc.sync.dma_start(out[cols, CHUNK * c : CHUNK * (c + 1)], prob[:])
+                nc.sync.dma_start(out[P * b : P * (b + 1), CHUNK * c : CHUNK * (c + 1)], prob[:])
 
         quantize_wb(0)
         wa_plane = own("wa_plane", [P, R], U8)
@@ -331,6 +329,8 @@ def tile_list_kg_tanh_sig_kernel(
         for b in range(PACK):
             for t in range(PACK):
                 v2_pass(0, 1, t, GROUP * b, GROUP, z[0][b][:, t, :], False, False)
+        for t in range(EARLY_SLOTS):
+            v2_pass(1, 1, t, 0, CHUNK, z[1][t][:], False, False)
 
         for c in range(2):
             gather_v(c, own("v_words%d" % c, [P, CHUNK], U32))
@@ -342,21 +342,20 @@ def tile_list_kg_tanh_sig_kernel(
             nc.scalar.activation(piece[:], z[0][b][:].rearrange("p t j -> p j t"), ACT.Tanh)
             tanh_z[0].append(piece)
         for t in range(PACK):
-            v_pass(1, t, 0, CHUNK, z[1][t][:], False, False)
-            v2_pass(1, 1, t, 0, CHUNK, z[1][t][:], False, True)
+            v_pass(1, t, 0, CHUNK, z[1][t][:], False, t < EARLY_SLOTS)
+            if t >= EARLY_SLOTS:
+                v2_pass(1, 1, t, 0, CHUNK, z[1][t][:], False, True)
         for a in range(V2_PASSES):
             move_rows(v2_planes_late[a], v2_rows_late, V2_ROWS_AT + BLOCKS * a, 1)
-        make_h(0, GROUP, scale_group, own("h_codes0", [P, CHUNK], U32))
+        make_h(0, GROUP, scale_group, place("h_codes0", [P, CHUNK], U32, "h_bf1", WORDS // 2))
         tanh_slots(1, place("tanh1", [P, PACK, CHUNK], F32, "tanh1"))
 
         last_piece = 4 * CHUNK * (PACK - 1)
         part_v2(2, place("v2_parted2", [P, WORDS], U8, "tanh0", last_piece - WORDS // 2))
         gather_v(2, place("v_words2", [P, CHUNK], U32, "tanh0", last_piece + WORDS // 2))
-        v_plane_late = own("v_plane_late", [P, 2 * CHUNK], U8)
-        gather_bytes(v_plane_late, v_scale_window, list1, 2 * CHUNK, J)
-        for c in range(2, CHUNKS):
-            v_planes[c] = v_plane_late[:, CHUNK * (c - 2) : CHUNK * (c - 1)]
-        score_chunk(0)
+        gather_v_plane(2, place("v_plane2", [P, CHUNK], U8, "wb_bf1"))
+        score_halves(0)
+        score(0, range(PACK, N // P))
         z[2] = [next_bank([P, CHUNK]) for t in range(PACK)]
         for t in range(PACK):
             for a in range(V2_PASSES):
@@ -369,15 +368,16 @@ def tile_list_kg_tanh_sig_kernel(
         gather_v2(3, place("v2_words3", [P, CHUNK], U32, "tanh1"))
         gather_v(3, place("v_words3", [P, CHUNK], U32, "tanh1", WORDS))
         part_v2(3, own("v2_parted3", [P, WORDS], U8))
-        score_chunk(1)
+        gather_v_plane(3, place("v_plane3", [P, CHUNK], U8, "tanh1", 2 * WORDS))
+        score(1, range(N // P))
         z[3] = [next_bank([P, CHUNK]) for t in range(PACK)]
         for t in range(PACK):
-            v_pass(3, t, 0, CHUNK, z[3][t][:], True, False)
-        for t in range(PACK):
             for a in range(V2_PASSES):
-                v2_pass(3, a, t, 0, CHUNK, z[3][t][:], False, a == V2_PASSES - 1)
+                v2_pass(3, a, t, 0, CHUNK, z[3][t][:], a == 0, False)
+        for t in range(PACK):
+            v_pass(3, t, 0, CHUNK, z[3][t][:], False, True)
         make_h(2, HALF, scale_half(2), own("h_codes2", [P, CHUNK], U32))
         tanh_slots(3, own("tanh3", [P, PACK, CHUNK], F32))
-        score_chunk(2)
+        score(2, range(N // P))
         make_h(3, HALF, scale_half(3), own("h_codes3", [P, CHUNK], U32))
-        score_chunk(3)
+        score(3, range(N // P))

@@ -61,15 +61,22 @@ def tile_list_kg_tanh_sig_kernel(
         cell("v2_words0", WORDS)
         cell("v2_words1", WORDS)
         cell("wb_bf1", 8 * R)
+        cell("v_rows_early", WORDS)
+        cell("tanh2", 4 * PACK * CHUNK)
         cell("tanh0", 4 * PACK * CHUNK + WORDS // 2)
         cell("tanh1", 4 * PACK * CHUNK)
 
         fills = [0]
 
+        def bank(b, shape):
+            return psum.tile(shape, F32, name="bank%d" % b)
+
+        def next_banks(count):
+            fills[0] = fills[0] + count
+            return [b % BANKS for b in range(fills[0] - count, fills[0])]
+
         def next_bank(shape):
-            bank = psum.tile(shape, F32, name="bank%d" % (fills[0] % BANKS))
-            fills[0] = fills[0] + 1
-            return bank
+            return bank(next_banks(1)[0], shape)
 
         def offsets(lst, j0, j1):
             return lst[:, j0 // 16 : j1 // 16]
@@ -127,7 +134,7 @@ def tile_list_kg_tanh_sig_kernel(
 
         v2_rows_early = keep.tile([P, J - CHUNK], U8, name="v2_rows_early", align_bytes=ALIGN)
         gather_bytes(v2_rows_early, v2_scale_window, list2, 0, J - CHUNK)
-        v_rows_early = keep.tile([P, 2 * CHUNK], U8, name="v_rows_early", align_bytes=ALIGN)
+        v_rows_early = place("v_rows_early", [P, 2 * CHUNK], U8, "v_rows_early")
         gather_bytes(v_rows_early, v_scale_window, list1, 0, 2 * CHUNK)
 
         v_window = keep.tile([P, T], I32, name="v_window", align_bytes=ALIGN)
@@ -257,10 +264,11 @@ def tile_list_kg_tanh_sig_kernel(
                     h_bf = place(name, [P, HALF, PACK], BF16, "h_bf1", 2 * PACK * j0)
                 else:
                     h_bf = own(name, [P, HALF, PACK], BF16)
+                source = tanh_z[c][j0 // HALF][:] if c == CHUNKS - 1 else tanh_z[c][:, :, j0 : j0 + HALF]
                 factor = sm_slots[:].rearrange("p (g t i) -> p g t i", g=1, i=1).to_broadcast([P, HALF // RUN, PACK, RUN])
                 nc.vector.tensor_tensor(
                     h_bf[:].rearrange("p (g i) t -> p g t i", i=RUN),
-                    tanh_z[c][:, :, j0 : j0 + HALF].rearrange("p t (g i) -> p g t i", i=RUN),
+                    source.rearrange("p t (g i) -> p g t i", i=RUN),
                     factor,
                     MULT,
                 )
@@ -291,9 +299,9 @@ def tile_list_kg_tanh_sig_kernel(
                     rows = out[2 * P * g : 2 * P * (g + 1), CHUNK * c + HALF * half : CHUNK * c + HALF * (half + 1)]
                     nc.sync.dma_start(rows.rearrange("(e p) j -> p e j", p=P), prob[:])
 
-        def score(c, blocks):
-            for b in blocks:
-                y = next_bank([P, CHUNK])
+        def score(c, blocks, banks):
+            for b, where in zip(blocks, banks):
+                y = bank(where, [P, CHUNK])
                 score_pass(c, b, 0, CHUNK, y[:])
                 prob = stage.tile([P, CHUNK], F32, name="prob")
                 nc.scalar.activation(prob[:], y[:], ACT.Sigmoid)
@@ -334,6 +342,7 @@ def tile_list_kg_tanh_sig_kernel(
 
         for c in range(2):
             gather_v(c, own("v_words%d" % c, [P, CHUNK], U32))
+        part_v2(2, place("v2_parted2", [P, WORDS], U8, "v_rows_early"))
         tanh_z[0] = []
         for b in range(PACK):
             for t in range(PACK):
@@ -351,11 +360,10 @@ def tile_list_kg_tanh_sig_kernel(
         tanh_slots(1, place("tanh1", [P, PACK, CHUNK], F32, "tanh1"))
 
         last_piece = 4 * CHUNK * (PACK - 1)
-        part_v2(2, place("v2_parted2", [P, WORDS], U8, "tanh0", last_piece - WORDS // 2))
         gather_v(2, place("v_words2", [P, CHUNK], U32, "tanh0", last_piece + WORDS // 2))
-        gather_v_plane(2, place("v_plane2", [P, CHUNK], U8, "wb_bf1"))
+        gather_v_plane(2, place("v_plane2", [P, CHUNK], U8, "tanh0", last_piece))
         score_halves(0)
-        score(0, range(PACK, N // P))
+        score(0, range(PACK, N // P), next_banks(PACK))
         z[2] = [next_bank([P, CHUNK]) for t in range(PACK)]
         for t in range(PACK):
             for a in range(V2_PASSES):
@@ -363,21 +371,35 @@ def tile_list_kg_tanh_sig_kernel(
         for t in range(PACK):
             v_pass(2, t, 0, CHUNK, z[2][t][:], False, True)
         make_h(1, HALF, scale_half(1), own("h_codes1", [P, CHUNK], U32))
-        tanh_slots(2, own("tanh2", [P, PACK, CHUNK], F32))
+        tanh_slots(2, place("tanh2", [P, PACK, CHUNK], F32, "tanh2"))
 
         gather_v2(3, place("v2_words3", [P, CHUNK], U32, "tanh1"))
-        gather_v(3, place("v_words3", [P, CHUNK], U32, "tanh1", WORDS))
         part_v2(3, own("v2_parted3", [P, WORDS], U8))
-        gather_v_plane(3, place("v_plane3", [P, CHUNK], U8, "tanh1", 2 * WORDS))
-        score(1, range(N // P))
-        z[3] = [next_bank([P, CHUNK]) for t in range(PACK)]
-        for t in range(PACK):
-            for a in range(V2_PASSES):
-                v2_pass(3, a, t, 0, CHUNK, z[3][t][:], a == 0, False)
-        for t in range(PACK):
-            v_pass(3, t, 0, CHUNK, z[3][t][:], False, True)
+        score(1, range(N // P), next_banks(BANKS))
         make_h(2, HALF, scale_half(2), own("h_codes2", [P, CHUNK], U32))
-        tanh_slots(3, own("tanh3", [P, PACK, CHUNK], F32))
-        score(2, range(N // P))
+        gather_v(3, place("v_words3", [P, CHUNK], U32, "tanh2"))
+        gather_v_plane(3, place("v_plane3", [P, CHUNK], U8, "tanh2", WORDS))
+        emptied = next_banks(BANKS)
+        z_banks = emptied[:2] + emptied[-2:]
+        score_banks = emptied[2:-2]
+        z[3] = {}
+
+        def open_last(b):
+            z[3][b] = bank(z_banks[b], [P, 2, HALF])
+            for a in range(V2_PASSES):
+                for e in range(2):
+                    v2_pass(3, a, 2 * (b % 2) + e, HALF * (b // 2), HALF, z[3][b][:, e, :], a == 0 and e == 0, False)
+
+        for b in range(2):
+            open_last(b)
+        score(2, range(PACK), score_banks)
+        for b in range(2, PACK):
+            open_last(b)
+        tanh_z[3] = [own("tanh3_%d" % half, [P, PACK, HALF], F32) for half in range(2)]
+        for b in range(PACK):
+            for e in range(2):
+                v_pass(3, 2 * (b % 2) + e, HALF * (b // 2), HALF, z[3][b][:, e, :], False, e == 1)
+            nc.scalar.activation(tanh_z[3][b // 2][:, 2 * (b % 2) : 2 * (b % 2) + 2, :], z[3][b][:], ACT.Tanh)
+        score(2, range(PACK, N // P), z_banks)
         make_h(3, HALF, scale_half(3), own("h_codes3", [P, CHUNK], U32))
-        score(3, range(N // P))
+        score(3, range(N // P), score_banks + z_banks)

@@ -27,12 +27,13 @@ BLOCKS = 16
 QUAD = 32
 QUAD_ROWS = 4
 V2_ROWS_AT = P - V2_PASSES * BLOCKS
-V_ROWS_AT = 4
-V_ROW_STEP = P // BLOCKS
+V_ROWS_AT = P - BLOCKS
+V_EARLY = 3 * CHUNK
+V2_EARLY = 2 * CHUNK
 GROUP = CHUNK // PACK
 RUN = 2
 BANKS = 8
-EARLY_SLOTS = 3
+EARLY_SLOTS = 0
 ALIGN = 64
 WORDS = 4 * CHUNK
 
@@ -57,13 +58,10 @@ def tile_list_kg_tanh_sig_kernel(
         def place(name, shape, dtype, where, skip=0):
             return arena.tile(shape, dtype, name=name, align_bytes=ALIGN, offset=cells[where] + skip)
 
-        cell("h_bf1", 2 * PACK * CHUNK)
-        cell("v2_words0", WORDS)
         cell("v2_words1", WORDS)
         cell("wb_bf1", 8 * R)
-        cell("v_rows_early", WORDS)
         cell("tanh2", 4 * PACK * CHUNK)
-        cell("tanh0", 4 * PACK * CHUNK + WORDS // 2)
+        cell("tanh0", 4 * PACK * CHUNK + WORDS)
         cell("tanh1", 4 * PACK * CHUNK)
 
         fills = [0]
@@ -86,68 +84,63 @@ def tile_list_kg_tanh_sig_kernel(
             nc.sync.dma_start(raw[:], wb[K_PASS * a : K_PASS * (a + 1), :].rearrange("(p i) r -> p i r", i=PACK))
             return raw
 
+        def own(name, shape, dtype):
+            return keep.tile(shape, dtype, name=name, align_bytes=ALIGN)
+
         list1 = keep.tile([P, J // 16], U16, name="list1")
         list2 = keep.tile([P, J // 16], U16, name="list2")
-        v2_scale_window = keep.tile([P, T // 4], I32, name="v2_scale_window", align_bytes=ALIGN)
-        v_scale_window = keep.tile([P, T // 4], I32, name="v_scale_window", align_bytes=ALIGN)
-        wa_plane_raw = keep.tile([P, R // 4], I32, name="wa_plane_raw", align_bytes=ALIGN)
-        en_plane = keep.tile([P, N // 4], I32, name="en_plane", align_bytes=ALIGN)
-        v2_planes_early = [
-            keep.tile([P, (J - CHUNK) // 4], I32, name="v2_plane_early%d" % a, align_bytes=ALIGN) for a in range(V2_PASSES)
-        ]
-        v2_planes_late = [
-            keep.tile([P, CHUNK // 4], I32, name="v2_plane_late%d" % a, align_bytes=ALIGN) for a in range(V2_PASSES)
-        ]
-        v_plane_early = keep.tile([P, 2 * CHUNK // 4], I32, name="v_plane_early", align_bytes=ALIGN)
+        v2_scale_window = own("v2_scale_window", [P, T // 4], I32)
+        v_scale_window = own("v_scale_window", [P, T // 4], I32)
+        wa_plane_raw = own("wa_plane_raw", [P, R // 4], I32)
+        en_plane = own("en_plane", [P, N // 4], I32)
+        v2_plane_early = own("v2_plane_early", [P, V2_PASSES * V2_EARLY // 4], I32)
+        v2_planes_late = {c: own("v2_plane_late%d" % c, [P, V2_PASSES * CHUNK // 4], I32) for c in (2, 3)}
+        v_plane_early = own("v_plane_early", [P, V_EARLY // 4], I32)
         warm = keep.tile([P, 2], F32, name="warm")
         nc.gpsimd.memset(warm[:, 0:1], 0.0)
         nc.scalar.activation(warm[:, 1:2], warm[:, 0:1], ACT.Sigmoid)
-        nc.gpsimd.memset(v_scale_window[:], 0)
-        nc.vector.memset(wa_plane_raw[:], 0)
+        nc.gpsimd.memset(wa_plane_raw[:], 0)
         nc.vector.memset(v2_scale_window[0:V2_ROWS_AT, :], 0)
-        for plane in v2_planes_early + v2_planes_late + [v_plane_early]:
-            nc.vector.memset(plane[:], 0)
-        nc.gpsimd.memset(en_plane[:], 0)
+        nc.gpsimd.memset(v_scale_window[0:V_ROWS_AT, :], 0)
 
         def load_plane(plane, scales):
             for r in range(QUAD_ROWS):
                 nc.sync.dma_start(plane[r:P:QUAD, :], scales[0, r:BLOCKS:QUAD_ROWS, :].bitcast(I32))
 
-        nc.sync.dma_start(v2_scale_window[V2_ROWS_AT:P, :], tab2_scales.rearrange("a q t -> (a q) t").bitcast(I32))
+        nc.sync.dma_start(v2_scale_window[V2_ROWS_AT:P, :], tab2_scales.rearrange("a q t -> q a t").bitcast(I32))
         nc.sync.dma_start(list2[:], offs2)
-        wb_raw = {0: load_wb(0)}
+        nc.sync.dma_start(v_scale_window[V_ROWS_AT:P, :], tab_scales[0].bitcast(I32))
         nc.sync.dma_start(list1[:], offs)
-        nc.sync.dma_start(v_scale_window[V_ROWS_AT:P:V_ROW_STEP, :], tab_scales[0].bitcast(I32))
+        wb_raw = {0: load_wb(0)}
         load_plane(wa_plane_raw, wa_scales)
-        v2_window = keep.tile([P, T], I32, name="v2_window", align_bytes=ALIGN)
+        v2_window = own("v2_window", [P, T], I32)
         nc.sync.dma_start(v2_window[:], tab2_words[0].rearrange("p t i -> p (t i)").bitcast(I32))
-        wa_words_raw = keep.tile([P, R // 2], I32, name="wa_words_raw", align_bytes=ALIGN)
+        wa_words_raw = own("wa_words_raw", [P, R // 2], I32)
         nc.sync.dma_start(wa_words_raw[:], wa_words[0].bitcast(I32))
 
         def gather_bytes(rows, window, lst, j0, j1):
             nc.vector.tensor_copy(rows[:], window[:].bitcast(U8).indirect(offsets(lst, j0, j1)))
 
-        def move_rows(plane, rows, first, step):
-            for r in range(QUAD_ROWS):
-                source = rows[first + step * r : first + step * (BLOCKS - 1) + 1 : step * QUAD_ROWS, :]
-                nc.sync.dma_start(plane[r:P:QUAD, :], source.bitcast(I32))
+        def move_rows(plane, rows, first, passes):
+            for q in range(P // QUAD):
+                count = passes * QUAD_ROWS
+                source = rows[first + count * q : first + count * (q + 1), :]
+                nc.sync.dma_start(plane[QUAD * q : QUAD * q + QUAD_ROWS, :], source.bitcast(I32))
 
-        v2_rows_early = keep.tile([P, J - CHUNK], U8, name="v2_rows_early", align_bytes=ALIGN)
-        gather_bytes(v2_rows_early, v2_scale_window, list2, 0, J - CHUNK)
-        v_rows_early = place("v_rows_early", [P, 2 * CHUNK], U8, "v_rows_early")
-        gather_bytes(v_rows_early, v_scale_window, list1, 0, 2 * CHUNK)
+        v2_rows_early = own("v2_rows_early", [P, V2_EARLY], U8)
+        gather_bytes(v2_rows_early, v2_scale_window, list2, 0, V2_EARLY)
+        v_rows_early = own("v_rows_early", [P, V_EARLY], U8)
+        gather_bytes(v_rows_early, v_scale_window, list1, 0, V_EARLY)
 
-        v_window = keep.tile([P, T], I32, name="v_window", align_bytes=ALIGN)
-        move_rows(v2_planes_early[0], v2_rows_early, V2_ROWS_AT, 1)
+        v_window = own("v_window", [P, T], I32)
+        move_rows(v2_plane_early, v2_rows_early, V2_ROWS_AT, V2_PASSES)
         wb_raw[1] = load_wb(1)
-        move_rows(v2_planes_early[1], v2_rows_early, V2_ROWS_AT + BLOCKS, 1)
+        move_rows(v_plane_early, v_rows_early, V_ROWS_AT, 1)
         nc.sync.dma_start(v_window[:], tab_words[0].rearrange("p t i -> p (t i)").bitcast(I32))
-        move_rows(v_plane_early, v_rows_early, V_ROWS_AT, V_ROW_STEP)
         sm_slots = keep.tile([P, PACK], F32, name="sm_slots")
         nc.sync.dma_start(sm_slots[:], sm.rearrange("(p t) -> p t", t=PACK))
-        en_codes = keep.tile([P, N], I32, name="en_codes", align_bytes=ALIGN)
+        en_codes = own("en_codes", [P, N], I32)
         nc.sync.dma_start(en_codes[:], en_words[0].rearrange("p n i -> p (n i)").bitcast(I32))
-        load_plane(v_scale_window, tab_scales)
         load_plane(en_plane, en_scales)
 
         v_words = {}
@@ -155,12 +148,12 @@ def tile_list_kg_tanh_sig_kernel(
         v2_parted = {}
         v_planes = {}
 
-        def gather_words(words, window, lst, c):
-            nc.vector.tensor_copy(words[:], window[:].bitcast(U32).indirect(offsets(lst, CHUNK * c, CHUNK * (c + 1))))
+        def gather_words(words, window, lst, j0, j1):
+            nc.vector.tensor_copy(words[:], window[:].bitcast(U32).indirect(offsets(lst, j0, j1)))
 
-        def gather_v(c, words):
-            v_words[c] = words
-            gather_words(words, v_window, list1, c)
+        def gather_v(c, words, j0=0, width=CHUNK):
+            v_words[c, j0] = words
+            gather_words(words, v_window, list1, CHUNK * c + j0, CHUNK * c + j0 + width)
 
         def gather_v_plane(c, plane):
             v_planes[c] = plane[:]
@@ -168,7 +161,7 @@ def tile_list_kg_tanh_sig_kernel(
 
         def gather_v2(c, words):
             v2_words[c] = words
-            gather_words(words, v2_window, list2, c)
+            gather_words(words, v2_window, list2, CHUNK * c, CHUNK * (c + 1))
 
         def part_v2(c, parted):
             v2_parted[c] = parted
@@ -176,9 +169,6 @@ def tile_list_kg_tanh_sig_kernel(
                 parted[:].bitcast(U16).rearrange("p (a j) -> p a j", a=V2_PASSES),
                 v2_words[c][:].bitcast(U16).rearrange("p (j a) -> p a j", a=V2_PASSES),
             )
-
-        def own(name, shape, dtype):
-            return keep.tile(shape, dtype, name=name, align_bytes=ALIGN)
 
         wb_bf = [own("wb_bf0", [P, PACK, P, PACK], BF16), place("wb_bf1", [P, PACK, P, PACK], BF16, "wb_bf1")]
         wb_codes = [own("wb_codes%d" % a, [P, R], U32) for a in range(V2_PASSES)]
@@ -198,10 +188,11 @@ def tile_list_kg_tanh_sig_kernel(
         def v2_pass(c, a, t, j0, width, target, start, stop):
             cols = slice(P * t, P * (t + 1))
             at = CHUNK * a + j0
-            if c < CHUNKS - 1:
-                plane = v2_planes_early[a][:].bitcast(U8)[:, CHUNK * c + j0 : CHUNK * c + j0 + width]
+            if c not in v2_planes_late:
+                first = V2_EARLY * a + CHUNK * c + j0
+                plane = v2_plane_early[:].bitcast(U8)[:, first : first + width]
             else:
-                plane = v2_planes_late[a][:].bitcast(U8)[:, j0 : j0 + width]
+                plane = v2_planes_late[c][:].bitcast(U8)[:, at : at + width]
             nc.tensor.matmul_mx(
                 out=target,
                 lhsT=wb_codes[a][:, cols].bitcast(FP8X4),
@@ -213,11 +204,12 @@ def tile_list_kg_tanh_sig_kernel(
             )
 
         def v_pass(c, t, j0, width, target, start, stop):
+            piece = max(first for chunk, first in v_words if chunk == c and first <= j0)
             nc.tensor.matmul_mx(
                 out=target,
                 lhsT=wa_codes[:, 2 * P * t : 2 * P * (t + 1)].bitcast(FP4X4),
                 lhsT_scale=wa_plane[:, P * t : P * (t + 1)],
-                rhs=v_words[c][:, j0 : j0 + width].bitcast(FP8X4),
+                rhs=v_words[c, piece][:, j0 - piece : j0 - piece + width].bitcast(FP8X4),
                 rhs_scale=v_planes[c][:, j0 : j0 + width],
                 start=start,
                 stop=stop,
@@ -260,10 +252,7 @@ def tile_list_kg_tanh_sig_kernel(
         def scale_half(c):
             def scale(j0):
                 name = "h_bf%d_%d" % (c, j0)
-                if c == 1:
-                    h_bf = place(name, [P, HALF, PACK], BF16, "h_bf1", 2 * PACK * j0)
-                else:
-                    h_bf = own(name, [P, HALF, PACK], BF16)
+                h_bf = own(name, [P, HALF, PACK], BF16)
                 source = tanh_z[c][j0 // HALF][:] if c == CHUNKS - 1 else tanh_z[c][:, :, j0 : j0 + HALF]
                 factor = sm_slots[:].rearrange("p (g t i) -> p g t i", g=1, i=1).to_broadcast([P, HALF // RUN, PACK, RUN])
                 nc.vector.tensor_tensor(
@@ -313,19 +302,22 @@ def tile_list_kg_tanh_sig_kernel(
             wa_plane[:].rearrange("p (t m) -> p t m", t=PACK),
             wa_plane_raw[:].bitcast(U8).rearrange("p (m t) -> p t m", t=PACK),
         )
-        for c in range(2):
-            gather_v2(c, place("v2_words%d" % c, [P, CHUNK], U32, "v2_words%d" % c))
-            part_v2(c, own("v2_parted%d" % c, [P, WORDS], U8))
-            v_planes[c] = v_plane_early[:].bitcast(U8)[:, CHUNK * c : CHUNK * (c + 1)]
-        wa_codes = place("wa_codes", [P, 2 * R], U8, "v2_words0")
-        nc.vector.tensor_copy(
+        wa_codes = own("wa_codes", [P, 2 * R], U8)
+        nc.scalar.copy(
             wa_codes[:].bitcast(U16).rearrange("p (t m) -> p t m", t=PACK),
             wa_words_raw[:].bitcast(U16).rearrange("p (m t) -> p t m", t=PACK),
         )
-        v2_rows_late = place("v2_rows_late", [P, CHUNK], U8, "v2_words1")
-        gather_bytes(v2_rows_late, v2_scale_window, list2, J - CHUNK, J)
+        gather_v2(0, own("v2_words0", [P, CHUNK], U32))
+        gather_v2(1, place("v2_words1", [P, CHUNK], U32, "v2_words1"))
+        for c in range(2):
+            part_v2(c, own("v2_parted%d" % c, [P, WORDS], U8))
+        for c in range(V_EARLY // CHUNK):
+            v_planes[c] = v_plane_early[:].bitcast(U8)[:, CHUNK * c : CHUNK * (c + 1)]
+        v2_rows_late = {2: place("v2_rows_late2", [P, CHUNK], U8, "v2_words1")}
+        gather_bytes(v2_rows_late[2], v2_scale_window, list2, 2 * CHUNK, 3 * CHUNK)
         quantize_wb(1)
-        gather_v2(2, place("v2_words2", [P, CHUNK], U32, "wb_bf1"))
+        v2_rows_late[3] = place("v2_rows_late3", [P, CHUNK], U8, "wb_bf1")
+        gather_bytes(v2_rows_late[3], v2_scale_window, list2, 3 * CHUNK, 4 * CHUNK)
 
         z[0] = [next_bank([P, PACK, GROUP]) for b in range(PACK)]
         z[1] = [next_bank([P, CHUNK]) for t in range(PACK)]
@@ -340,9 +332,9 @@ def tile_list_kg_tanh_sig_kernel(
         for t in range(EARLY_SLOTS):
             v2_pass(1, 1, t, 0, CHUNK, z[1][t][:], False, False)
 
-        for c in range(2):
-            gather_v(c, own("v_words%d" % c, [P, CHUNK], U32))
-        part_v2(2, place("v2_parted2", [P, WORDS], U8, "v_rows_early"))
+        for j0 in range(0, CHUNK, HALF):
+            gather_v(0, own("v_words0_%d" % j0, [P, HALF], U32), j0, HALF)
+        gather_v(1, own("v_words1", [P, CHUNK], U32))
         tanh_z[0] = []
         for b in range(PACK):
             for t in range(PACK):
@@ -354,22 +346,24 @@ def tile_list_kg_tanh_sig_kernel(
             v_pass(1, t, 0, CHUNK, z[1][t][:], False, t < EARLY_SLOTS)
             if t >= EARLY_SLOTS:
                 v2_pass(1, 1, t, 0, CHUNK, z[1][t][:], False, True)
-        for a in range(V2_PASSES):
-            move_rows(v2_planes_late[a], v2_rows_late, V2_ROWS_AT + BLOCKS * a, 1)
-        make_h(0, GROUP, scale_group, place("h_codes0", [P, CHUNK], U32, "h_bf1", WORDS // 2))
+        for c in v2_planes_late:
+            move_rows(v2_planes_late[c], v2_rows_late[c], V2_ROWS_AT, V2_PASSES)
+        load_plane(v_scale_window, tab_scales)
+        make_h(0, GROUP, scale_group, own("h_codes0", [P, CHUNK], U32))
         tanh_slots(1, place("tanh1", [P, PACK, CHUNK], F32, "tanh1"))
 
         last_piece = 4 * CHUNK * (PACK - 1)
+        gather_v2(2, place("v2_words2", [P, CHUNK], U32, "tanh0", last_piece - WORDS // 2))
         gather_v(2, place("v_words2", [P, CHUNK], U32, "tanh0", last_piece + WORDS // 2))
-        gather_v_plane(2, place("v_plane2", [P, CHUNK], U8, "tanh0", last_piece))
+        part_v2(2, own("v2_parted2", [P, WORDS], U8))
         score_halves(0)
         score(0, range(PACK, N // P), next_banks(PACK))
         z[2] = [next_bank([P, CHUNK]) for t in range(PACK)]
         for t in range(PACK):
-            for a in range(V2_PASSES):
-                v2_pass(2, a, t, 0, CHUNK, z[2][t][:], a == 0, False)
+            v_pass(2, t, 0, CHUNK, z[2][t][:], True, False)
         for t in range(PACK):
-            v_pass(2, t, 0, CHUNK, z[2][t][:], False, True)
+            for a in range(V2_PASSES):
+                v2_pass(2, a, t, 0, CHUNK, z[2][t][:], False, a == V2_PASSES - 1)
         make_h(1, HALF, scale_half(1), own("h_codes1", [P, CHUNK], U32))
         tanh_slots(2, place("tanh2", [P, PACK, CHUNK], F32, "tanh2"))
 

@@ -33,7 +33,7 @@ V2_EARLY = 2 * CHUNK
 GROUP = CHUNK // PACK
 RUN = 2
 BANKS = 8
-EARLY_SLOTS = 0
+EARLY_SLOTS = 2
 ALIGN = 64
 WORDS = 4 * CHUNK
 
@@ -60,6 +60,7 @@ def tile_list_kg_tanh_sig_kernel(
 
         cell("v2_words1", WORDS)
         cell("wb_bf1", 8 * R)
+        cell("v_words0_0", WORDS)
         cell("tanh2", 4 * PACK * CHUNK)
         cell("tanh0", 4 * PACK * CHUNK + WORDS)
         cell("tanh1", 4 * PACK * CHUNK)
@@ -109,9 +110,9 @@ def tile_list_kg_tanh_sig_kernel(
 
         nc.sync.dma_start(v2_scale_window[V2_ROWS_AT:P, :], tab2_scales.rearrange("a q t -> q a t").bitcast(I32))
         nc.sync.dma_start(list2[:], offs2)
-        nc.sync.dma_start(v_scale_window[V_ROWS_AT:P, :], tab_scales[0].bitcast(I32))
-        nc.sync.dma_start(list1[:], offs)
         wb_raw = {0: load_wb(0)}
+        nc.sync.dma_start(list1[:], offs)
+        nc.sync.dma_start(v_scale_window[V_ROWS_AT:P, :], tab_scales[0].bitcast(I32))
         load_plane(wa_plane_raw, wa_scales)
         v2_window = own("v2_window", [P, T], I32)
         nc.sync.dma_start(v2_window[:], tab2_words[0].rearrange("p t i -> p (t i)").bitcast(I32))
@@ -135,8 +136,8 @@ def tile_list_kg_tanh_sig_kernel(
         v_window = own("v_window", [P, T], I32)
         move_rows(v2_plane_early, v2_rows_early, V2_ROWS_AT, V2_PASSES)
         wb_raw[1] = load_wb(1)
-        move_rows(v_plane_early, v_rows_early, V_ROWS_AT, 1)
         nc.sync.dma_start(v_window[:], tab_words[0].rearrange("p t i -> p (t i)").bitcast(I32))
+        move_rows(v_plane_early, v_rows_early, V_ROWS_AT, 1)
         sm_slots = keep.tile([P, PACK], F32, name="sm_slots")
         nc.sync.dma_start(sm_slots[:], sm.rearrange("(p t) -> p t", t=PACK))
         en_codes = own("en_codes", [P, N], I32)
@@ -332,9 +333,10 @@ def tile_list_kg_tanh_sig_kernel(
         for t in range(EARLY_SLOTS):
             v2_pass(1, 1, t, 0, CHUNK, z[1][t][:], False, False)
 
-        for j0 in range(0, CHUNK, HALF):
-            gather_v(0, own("v_words0_%d" % j0, [P, HALF], U32), j0, HALF)
+        gather_v(0, place("v_words0_0", [P, HALF], U32, "v_words0_0"), 0, HALF)
+        gather_v(0, own("v_words0_1", [P, HALF], U32), HALF, HALF)
         gather_v(1, own("v_words1", [P, CHUNK], U32))
+        gather_v2(2, place("v2_words2", [P, CHUNK], U32, "v_words0_0"))
         tanh_z[0] = []
         for b in range(PACK):
             for t in range(PACK):
@@ -353,9 +355,8 @@ def tile_list_kg_tanh_sig_kernel(
         tanh_slots(1, place("tanh1", [P, PACK, CHUNK], F32, "tanh1"))
 
         last_piece = 4 * CHUNK * (PACK - 1)
-        gather_v2(2, place("v2_words2", [P, CHUNK], U32, "tanh0", last_piece - WORDS // 2))
         gather_v(2, place("v_words2", [P, CHUNK], U32, "tanh0", last_piece + WORDS // 2))
-        part_v2(2, own("v2_parted2", [P, WORDS], U8))
+        part_v2(2, place("v2_parted2", [P, WORDS], U8, "tanh0", last_piece - WORDS // 2))
         score_halves(0)
         score(0, range(PACK, N // P), next_banks(PACK))
         z[2] = [next_bank([P, CHUNK]) for t in range(PACK)]

@@ -27,13 +27,14 @@ BLOCKS = 16
 QUAD = 32
 QUAD_ROWS = 4
 V2_ROWS_AT = P - V2_PASSES * BLOCKS
-V_ROWS_AT = P - BLOCKS
+V_ROWS_AT = QUAD + 1
+V_ROW_STEP = 4
 V_EARLY = 3 * CHUNK
 V2_EARLY = 2 * CHUNK
 GROUP = CHUNK // PACK
 RUN = 2
 BANKS = 8
-EARLY_SLOTS = 2
+EARLY_SLOTS = 1
 ALIGN = 64
 WORDS = 4 * CHUNK
 
@@ -60,7 +61,6 @@ def tile_list_kg_tanh_sig_kernel(
 
         cell("v2_words1", WORDS)
         cell("wb_bf1", 8 * R)
-        cell("v_words0_0", WORDS)
         cell("tanh2", 4 * PACK * CHUNK)
         cell("tanh0", 4 * PACK * CHUNK + WORDS)
         cell("tanh1", 4 * PACK * CHUNK)
@@ -94,15 +94,15 @@ def tile_list_kg_tanh_sig_kernel(
         v_scale_window = own("v_scale_window", [P, T // 4], I32)
         wa_plane_raw = own("wa_plane_raw", [P, R // 4], I32)
         en_plane = own("en_plane", [P, N // 4], I32)
-        v2_plane_early = own("v2_plane_early", [P, V2_PASSES * V2_EARLY // 4], I32)
+        v2_planes_early = [own("v2_plane_early%d" % a, [P, V2_EARLY // 4], I32) for a in range(V2_PASSES)]
         v2_planes_late = {c: own("v2_plane_late%d" % c, [P, V2_PASSES * CHUNK // 4], I32) for c in (2, 3)}
         v_plane_early = own("v_plane_early", [P, V_EARLY // 4], I32)
         warm = keep.tile([P, 2], F32, name="warm")
         nc.gpsimd.memset(warm[:, 0:1], 0.0)
         nc.scalar.activation(warm[:, 1:2], warm[:, 0:1], ACT.Sigmoid)
-        nc.gpsimd.memset(wa_plane_raw[:], 0)
+        nc.vector.memset(wa_plane_raw[:], 0)
         nc.vector.memset(v2_scale_window[0:V2_ROWS_AT, :], 0)
-        nc.gpsimd.memset(v_scale_window[0:V_ROWS_AT, :], 0)
+        nc.gpsimd.memset(v_scale_window[:], 0)
 
         def load_plane(plane, scales):
             for r in range(QUAD_ROWS):
@@ -112,7 +112,8 @@ def tile_list_kg_tanh_sig_kernel(
         nc.sync.dma_start(list2[:], offs2)
         wb_raw = {0: load_wb(0)}
         nc.sync.dma_start(list1[:], offs)
-        nc.sync.dma_start(v_scale_window[V_ROWS_AT:P, :], tab_scales[0].bitcast(I32))
+        v_rows = slice(V_ROWS_AT, V_ROWS_AT + V_ROW_STEP * (BLOCKS - 1) + 1, V_ROW_STEP)
+        nc.sync.dma_start(v_scale_window[v_rows, :], tab_scales[0].bitcast(I32))
         load_plane(wa_plane_raw, wa_scales)
         v2_window = own("v2_window", [P, T], I32)
         nc.sync.dma_start(v2_window[:], tab2_words[0].rearrange("p t i -> p (t i)").bitcast(I32))
@@ -122,10 +123,15 @@ def tile_list_kg_tanh_sig_kernel(
         def gather_bytes(rows, window, lst, j0, j1):
             nc.vector.tensor_copy(rows[:], window[:].bitcast(U8).indirect(offsets(lst, j0, j1)))
 
-        def move_rows(plane, rows, first, passes):
+        def move_rows(plane, rows, first, step):
+            for r in range(QUAD_ROWS):
+                source = rows[first + step * r : first + step * (BLOCKS - 1) + 1 : step * QUAD_ROWS, :]
+                nc.sync.dma_start(plane[r:P:QUAD, :], source.bitcast(I32))
+
+        def move_pairs(plane, rows):
+            count = V2_PASSES * QUAD_ROWS
             for q in range(P // QUAD):
-                count = passes * QUAD_ROWS
-                source = rows[first + count * q : first + count * (q + 1), :]
+                source = rows[V2_ROWS_AT + count * q : V2_ROWS_AT + count * (q + 1), :]
                 nc.sync.dma_start(plane[QUAD * q : QUAD * q + QUAD_ROWS, :], source.bitcast(I32))
 
         v2_rows_early = own("v2_rows_early", [P, V2_EARLY], U8)
@@ -134,10 +140,11 @@ def tile_list_kg_tanh_sig_kernel(
         gather_bytes(v_rows_early, v_scale_window, list1, 0, V_EARLY)
 
         v_window = own("v_window", [P, T], I32)
-        move_rows(v2_plane_early, v2_rows_early, V2_ROWS_AT, V2_PASSES)
+        move_rows(v2_planes_early[0], v2_rows_early, V2_ROWS_AT, V2_PASSES)
         wb_raw[1] = load_wb(1)
+        move_rows(v2_planes_early[1], v2_rows_early, V2_ROWS_AT + 1, V2_PASSES)
         nc.sync.dma_start(v_window[:], tab_words[0].rearrange("p t i -> p (t i)").bitcast(I32))
-        move_rows(v_plane_early, v_rows_early, V_ROWS_AT, 1)
+        move_rows(v_plane_early, v_rows_early, V_ROWS_AT, V_ROW_STEP)
         sm_slots = keep.tile([P, PACK], F32, name="sm_slots")
         nc.sync.dma_start(sm_slots[:], sm.rearrange("(p t) -> p t", t=PACK))
         en_codes = own("en_codes", [P, N], I32)
@@ -190,8 +197,7 @@ def tile_list_kg_tanh_sig_kernel(
             cols = slice(P * t, P * (t + 1))
             at = CHUNK * a + j0
             if c not in v2_planes_late:
-                first = V2_EARLY * a + CHUNK * c + j0
-                plane = v2_plane_early[:].bitcast(U8)[:, first : first + width]
+                plane = v2_planes_early[a][:].bitcast(U8)[:, CHUNK * c + j0 : CHUNK * c + j0 + width]
             else:
                 plane = v2_planes_late[c][:].bitcast(U8)[:, at : at + width]
             nc.tensor.matmul_mx(
@@ -333,10 +339,9 @@ def tile_list_kg_tanh_sig_kernel(
         for t in range(EARLY_SLOTS):
             v2_pass(1, 1, t, 0, CHUNK, z[1][t][:], False, False)
 
-        gather_v(0, place("v_words0_0", [P, HALF], U32, "v_words0_0"), 0, HALF)
+        gather_v(0, own("v_words0_0", [P, HALF], U32), 0, HALF)
         gather_v(0, own("v_words0_1", [P, HALF], U32), HALF, HALF)
         gather_v(1, own("v_words1", [P, CHUNK], U32))
-        gather_v2(2, place("v2_words2", [P, CHUNK], U32, "v_words0_0"))
         tanh_z[0] = []
         for b in range(PACK):
             for t in range(PACK):
@@ -349,14 +354,15 @@ def tile_list_kg_tanh_sig_kernel(
             if t >= EARLY_SLOTS:
                 v2_pass(1, 1, t, 0, CHUNK, z[1][t][:], False, True)
         for c in v2_planes_late:
-            move_rows(v2_planes_late[c], v2_rows_late[c], V2_ROWS_AT, V2_PASSES)
+            move_pairs(v2_planes_late[c], v2_rows_late[c])
         load_plane(v_scale_window, tab_scales)
         make_h(0, GROUP, scale_group, own("h_codes0", [P, CHUNK], U32))
         tanh_slots(1, place("tanh1", [P, PACK, CHUNK], F32, "tanh1"))
 
         last_piece = 4 * CHUNK * (PACK - 1)
+        gather_v2(2, place("v2_words2", [P, CHUNK], U32, "tanh0", last_piece - WORDS // 2))
         gather_v(2, place("v_words2", [P, CHUNK], U32, "tanh0", last_piece + WORDS // 2))
-        part_v2(2, place("v2_parted2", [P, WORDS], U8, "tanh0", last_piece - WORDS // 2))
+        part_v2(2, own("v2_parted2", [P, WORDS], U8))
         score_halves(0)
         score(0, range(PACK, N // P), next_banks(PACK))
         z[2] = [next_bank([P, CHUNK]) for t in range(PACK)]

@@ -96,7 +96,8 @@ def tile_list_kg_tanh_sig_kernel(
         en_plane = own("en_plane", [P, N // 4], I32)
         v2_planes_early = [own("v2_plane_early%d" % a, [P, V2_EARLY // 4], I32) for a in range(V2_PASSES)]
         v2_planes_late = {c: own("v2_plane_late%d" % c, [P, V2_PASSES * CHUNK // 4], I32) for c in (2, 3)}
-        v_plane_early = own("v_plane_early", [P, V_EARLY // 4], I32)
+        v_plane0 = own("v_plane0", [P, CHUNK // 4], I32)
+        v_plane_next = own("v_plane_next", [P, (V_EARLY - CHUNK) // 4], I32)
         warm = keep.tile([P, 2], F32, name="warm")
         nc.gpsimd.memset(warm[:, 0:1], 0.0)
         nc.scalar.activation(warm[:, 1:2], warm[:, 0:1], ACT.Sigmoid)
@@ -144,9 +145,10 @@ def tile_list_kg_tanh_sig_kernel(
         wb_raw[1] = load_wb(1)
         move_rows(v2_planes_early[1], v2_rows_early, V2_ROWS_AT + 1, V2_PASSES)
         nc.sync.dma_start(v_window[:], tab_words[0].rearrange("p t i -> p (t i)").bitcast(I32))
-        move_rows(v_plane_early, v_rows_early, V_ROWS_AT, V_ROW_STEP)
+        move_rows(v_plane0, v_rows_early[:, 0:CHUNK], V_ROWS_AT, V_ROW_STEP)
         sm_slots = keep.tile([P, PACK], F32, name="sm_slots")
         nc.sync.dma_start(sm_slots[:], sm.rearrange("(p t) -> p t", t=PACK))
+        move_rows(v_plane_next, v_rows_early[:, CHUNK:V_EARLY], V_ROWS_AT, V_ROW_STEP)
         en_codes = own("en_codes", [P, N], I32)
         nc.sync.dma_start(en_codes[:], en_words[0].rearrange("p n i -> p (n i)").bitcast(I32))
         load_plane(en_plane, en_scales)
@@ -318,8 +320,9 @@ def tile_list_kg_tanh_sig_kernel(
         gather_v2(1, place("v2_words1", [P, CHUNK], U32, "v2_words1"))
         for c in range(2):
             part_v2(c, own("v2_parted%d" % c, [P, WORDS], U8))
-        for c in range(V_EARLY // CHUNK):
-            v_planes[c] = v_plane_early[:].bitcast(U8)[:, CHUNK * c : CHUNK * (c + 1)]
+        v_planes[0] = v_plane0[:].bitcast(U8)
+        for c in range(1, V_EARLY // CHUNK):
+            v_planes[c] = v_plane_next[:].bitcast(U8)[:, CHUNK * (c - 1) : CHUNK * c]
         v2_rows_late = {2: place("v2_rows_late2", [P, CHUNK], U8, "v2_words1")}
         gather_bytes(v2_rows_late[2], v2_scale_window, list2, 2 * CHUNK, 3 * CHUNK)
         quantize_wb(1)

@@ -60,6 +60,7 @@ def tile_list_kg_tanh_sig_kernel(
             return arena.tile(shape, dtype, name=name, align_bytes=ALIGN, offset=cells[where] + skip)
 
         cell("v2_words1", WORDS)
+        cell("wb_bf0", 8 * R)
         cell("wb_bf1", 8 * R)
         cell("tanh2", 4 * PACK * CHUNK)
         cell("tanh0", 4 * PACK * CHUNK + WORDS)
@@ -96,7 +97,8 @@ def tile_list_kg_tanh_sig_kernel(
         en_plane = own("en_plane", [P, N // 4], I32)
         v2_planes_early = [own("v2_plane_early%d" % a, [P, V2_EARLY // 4], I32) for a in range(V2_PASSES)]
         v2_planes_late = {c: own("v2_plane_late%d" % c, [P, V2_PASSES * CHUNK // 4], I32) for c in (2, 3)}
-        v_plane0 = own("v_plane0", [P, CHUNK // 4], I32)
+        first_planes = own("first_planes", [P, (CHUNK + R) // 4], I32)
+        wa_plane = first_planes[:].bitcast(U8)[:, CHUNK:]
         v_plane_next = own("v_plane_next", [P, (V_EARLY - CHUNK) // 4], I32)
         warm = keep.tile([P, 2], F32, name="warm")
         nc.gpsimd.memset(warm[:, 0:1], 0.0)
@@ -115,7 +117,7 @@ def tile_list_kg_tanh_sig_kernel(
         nc.sync.dma_start(list1[:], offs)
         v_rows = slice(V_ROWS_AT, V_ROWS_AT + V_ROW_STEP * (BLOCKS - 1) + 1, V_ROW_STEP)
         nc.sync.dma_start(v_scale_window[v_rows, :], tab_scales[0].bitcast(I32))
-        load_plane(wa_plane_raw, wa_scales)
+        nc.sync.dma_start(wa_plane_raw[v_rows, :], wa_scales[0].bitcast(I32))
         v2_window = own("v2_window", [P, T], I32)
         nc.sync.dma_start(v2_window[:], tab2_words[0].rearrange("p t i -> p (t i)").bitcast(I32))
         wa_words_raw = own("wa_words_raw", [P, R // 2], I32)
@@ -145,13 +147,6 @@ def tile_list_kg_tanh_sig_kernel(
         wb_raw[1] = load_wb(1)
         move_rows(v2_planes_early[1], v2_rows_early, V2_ROWS_AT + 1, V2_PASSES)
         nc.sync.dma_start(v_window[:], tab_words[0].rearrange("p t i -> p (t i)").bitcast(I32))
-        move_rows(v_plane0, v_rows_early[:, 0:CHUNK], V_ROWS_AT, V_ROW_STEP)
-        sm_slots = keep.tile([P, PACK], F32, name="sm_slots")
-        nc.sync.dma_start(sm_slots[:], sm.rearrange("(p t) -> p t", t=PACK))
-        move_rows(v_plane_next, v_rows_early[:, CHUNK:V_EARLY], V_ROWS_AT, V_ROW_STEP)
-        en_codes = own("en_codes", [P, N], I32)
-        nc.sync.dma_start(en_codes[:], en_words[0].rearrange("p n i -> p (n i)").bitcast(I32))
-        load_plane(en_plane, en_scales)
 
         v_words = {}
         v2_words = {}
@@ -180,7 +175,7 @@ def tile_list_kg_tanh_sig_kernel(
                 v2_words[c][:].bitcast(U16).rearrange("p (j a) -> p a j", a=V2_PASSES),
             )
 
-        wb_bf = [own("wb_bf0", [P, PACK, P, PACK], BF16), place("wb_bf1", [P, PACK, P, PACK], BF16, "wb_bf1")]
+        wb_bf = [place("wb_bf0", [P, PACK, P, PACK], BF16, "wb_bf0"), place("wb_bf1", [P, PACK, P, PACK], BF16, "wb_bf1")]
         wb_codes = [own("wb_codes%d" % a, [P, R], U32) for a in range(V2_PASSES)]
         wb_plane = [own("wb_plane%d" % a, [P, R], U8) for a in range(V2_PASSES)]
 
@@ -306,11 +301,19 @@ def tile_list_kg_tanh_sig_kernel(
                 nc.sync.dma_start(out[P * b : P * (b + 1), CHUNK * c : CHUNK * (c + 1)], prob[:])
 
         quantize_wb(0)
-        wa_plane = own("wa_plane", [P, R], U8)
+        first_rows = place("first_rows", [P, CHUNK + R], U8, "wb_bf0")
         nc.vector.tensor_copy(
-            wa_plane[:].rearrange("p (t m) -> p t m", t=PACK),
+            first_rows[:, CHUNK:].rearrange("p (t m) -> p t m", t=PACK),
             wa_plane_raw[:].bitcast(U8).rearrange("p (m t) -> p t m", t=PACK),
         )
+        nc.vector.tensor_copy(first_rows[:, 0:CHUNK].bitcast(I32), v_rows_early[:, 0:CHUNK].bitcast(I32))
+        move_rows(first_planes, first_rows, V_ROWS_AT, V_ROW_STEP)
+        sm_slots = keep.tile([P, PACK], F32, name="sm_slots")
+        nc.sync.dma_start(sm_slots[:], sm.rearrange("(p t) -> p t", t=PACK))
+        move_rows(v_plane_next, v_rows_early[:, CHUNK:V_EARLY], V_ROWS_AT, V_ROW_STEP)
+        en_codes = own("en_codes", [P, N], I32)
+        nc.sync.dma_start(en_codes[:], en_words[0].rearrange("p n i -> p (n i)").bitcast(I32))
+        load_plane(en_plane, en_scales)
         wa_codes = own("wa_codes", [P, 2 * R], U8)
         nc.scalar.copy(
             wa_codes[:].bitcast(U16).rearrange("p (t m) -> p t m", t=PACK),
@@ -320,7 +323,7 @@ def tile_list_kg_tanh_sig_kernel(
         gather_v2(1, place("v2_words1", [P, CHUNK], U32, "v2_words1"))
         for c in range(2):
             part_v2(c, own("v2_parted%d" % c, [P, WORDS], U8))
-        v_planes[0] = v_plane0[:].bitcast(U8)
+        v_planes[0] = first_planes[:].bitcast(U8)[:, 0:CHUNK]
         for c in range(1, V_EARLY // CHUNK):
             v_planes[c] = v_plane_next[:].bitcast(U8)[:, CHUNK * (c - 1) : CHUNK * c]
         v2_rows_late = {2: place("v2_rows_late2", [P, CHUNK], U8, "v2_words1")}

@@ -247,17 +247,20 @@ def tile_list_kg_tanh_sig_kernel(
                 quantize(j0 - width)
             quantize(CHUNK - width)
 
-        def scale_group(j0):
-            h_bf = own("h_bf0_%d" % j0, [P, GROUP, PACK], BF16)
-            factor = sm_slots[:].rearrange("p (j t) -> p j t", j=1).to_broadcast([P, GROUP, PACK])
-            nc.vector.tensor_tensor(h_bf[:], tanh_z[0][j0 // GROUP][:], factor, MULT)
-            return h_bf
+        def scale_group(c):
+            def scale(j0):
+                h_bf = own("h_bf%d_%d" % (c, j0), [P, GROUP, PACK], BF16)
+                factor = sm_slots[:].rearrange("p (j t) -> p j t", j=1).to_broadcast([P, GROUP, PACK])
+                nc.vector.tensor_tensor(h_bf[:], tanh_z[c][j0 // GROUP][:], factor, MULT)
+                return h_bf
+
+            return scale
 
         def scale_half(c):
             def scale(j0):
                 name = "h_bf%d_%d" % (c, j0)
                 h_bf = own(name, [P, HALF, PACK], BF16)
-                source = tanh_z[c][j0 // HALF][:] if c == CHUNKS - 1 else tanh_z[c][:, :, j0 : j0 + HALF]
+                source = tanh_z[c][:, :, j0 : j0 + HALF]
                 factor = sm_slots[:].rearrange("p (g t i) -> p g t i", g=1, i=1).to_broadcast([P, HALF // RUN, PACK, RUN])
                 nc.vector.tensor_tensor(
                     h_bf[:].rearrange("p (g i) t -> p g t i", i=RUN),
@@ -362,7 +365,7 @@ def tile_list_kg_tanh_sig_kernel(
         for c in v2_planes_late:
             move_pairs(v2_planes_late[c], v2_rows_late[c])
         load_plane(v_scale_window, tab_scales)
-        make_h(0, GROUP, scale_group, own("h_codes0", [P, CHUNK], U32))
+        make_h(0, GROUP, scale_group(0), own("h_codes0", [P, CHUNK], U32))
         tanh_slots(1, place("tanh1", [P, PACK, CHUNK], F32, "tanh1"))
 
         last_piece = 4 * CHUNK * (PACK - 1)
@@ -382,31 +385,32 @@ def tile_list_kg_tanh_sig_kernel(
 
         gather_v2(3, place("v2_words3", [P, CHUNK], U32, "tanh1"))
         part_v2(3, own("v2_parted3", [P, WORDS], U8))
+        gather_v(3, place("v_words3_0", [P, HALF], U32, "tanh1", WORDS), 0, HALF)
         score(1, range(N // P), next_banks(BANKS))
         make_h(2, HALF, scale_half(2), own("h_codes2", [P, CHUNK], U32))
-        gather_v(3, place("v_words3", [P, CHUNK], U32, "tanh2"))
         gather_v_plane(3, place("v_plane3", [P, CHUNK], U8, "tanh2", WORDS))
+        gather_v(3, place("v_words3_1", [P, HALF], U32, "tanh2"), HALF, HALF)
         emptied = next_banks(BANKS)
         z_banks = emptied[:2] + emptied[-2:]
         score_banks = emptied[2:-2]
         z[3] = {}
 
         def open_last(b):
-            z[3][b] = bank(z_banks[b], [P, 2, HALF])
+            z[3][b] = bank(z_banks[b], [P, PACK, GROUP])
             for a in range(V2_PASSES):
-                for e in range(2):
-                    v2_pass(3, a, 2 * (b % 2) + e, HALF * (b // 2), HALF, z[3][b][:, e, :], a == 0 and e == 0, False)
+                for t in range(PACK):
+                    v2_pass(3, a, t, GROUP * b, GROUP, z[3][b][:, t, :], a == 0 and t == 0, False)
 
         for b in range(2):
             open_last(b)
         score(2, range(PACK), score_banks)
         for b in range(2, PACK):
             open_last(b)
-        tanh_z[3] = [own("tanh3_%d" % half, [P, PACK, HALF], F32) for half in range(2)]
+        tanh_z[3] = [own("tanh3_%d" % b, [P, GROUP, PACK], F32) for b in range(PACK)]
         for b in range(PACK):
-            for e in range(2):
-                v_pass(3, 2 * (b % 2) + e, HALF * (b // 2), HALF, z[3][b][:, e, :], False, e == 1)
-            nc.scalar.activation(tanh_z[3][b // 2][:, 2 * (b % 2) : 2 * (b % 2) + 2, :], z[3][b][:], ACT.Tanh)
+            for t in range(PACK):
+                v_pass(3, t, GROUP * b, GROUP, z[3][b][:, t, :], False, t == PACK - 1)
+            nc.scalar.activation(tanh_z[3][b][:], z[3][b][:].rearrange("p t j -> p j t"), ACT.Tanh)
         score(2, range(PACK, N // P), z_banks)
-        make_h(3, HALF, scale_half(3), own("h_codes3", [P, CHUNK], U32))
+        make_h(3, GROUP, scale_group(3), own("h_codes3", [P, CHUNK], U32))
         score(3, range(N // P), score_banks + z_banks)

@@ -250,8 +250,13 @@ def tile_list_kg_tanh_sig_kernel(
         def scale_group(c):
             def scale(j0):
                 h_bf = own("h_bf%d_%d" % (c, j0), [P, GROUP, PACK], BF16)
-                factor = sm_slots[:].rearrange("p (j t) -> p j t", j=1).to_broadcast([P, GROUP, PACK])
-                nc.vector.tensor_tensor(h_bf[:], tanh_z[c][j0 // GROUP][:], factor, MULT)
+                factor = sm_slots[:].rearrange("p (g t i) -> p g t i", g=1, i=1).to_broadcast([P, GROUP // RUN, PACK, RUN])
+                nc.vector.tensor_tensor(
+                    h_bf[:].rearrange("p (g i) t -> p g t i", i=RUN),
+                    tanh_z[c][j0 // GROUP][:].rearrange("p t (g i) -> p g t i", i=RUN),
+                    factor,
+                    MULT,
+                )
                 return h_bf
 
             return scale
@@ -355,8 +360,8 @@ def tile_list_kg_tanh_sig_kernel(
         for b in range(PACK):
             for t in range(PACK):
                 v_pass(0, t, GROUP * b, GROUP, z[0][b][:, t, :], False, t == PACK - 1)
-            piece = place("tanh0_%d" % b, [P, GROUP, PACK], F32, "tanh0", 4 * CHUNK * b)
-            nc.scalar.activation(piece[:], z[0][b][:].rearrange("p t j -> p j t"), ACT.Tanh)
+            piece = place("tanh0_%d" % b, [P, PACK, GROUP], F32, "tanh0", 4 * CHUNK * b)
+            nc.scalar.activation(piece[:], z[0][b][:], ACT.Tanh)
             tanh_z[0].append(piece)
         for t in range(PACK):
             v_pass(1, t, 0, CHUNK, z[1][t][:], False, t < EARLY_SLOTS)
@@ -406,11 +411,11 @@ def tile_list_kg_tanh_sig_kernel(
         score(2, range(PACK), score_banks)
         for b in range(2, PACK):
             open_last(b)
-        tanh_z[3] = [own("tanh3_%d" % b, [P, GROUP, PACK], F32) for b in range(PACK)]
+        tanh_z[3] = [own("tanh3_%d" % b, [P, PACK, GROUP], F32) for b in range(PACK)]
         for b in range(PACK):
             for t in range(PACK):
                 v_pass(3, t, GROUP * b, GROUP, z[3][b][:, t, :], False, t == PACK - 1)
-            nc.scalar.activation(tanh_z[3][b][:], z[3][b][:].rearrange("p t j -> p j t"), ACT.Tanh)
+            nc.scalar.activation(tanh_z[3][b][:], z[3][b][:], ACT.Tanh)
         score(2, range(PACK, N // P), z_banks)
         make_h(3, GROUP, scale_group(3), own("h_codes3", [P, CHUNK], U32))
         score(3, range(N // P), score_banks + z_banks)

@@ -59,6 +59,7 @@ def tile_list_kg_tanh_sig_kernel(
         def place(name, shape, dtype, where, skip=0):
             return arena.tile(shape, dtype, name=name, align_bytes=ALIGN, offset=cells[where] + skip)
 
+        cell("v_scale_window", T)
         cell("v2_words1", WORDS)
         cell("wb_bf0", 8 * R)
         cell("wb_bf1", 8 * R)
@@ -92,7 +93,7 @@ def tile_list_kg_tanh_sig_kernel(
         list1 = keep.tile([P, J // 16], U16, name="list1")
         list2 = keep.tile([P, J // 16], U16, name="list2")
         v2_scale_window = own("v2_scale_window", [P, T // 4], I32)
-        v_scale_window = own("v_scale_window", [P, T // 4], I32)
+        v_scale_window = place("v_scale_window", [P, T // 4], I32, "v_scale_window")
         wa_plane_raw = own("wa_plane_raw", [P, R // 4], I32)
         en_plane = own("en_plane", [P, N // 4], I32)
         v2_planes_early = [own("v2_plane_early%d" % a, [P, V2_EARLY // 4], I32) for a in range(V2_PASSES)]
@@ -300,10 +301,12 @@ def tile_list_kg_tanh_sig_kernel(
                     rows = out[2 * P * g : 2 * P * (g + 1), CHUNK * c + HALF * half : CHUNK * c + HALF * (half + 1)]
                     nc.sync.dma_start(rows.rearrange("(e p) j -> p e j", p=P), prob[:])
 
-        def score(c, blocks, banks):
+        def score(c, blocks, banks, piece=CHUNK):
             for b, where in zip(blocks, banks):
                 y = bank(where, [P, CHUNK])
-                score_pass(c, b, 0, CHUNK, y[:])
+                width = piece if b == 0 else CHUNK
+                for j0 in range(0, CHUNK, width):
+                    score_pass(c, b, j0, width, y[:, j0 : j0 + width])
                 prob = stage.tile([P, CHUNK], F32, name="prob")
                 nc.scalar.activation(prob[:], y[:], ACT.Sigmoid)
                 nc.sync.dma_start(out[P * b : P * (b + 1), CHUNK * c : CHUNK * (c + 1)], prob[:])
@@ -390,11 +393,11 @@ def tile_list_kg_tanh_sig_kernel(
 
         gather_v2(3, place("v2_words3", [P, CHUNK], U32, "tanh1"))
         part_v2(3, own("v2_parted3", [P, WORDS], U8))
-        gather_v(3, place("v_words3_0", [P, HALF], U32, "tanh1", WORDS), 0, HALF)
         score(1, range(N // P), next_banks(BANKS))
         make_h(2, HALF, scale_half(2), own("h_codes2", [P, CHUNK], U32))
         gather_v_plane(3, place("v_plane3", [P, CHUNK], U8, "tanh2", WORDS))
-        gather_v(3, place("v_words3_1", [P, HALF], U32, "tanh2"), HALF, HALF)
+        for half in range(2):
+            gather_v(3, place("v_words3_%d" % half, [P, HALF], U32, "v_scale_window", half * WORDS // 2), HALF * half, HALF)
         emptied = next_banks(BANKS)
         z_banks = emptied[:2] + emptied[-2:]
         score_banks = emptied[2:-2]
@@ -408,14 +411,15 @@ def tile_list_kg_tanh_sig_kernel(
 
         for b in range(2):
             open_last(b)
-        score(2, range(PACK), score_banks)
-        for b in range(2, PACK):
-            open_last(b)
+        score(2, range(PACK), score_banks, HALF)
+        open_last(2)
         tanh_z[3] = [own("tanh3_%d" % b, [P, PACK, GROUP], F32) for b in range(PACK)]
         for b in range(PACK):
+            if b == 2:
+                open_last(3)
             for t in range(PACK):
                 v_pass(3, t, GROUP * b, GROUP, z[3][b][:, t, :], False, t == PACK - 1)
             nc.scalar.activation(tanh_z[3][b][:], z[3][b][:], ACT.Tanh)
         score(2, range(PACK, N // P), z_banks)
         make_h(3, GROUP, scale_group(3), own("h_codes3", [P, CHUNK], U32))
-        score(3, range(N // P), score_banks + z_banks)
+        score(3, range(N // P), score_banks + z_banks, GROUP)

@@ -311,6 +311,14 @@ def tile_list_kg_tanh_sig_kernel(
                 nc.scalar.activation(prob[:], y[:], ACT.Sigmoid)
                 nc.sync.dma_start(out[P * b : P * (b + 1), CHUNK * c : CHUNK * (c + 1)], prob[:])
 
+        def score_in_halves(c, b, where):
+            y = bank(where, [P, CHUNK])
+            score_pass(c, b, 0, CHUNK, y[:])
+            for j0 in range(0, CHUNK, HALF):
+                prob = own("prob_half%d" % j0, [P, HALF], F32)
+                nc.scalar.activation(prob[:], y[:, j0 : j0 + HALF], ACT.Sigmoid)
+                nc.sync.dma_start(out[P * b : P * (b + 1), CHUNK * c + j0 : CHUNK * c + j0 + HALF], prob[:])
+
         quantize_wb(0)
         first_rows = place("first_rows", [P, CHUNK + R], U8, "wb_bf0")
         nc.vector.tensor_copy(
@@ -417,9 +425,12 @@ def tile_list_kg_tanh_sig_kernel(
         for b in range(PACK):
             if b == 2:
                 open_last(3)
+            if b == 3:
+                score(2, [PACK], z_banks[:1])
             for t in range(PACK):
                 v_pass(3, t, GROUP * b, GROUP, z[3][b][:, t, :], False, t == PACK - 1)
             nc.scalar.activation(tanh_z[3][b][:], z[3][b][:], ACT.Tanh)
-        score(2, range(PACK, N // P), z_banks)
+        score_in_halves(2, PACK + 1, z_banks[1])
+        score(2, range(PACK + 2, N // P), z_banks[2:])
         make_h(3, GROUP, scale_group(3), own("h_codes3", [P, CHUNK], U32))
         score(3, range(N // P), score_banks + z_banks, GROUP)

from contextlib import ExitStack

import concourse.mybir as mybir

K, L, R, N, T, J = 512, 1024, 512, 1024, 4096, 2048
FLOPS = 2 * J * (K * R + L * R + R * N)

F32 = mybir.dt.float32
BF16 = mybir.dt.bfloat16
I32 = mybir.dt.int32
U32 = mybir.dt.uint32
U16 = mybir.dt.uint16
U8 = mybir.dt.uint8
FP8X4 = mybir.dt.float8_e4m3fn_x4
FP4X4 = mybir.dt.float4_e2m1fn_x4
ACT = mybir.ActivationFunctionType
MULT = mybir.AluOpType.mult

P = 128
PACK = 4
K_PASS = P * PACK
V2_PASSES = L // K_PASS
CHUNK = 512
CHUNKS = J // CHUNK
HALF = CHUNK // 2
BLOCKS = 16
QUAD = 32
QUAD_ROWS = 4
V2_ROWS_AT = P - V2_PASSES * BLOCKS
V_ROWS_AT = QUAD + 1
V_ROW_STEP = 4
V_EARLY = 3 * CHUNK
V2_EARLY = 2 * CHUNK
GROUP = CHUNK // PACK
RUN = 2
BANKS = 8
EARLY_SLOTS = 1
ALIGN = 64
WORDS = 4 * CHUNK


def tile_list_kg_tanh_sig_kernel(
    tc, tab_words, tab_scales, tab2_words, tab2_scales, wa_words, wa_scales, wb, sm, en_words, en_scales, offs, offs2, out
):
    nc = tc.nc
    with ExitStack() as ctx:
        keep = ctx.enter_context(tc.tile_pool(name="keep", bufs=1))
        arena = ctx.enter_context(tc.tile_pool(name="arena", bufs=1))
        stage = ctx.enter_context(tc.tile_pool(name="stage", bufs=CHUNKS * N // P))
        psum = ctx.enter_context(tc.psum_pool(name="psum", bufs=1))

        cells = {}
        free = [0]

        def cell(name, size):
            cells[name] = free[0]
            free[0] = free[0] + size

        def place(name, shape, dtype, where, skip=0):
            return arena.tile(shape, dtype, name=name, align_bytes=ALIGN, offset=cells[where] + skip)

        cell("v_scale_window", T)
        cell("v2_words1", WORDS)
        cell("wb_bf0", 8 * R)
        cell("wb_bf1", 8 * R)
        cell("tanh2", 4 * PACK * CHUNK)
        cell("tanh0", 4 * PACK * CHUNK + WORDS)
        cell("tanh1", 4 * PACK * CHUNK)

        fills = [0]

        def bank(b, shape):
            return psum.tile(shape, F32, name="bank%d" % b)

        def next_banks(count):
            fills[0] = fills[0] + count
            return [b % BANKS for b in range(fills[0] - count, fills[0])]

        def next_bank(shape):
            return bank(next_banks(1)[0], shape)

        def offsets(lst, j0, j1):
            return lst[:, j0 // 16 : j1 // 16]

        def load_wb(a):
            raw = keep.tile([P, PACK, R], F32, name="wb_raw%d" % a)
            nc.sync.dma_start(raw[:], wb[K_PASS * a : K_PASS * (a + 1), :].rearrange("(p i) r -> p i r", i=PACK))
            return raw

        def own(name, shape, dtype):
            return keep.tile(shape, dtype, name=name, align_bytes=ALIGN)

        list1 = keep.tile([P, J // 16], U16, name="list1")
        list2 = keep.tile([P, J // 16], U16, name="list2")
        v2_scale_window = own("v2_scale_window", [P, T // 4], I32)
        v_scale_window = place("v_scale_window", [P, T // 4], I32, "v_scale_window")
        wa_plane_raw = own("wa_plane_raw", [P, R // 4], I32)
        en_plane = own("en_plane", [P, N // 4], I32)
        v2_planes_early = [own("v2_plane_early%d" % a, [P, V2_EARLY // 4], I32) for a in range(V2_PASSES)]
        v2_planes_late = {c: own("v2_plane_late%d" % c, [P, V2_PASSES * CHUNK // 4], I32) for c in (2, 3)}
        first_planes = own("first_planes", [P, (CHUNK + R) // 4], I32)
        wa_plane = first_planes[:].bitcast(U8)[:, CHUNK:]
        v_plane_next = own("v_plane_next", [P, (V_EARLY - CHUNK) // 4], I32)
        warm = keep.tile([P, 2], F32, name="warm")
        nc.gpsimd.memset(warm[:, 0:1], 0.0)
        nc.scalar.activation(warm[:, 1:2], warm[:, 0:1], ACT.Sigmoid)
        nc.vector.memset(wa_plane_raw[:], 0)
        nc.vector.memset(v2_scale_window[0:V2_ROWS_AT, :], 0)
        nc.gpsimd.memset(v_scale_window[:], 0)

        def load_plane(plane, scales):
            for r in range(QUAD_ROWS):
                nc.sync.dma_start(plane[r:P:QUAD, :], scales[0, r:BLOCKS:QUAD_ROWS, :].bitcast(I32))

        nc.sync.dma_start(v2_scale_window[V2_ROWS_AT:P, :], tab2_scales.rearrange("a q t -> q a t").bitcast(I32))
        nc.sync.dma_start(list2[:], offs2)
        wb_raw = {0: load_wb(0)}
        nc.sync.dma_start(list1[:], offs)
        v_rows = slice(V_ROWS_AT, V_ROWS_AT + V_ROW_STEP * (BLOCKS - 1) + 1, V_ROW_STEP)
        nc.sync.dma_start(v_scale_window[v_rows, :], tab_scales[0].bitcast(I32))
        nc.sync.dma_start(wa_plane_raw[v_rows, :], wa_scales[0].bitcast(I32))
        v2_window = own("v2_window", [P, T], I32)
        nc.sync.dma_start(v2_window[:], tab2_words[0].rearrange("p t i -> p (t i)").bitcast(I32))
        wa_words_raw = own("wa_words_raw", [P, R // 2], I32)
        nc.sync.dma_start(wa_words_raw[:], wa_words[0].bitcast(I32))

        def gather_bytes(rows, window, lst, j0, j1):
            nc.vector.tensor_copy(rows[:], window[:].bitcast(U8).indirect(offsets(lst, j0, j1)))

        def move_rows(plane, rows, first, step):
            for r in range(QUAD_ROWS):
                source = rows[first + step * r : first + step * (BLOCKS - 1) + 1 : step * QUAD_ROWS, :]
                nc.sync.dma_start(plane[r:P:QUAD, :], source.bitcast(I32))

        def move_pairs(plane, rows):
            count = V2_PASSES * QUAD_ROWS
            for q in range(P // QUAD):
                source = rows[V2_ROWS_AT + count * q : V2_ROWS_AT + count * (q + 1), :]
                nc.sync.dma_start(plane[QUAD * q : QUAD * q + QUAD_ROWS, :], source.bitcast(I32))

        v2_rows_early = own("v2_rows_early", [P, V2_EARLY], U8)
        gather_bytes(v2_rows_early, v2_scale_window, list2, 0, V2_EARLY)
        v_rows_early = own("v_rows_early", [P, V_EARLY], U8)
        gather_bytes(v_rows_early, v_scale_window, list1, 0, V_EARLY)

        v_window = own("v_window", [P, T], I32)
        move_rows(v2_planes_early[0], v2_rows_early, V2_ROWS_AT, V2_PASSES)
        wb_raw[1] = load_wb(1)
        move_rows(v2_planes_early[1], v2_rows_early, V2_ROWS_AT + 1, V2_PASSES)
        nc.sync.dma_start(v_window[:], tab_words[0].rearrange("p t i -> p (t i)").bitcast(I32))

        v_words = {}
        v2_words = {}
        v2_parted = {}
        v_planes = {}

        def gather_words(words, window, lst, j0, j1):
            nc.vector.tensor_copy(words[:], window[:].bitcast(U32).indirect(offsets(lst, j0, j1)))

        def gather_v(c, words, j0=0, width=CHUNK):
            v_words[c, j0] = words
            gather_words(words, v_window, list1, CHUNK * c + j0, CHUNK * c + j0 + width)

        def gather_v_plane(c, plane):
            v_planes[c] = plane[:]
            gather_bytes(plane, v_scale_window, list1, CHUNK * c, CHUNK * (c + 1))

        def gather_v2(c, words):
            v2_words[c] = words
            gather_words(words, v2_window, list2, CHUNK * c, CHUNK * (c + 1))

        def part_v2(c, parted):
            v2_parted[c] = parted
            nc.vector.tensor_copy(
                parted[:].bitcast(U16).rearrange("p (a j) -> p a j", a=V2_PASSES),
                v2_words[c][:].bitcast(U16).rearrange("p (j a) -> p a j", a=V2_PASSES),
            )

        wb_bf = [place("wb_bf0", [P, PACK, P, PACK], BF16, "wb_bf0"), place("wb_bf1", [P, PACK, P, PACK], BF16, "wb_bf1")]
        wb_codes = [own("wb_codes%d" % a, [P, R], U32) for a in range(V2_PASSES)]
        wb_plane = [own("wb_plane%d" % a, [P, R], U8) for a in range(V2_PASSES)]

        def quantize_wb(a):
            nc.scalar.copy(
                wb_bf[a][:].rearrange("p (u e) m i -> p u m i e", e=2),
                wb_raw[a][:].rearrange("p i (m u e) -> p u m i e", u=2, e=2),
            )
            nc.vector.quantize_mx(
                out=wb_codes[a][:].bitcast(FP8X4),
                scales=wb_plane[a][:],
                in_=wb_bf[a][:].rearrange("p t m i -> p (t m i)"),
            )

        def v2_pass(c, a, t, j0, width, target, start, stop):
            cols = slice(P * t, P * (t + 1))
            at = CHUNK * a + j0
            if c not in v2_planes_late:
                plane = v2_planes_early[a][:].bitcast(U8)[:, CHUNK * c + j0 : CHUNK * c + j0 + width]
            else:
                plane = v2_planes_late[c][:].bitcast(U8)[:, at : at + width]
            nc.tensor.matmul_mx(
                out=target,
                lhsT=wb_codes[a][:, cols].bitcast(FP8X4),
                lhsT_scale=wb_plane[a][:, cols],
                rhs=v2_parted[c][:, 2 * at : 2 * (at + width)].bitcast(FP4X4),
                rhs_scale=plane,
                start=start,
                stop=stop,
            )

        def v_pass(c, t, j0, width, target, start, stop):
            piece = max(first for chunk, first in v_words if chunk == c and first <= j0)
            nc.tensor.matmul_mx(
                out=target,
                lhsT=wa_codes[:, 2 * P * t : 2 * P * (t + 1)].bitcast(FP4X4),
                lhsT_scale=wa_plane[:, P * t : P * (t + 1)],
                rhs=v_words[c, piece][:, j0 - piece : j0 - piece + width].bitcast(FP8X4),
                rhs_scale=v_planes[c][:, j0 : j0 + width],
                start=start,
                stop=stop,
            )

        z = {}
        tanh_z = {}
        h_codes = {}
        h_plane = {}

        def tanh_slots(c, tile):
            tanh_z[c] = tile
            for t in range(PACK):
                nc.scalar.activation(tile[:, t, :], z[c][t][:], ACT.Tanh)

        def make_h(c, width, scale, codes):
            h_codes[c] = codes
            h_plane[c] = own("h_plane%d" % c, [P, CHUNK], U8)
            h_bf = {}

            def quantize(j0):
                nc.vector.quantize_mx(
                    out=h_codes[c][:, j0 : j0 + width].bitcast(FP8X4),
                    scales=h_plane[c][:, j0 : j0 + width],
                    in_=h_bf[j0][:].rearrange("p j t -> p (j t)"),
                )

            h_bf[0] = scale(0)
            for j0 in range(width, CHUNK, width):
                h_bf[j0] = scale(j0)
                quantize(j0 - width)
            quantize(CHUNK - width)

        def scale_group(c):
            def scale(j0):
                h_bf = own("h_bf%d_%d" % (c, j0), [P, GROUP, PACK], BF16)
                factor = sm_slots[:].rearrange("p (g t i) -> p g t i", g=1, i=1).to_broadcast([P, GROUP // RUN, PACK, RUN])
                nc.vector.tensor_tensor(
                    h_bf[:].rearrange("p (g i) t -> p g t i", i=RUN),
                    tanh_z[c][j0 // GROUP][:].rearrange("p t (g i) -> p g t i", i=RUN),
                    factor,
                    MULT,
                )
                return h_bf

            return scale

        def scale_half(c):
            def scale(j0):
                name = "h_bf%d_%d" % (c, j0)
                h_bf = own(name, [P, HALF, PACK], BF16)
                source = tanh_z[c][:, :, j0 : j0 + HALF]
                factor = sm_slots[:].rearrange("p (g t i) -> p g t i", g=1, i=1).to_broadcast([P, HALF // RUN, PACK, RUN])
                nc.vector.tensor_tensor(
                    h_bf[:].rearrange("p (g i) t -> p g t i", i=RUN),
                    source.rearrange("p t (g i) -> p g t i", i=RUN),
                    factor,
                    MULT,
                )
                return h_bf

            return scale

        def score_pass(c, b, j0, width, target):
            cols = slice(P * b, P * (b + 1))
            nc.tensor.matmul_mx(
                out=target,
                lhsT=en_codes[:, cols].bitcast(FP8X4),
                lhsT_scale=en_plane[:].bitcast(U8)[:, cols],
                rhs=h_codes[c][:, j0 : j0 + width].bitcast(FP8X4),
                rhs_scale=h_plane[c][:, j0 : j0 + width],
                start=True,
                stop=True,
            )

        def score_halves(c):
            for half in range(2):
                for g in range(2):
                    y = next_bank([P, 2, HALF])
                    for e in range(2):
                        score_pass(c, 2 * g + e, HALF * half, HALF, y[:, e, :])
                    prob = stage.tile([P, 2, HALF], F32, name="prob")
                    nc.scalar.activation(prob[:], y[:], ACT.Sigmoid)
                    rows = out[2 * P * g : 2 * P * (g + 1), CHUNK * c + HALF * half : CHUNK * c + HALF * (half + 1)]
                    nc.sync.dma_start(rows.rearrange("(e p) j -> p e j", p=P), prob[:])

        def score(c, blocks, banks, piece=CHUNK):
            for b, where in zip(blocks, banks):
                y = bank(where, [P, CHUNK])
                width = piece if b == 0 else CHUNK
                for j0 in range(0, CHUNK, width):
                    score_pass(c, b, j0, width, y[:, j0 : j0 + width])
                prob = stage.tile([P, CHUNK], F32, name="prob")
                nc.scalar.activation(prob[:], y[:], ACT.Sigmoid)
                nc.sync.dma_start(out[P * b : P * (b + 1), CHUNK * c : CHUNK * (c + 1)], prob[:])

        def score_in_halves(c, b, where):
            y = bank(where, [P, CHUNK])
            score_pass(c, b, 0, CHUNK, y[:])
            for j0 in range(0, CHUNK, HALF):
                prob = own("prob_half%d" % j0, [P, HALF], F32)
                nc.scalar.activation(prob[:], y[:, j0 : j0 + HALF], ACT.Sigmoid)
                nc.sync.dma_start(out[P * b : P * (b + 1), CHUNK * c + j0 : CHUNK * c + j0 + HALF], prob[:])

        quantize_wb(0)
        first_rows = place("first_rows", [P, CHUNK + R], U8, "wb_bf0")
        nc.vector.tensor_copy(
            first_rows[:, CHUNK:].rearrange("p (t m) -> p t m", t=PACK),
            wa_plane_raw[:].bitcast(U8).rearrange("p (m t) -> p t m", t=PACK),
        )
        nc.vector.tensor_copy(first_rows[:, 0:CHUNK].bitcast(I32), v_rows_early[:, 0:CHUNK].bitcast(I32))
        move_rows(first_planes, first_rows, V_ROWS_AT, V_ROW_STEP)
        sm_slots = keep.tile([P, PACK], F32, name="sm_slots")
        nc.sync.dma_start(sm_slots[:], sm.rearrange("(p t) -> p t", t=PACK))
        move_rows(v_plane_next, v_rows_early[:, CHUNK:V_EARLY], V_ROWS_AT, V_ROW_STEP)
        en_codes = own("en_codes", [P, N], I32)
        nc.sync.dma_start(en_codes[:], en_words[0].rearrange("p n i -> p (n i)").bitcast(I32))
        load_plane(en_plane, en_scales)
        wa_codes = own("wa_codes", [P, 2 * R], U8)
        nc.scalar.copy(
            wa_codes[:].bitcast(U16).rearrange("p (t m) -> p t m", t=PACK),
            wa_words_raw[:].bitcast(U16).rearrange("p (m t) -> p t m", t=PACK),
        )
        gather_v2(0, own("v2_words0", [P, CHUNK], U32))
        gather_v2(1, place("v2_words1", [P, CHUNK], U32, "v2_words1"))
        for c in range(2):
            part_v2(c, own("v2_parted%d" % c, [P, WORDS], U8))
        v_planes[0] = first_planes[:].bitcast(U8)[:, 0:CHUNK]
        for c in range(1, V_EARLY // CHUNK):
            v_planes[c] = v_plane_next[:].bitcast(U8)[:, CHUNK * (c - 1) : CHUNK * c]
        v2_rows_late = {2: place("v2_rows_late2", [P, CHUNK], U8, "v2_words1")}
        gather_bytes(v2_rows_late[2], v2_scale_window, list2, 2 * CHUNK, 3 * CHUNK)
        quantize_wb(1)
        v2_rows_late[3] = place("v2_rows_late3", [P, CHUNK], U8, "wb_bf1")
        gather_bytes(v2_rows_late[3], v2_scale_window, list2, 3 * CHUNK, 4 * CHUNK)

        z[0] = [next_bank([P, PACK, GROUP]) for b in range(PACK)]
        z[1] = [next_bank([P, CHUNK]) for t in range(PACK)]
        for b in range(PACK):
            for t in range(PACK):
                v2_pass(0, 0, t, GROUP * b, GROUP, z[0][b][:, t, :], t == 0, False)
        for t in range(PACK):
            v2_pass(1, 0, t, 0, CHUNK, z[1][t][:], True, False)
        for b in range(PACK):
            for t in range(PACK):
                v2_pass(0, 1, t, GROUP * b, GROUP, z[0][b][:, t, :], False, False)
        for t in range(EARLY_SLOTS):
            v2_pass(1, 1, t, 0, CHUNK, z[1][t][:], False, False)

        gather_v(0, own("v_words0_0", [P, HALF], U32), 0, HALF)
        gather_v(0, own("v_words0_1", [P, HALF], U32), HALF, HALF)
        gather_v(1, own("v_words1", [P, CHUNK], U32))
        tanh_z[0] = []
        for b in range(PACK):
            for t in range(PACK):
                v_pass(0, t, GROUP * b, GROUP, z[0][b][:, t, :], False, t == PACK - 1)
            piece = place("tanh0_%d" % b, [P, PACK, GROUP], F32, "tanh0", 4 * CHUNK * b)
            nc.scalar.activation(piece[:], z[0][b][:], ACT.Tanh)
            tanh_z[0].append(piece)
        for t in range(PACK):
            v_pass(1, t, 0, CHUNK, z[1][t][:], False, t < EARLY_SLOTS)
            if t >= EARLY_SLOTS:
                v2_pass(1, 1, t, 0, CHUNK, z[1][t][:], False, True)
        for c in v2_planes_late:
            move_pairs(v2_planes_late[c], v2_rows_late[c])
        load_plane(v_scale_window, tab_scales)
        make_h(0, GROUP, scale_group(0), own("h_codes0", [P, CHUNK], U32))
        tanh_slots(1, place("tanh1", [P, PACK, CHUNK], F32, "tanh1"))

        last_piece = 4 * CHUNK * (PACK - 1)
        gather_v2(2, place("v2_words2", [P, CHUNK], U32, "tanh0", last_piece - WORDS // 2))
        gather_v(2, place("v_words2", [P, CHUNK], U32, "tanh0", last_piece + WORDS // 2))
        part_v2(2, own("v2_parted2", [P, WORDS], U8))
        score_halves(0)
        score(0, range(PACK, N // P), next_banks(PACK))
        z[2] = [next_bank([P, CHUNK]) for t in range(PACK)]
        for t in range(PACK):
            v_pass(2, t, 0, CHUNK, z[2][t][:], True, False)
        for t in range(PACK):
            for a in range(V2_PASSES):
                v2_pass(2, a, t, 0, CHUNK, z[2][t][:], False, a == V2_PASSES - 1)
        make_h(1, HALF, scale_half(1), own("h_codes1", [P, CHUNK], U32))
        tanh_slots(2, place("tanh2", [P, PACK, CHUNK], F32, "tanh2"))

        gather_v2(3, place("v2_words3", [P, CHUNK], U32, "tanh1"))
        part_v2(3, own("v2_parted3", [P, WORDS], U8))
        score(1, range(N // P), next_banks(BANKS))
        make_h(2, HALF, scale_half(2), own("h_codes2", [P, CHUNK], U32))
        gather_v_plane(3, place("v_plane3", [P, CHUNK], U8, "tanh2", WORDS))
        for half in range(2):
            gather_v(3, place("v_words3_%d" % half, [P, HALF], U32, "v_scale_window", half * WORDS // 2), HALF * half, HALF)
        emptied = next_banks(BANKS)
        z_banks = emptied[:2] + emptied[-2:]
        score_banks = emptied[2:-2]
        z[3] = {}

        def open_last(b):
            z[3][b] = bank(z_banks[b], [P, PACK, GROUP])
            for a in range(V2_PASSES):
                for t in range(PACK):
                    v2_pass(3, a, t, GROUP * b, GROUP, z[3][b][:, t, :], a == 0 and t == 0, False)

        for b in range(2):
            open_last(b)
        score(2, range(PACK), score_banks, HALF)
        open_last(2)
        tanh_z[3] = [own("tanh3_%d" % b, [P, PACK, GROUP], F32) for b in range(PACK)]
        for b in range(PACK):
            if b == 2:
                open_last(3)
            if b == 3:
                score(2, [PACK], z_banks[:1])
            for t in range(PACK):
                v_pass(3, t, GROUP * b, GROUP, z[3][b][:, t, :], False, t == PACK - 1)
            nc.scalar.activation(tanh_z[3][b][:], z[3][b][:], ACT.Tanh)
        score_in_halves(2, PACK + 1, z_banks[1])
        score(2, range(PACK + 2, N // P), z_banks[2:])
        make_h(3, GROUP, scale_group(3), own("h_codes3", [P, CHUNK], U32))
        score(3, range(N // P), score_banks + z_banks, GROUP)
